import numpy as np
import ml_dtypes


def mxq(x, axis, fmt="e4m3"):
    dtype, down = {"e4m3": (ml_dtypes.float8_e4m3fn, 7), "e5m2": (ml_dtypes.float8_e5m2, 14)}[fmt]
    v = np.moveaxis(np.asarray(x, np.float32).astype(ml_dtypes.bfloat16).astype(np.float64), axis, -1)
    blocks = v.reshape(v.shape[:-1] + (-1, 32))
    amax = np.abs(blocks).max(-1, keepdims=True)
    byte = np.maximum(np.where(amax > 0, np.frexp(amax)[1] - 1 + 127, 0) - down, 1)
    scale = np.exp2(byte - 127.0)
    codes = (blocks / scale).astype(np.float32).astype(dtype).astype(np.float64)
    return np.moveaxis((codes * scale).reshape(v.shape), -1, axis)


WIDE = False


def mx_kscale(k):
    if not WIDE:
        return np.ones(k)
    levels = np.array([30, -30])
    if k % 512:
        return np.exp2(np.random.permutation(np.resize(levels, k // 32))).repeat(32)
    a = np.empty((k // 512, 16))
    for p in range(k // 512):
        a[p, :8] = np.random.permutation(np.resize(levels, 8))
        for g in range(8):
            far = levels[np.abs(levels - a[p, g]) >= 10]
            a[p, g + 8] = far[np.random.randint(len(far))]
    return np.exp2(a.ravel()).repeat(32)


def f64(x):
    return np.asarray(x).astype(np.float64)


def striped(idx):
    return np.tile(idx.reshape(-1, 16).T, (8, 1)).astype(np.uint16)


def unstriped(offs):
    return offs[:16].T.reshape(-1).astype(np.int64)


def bf(x):
    return np.asarray(x, np.float32).astype(ml_dtypes.bfloat16)


E2M1 = np.array([0.0, 0.5, 1.0, 1.5, 2.0, 3.0, 4.0, 6.0, -0.0, -0.5, -1.0, -1.5, -2.0, -3.0, -4.0, -6.0])


def pack_weight(w, fmt):
    k, n = w.shape
    w = f64(bf(w)).reshape(k // 32, 32, n)
    amax = np.abs(w).max(1)
    if fmt in ("e4m3", "e5m2"):
        byte = np.frexp(amax)[1] - 1 + 127 - (7 if fmt == "e4m3" else 14)
    else:
        mant, ex = np.frexp(amax / 6.0)
        byte = np.where(mant > 0.5, ex, ex - 1) + 127
    byte = np.clip(np.where(amax > 0, byte, 1), 1, 254)
    scaled = (w * np.exp2(127.0 - byte)[:, None, :]).reshape(k, n).astype(np.float32)
    by_word = np.ascontiguousarray(scaled.reshape(k // 512, 128, 4, n).transpose(0, 1, 3, 2))
    if fmt in ("e4m3", "e5m2"):
        words = by_word.astype(ml_dtypes.float8_e4m3fn if fmt == "e4m3" else ml_dtypes.float8_e5m2).view(np.uint8)
    else:
        c = by_word.astype(ml_dtypes.float4_e2m1fn).view(np.uint8) & 0xF
        words = c[..., 0::2] | (c[..., 1::2] << 4)
    return np.ascontiguousarray(words), np.ascontiguousarray(byte.astype(np.uint8).reshape(k // 512, 16, n))


def unpack_weight(words, scales, fmt):
    g, p, n, _ = words.shape
    if fmt in ("e4m3", "e5m2"):
        vals = np.ascontiguousarray(words).view(ml_dtypes.float8_e4m3fn if fmt == "e4m3" else ml_dtypes.float8_e5m2).astype(np.float64)
    else:
        nib = np.empty((g, p, n, 4), np.uint8)
        nib[..., 0::2] = words & 0xF
        nib[..., 1::2] = words >> 4
        vals = E2M1[nib]
    vals = vals * np.repeat(np.exp2(scales.astype(np.float64) - 127.0), 8, axis=1)[..., None]
    return vals.transpose(0, 1, 3, 2).reshape(g * 512, n)


K, T, S, H, N, T2 = 1024, 2048, 1024, 1024, 512, 2048

def setup_inputs():
    n = np.random.standard_normal
    s = mx_kscale(K)[:, None]
    u = mx_kscale(H)[:, None]
    tab_words, tab_scales = pack_weight(n((K, T)) * np.exp(1.0 * n((1, T))) * s, "e5m2")
    wv_words, wv_scales = pack_weight(3.0 * n((H, N)) / np.sqrt(H) / u, "e4m3")
    return {
        "tab_words": tab_words, "tab_scales": tab_scales,
        "offs": striped(np.random.permutation(T)[:S]),
        "offs2": striped(np.random.permutation(T2)[:S]),
        "sT": (1.0 / (1.0 + np.exp(-n((H, T))))).astype(np.float32),
        "w1": (n((K, H)) / np.sqrt(K) / s * u.T).astype(np.float32),
        "wv_words": wv_words, "wv_scales": wv_scales,
        "wg": (1.5 * n((H, N)) / np.sqrt(H) / u).astype(np.float32),
        "wgo": np.exp(0.3 * n((128, S))).astype(np.float32),
    }

def reference(tab_words, tab_scales, offs, offs2, sT, w1, wv_words, wv_scales, wg, wgo):
    v = unpack_weight(tab_words, tab_scales, "e5m2")[:, unstriped(offs)]
    s_ = f64(sT)[:, unstriped(offs)]
    h = mxq(f64(w1), 0, "e4m3").T @ v
    d = h * (s_ * (1.0 - s_))
    dq = mxq(d, 0, "e4m3")
    val = unpack_weight(wv_words, wv_scales, "e4m3").T @ dq
    gate = mxq(f64(wg), 0, "e4m3").T @ dq
    y = val / (1.0 + np.exp(-gate))
    out = np.zeros((N, T2))
    out[:, unstriped(offs2)] = np.tile(f64(wgo), (N // 128, 1)) * y
    return out

@@ -1,0 +1,236 @@
+from contextlib import ExitStack
+
+import concourse.mybir as mybir
+
+K, T, S, H, N, T2 = 1024, 2048, 1024, 1024, 512, 2048
+FLOPS = 2 * K * H * S + 2 * 2 * H * N * S
+
+F32 = mybir.dt.float32
+BF16 = mybir.dt.bfloat16
+I32 = mybir.dt.int32
+U32 = mybir.dt.uint32
+U16 = mybir.dt.uint16
+U8 = mybir.dt.uint8
+E4M3 = mybir.dt.float8_e4m3fn_x4
+E5M2 = mybir.dt.float8_e5m2_x4
+MULT = mybir.AluOpType.mult
+ADD = mybir.AluOpType.add
+SIGMOID = mybir.ActivationFunctionType.Sigmoid
+
+P = 128
+PACK = 4
+PASS = P * PACK
+HALF = 512
+LCOLS = HALF // 16
+
+
+def tile_list_botnet_gated_gradients_kernel(
+    tc, tab_words, tab_scales, offs, offs2, sT, w1, wv_words, wv_scales, wg, wgo, out
+):
+    nc = tc.nc
+    with ExitStack() as ctx:
+        keep = ctx.enter_context(tc.tile_pool(name="keep", bufs=1))
+        ring = ctx.enter_context(tc.tile_pool(name="ring", bufs=2))
+        psum = ctx.enter_context(tc.psum_pool(name="psum", bufs=1))
+
+        def held(shape, dtype, name, tag=None):
+            return keep.tile(shape, dtype, name=name, tag=tag or name, align_bytes=64)
+
+        lst = held([P, S // 16], U16, "lst")
+        lst2 = held([P, S // 16], U16, "lst2")
+        tab_sc = held([P, T], U8, "tab_sc")
+        v_sc = [held([P, S], U8, "v_sc%d" % a) for a in range(2)]
+        wv_sc = held([P, N], U8, "wv_sc")
+        page = [held([P, T2], F32, "page%d" % c) for c in range(N // P)]
+
+        nc.vector.memset(tab_sc[:].bitcast(I32), 0)
+        nc.vector.memset(v_sc[1][:].bitcast(I32), 0)
+        nc.vector.memset(wv_sc[:].bitcast(I32), 0)
+        for c in range(N // P):
+            nc.vector.memset(page[c][:].bitcast(I32), 0)
+
+        s_rows = sT.rearrange("(b p t) c -> b t p c", p=P, t=PACK)
+        s_win = {}
+
+        def load_s(u):
+            s_win[u] = ring.tile([P, T], F32, name="s_win%d" % u, tag="s_win", bufs=3)
+            nc.sync.dma_start(out=s_win[u][:], in_=s_rows[u // PACK, u % PACK])
+
+        def load_scale_rows(queue, tile, scales):
+            for q in range(4):
+                queue.dma_start(
+                    out=tile[32 * q : 32 * q + 8, :].bitcast(I32),
+                    in_=scales[:, 4 * q : 4 * q + 4, :].bitcast(I32),
+                )
+
+        tab_w = {}
+
+        def load_tab(a):
+            tab_w[a] = held([P, T], U32, "tab_w%d" % a)
+            nc.sync.dma_start(
+                out=tab_w[a][:].bitcast(I32),
+                in_=tab_words[a].rearrange("p t i -> p (t i)").bitcast(I32),
+            )
+
+        raw = {}
+
+        def load_weight(key, rows):
+            raw[key] = ring.tile([P, PACK, HALF], F32, name="raw_%s" % key, tag="raw", bufs=3)
+            nc.sync.dma_start(out=raw[key][:], in_=rows.rearrange("(p j) c -> p j c", j=PACK))
+
+        codes, scales = {}, {}
+
+        def quantize(key, grouped):
+            codes[key] = held([P, HALF], U32, "codes_%s" % key)
+            scales[key] = held([P, HALF], U8, "scales_%s" % key)
+            nc.vector.quantize_mx(out=codes[key][:].bitcast(E4M3), scales=scales[key][:], in_=grouped[:])
+
+        def grouped_tile(key):
+            return ring.tile([P, PACK * HALF], BF16, name="grouped_%s" % key, tag="grouped", bufs=3, align_bytes=64)
+
+        def quantize_w1(a, b):
+            key = "w1_%d%d" % (a, b)
+            grouped = grouped_tile(key)
+            nc.scalar.copy(
+                out=grouped[:].rearrange("p (t m j) -> p m j t", t=PACK, j=PACK),
+                in_=raw[key][:].rearrange("p j (m t) -> p m j t", t=PACK),
+            )
+            quantize(key, grouped)
+
+        def interleave_and_quantize(key, planes):
+            grouped = grouped_tile(key)
+            nc.scalar.copy(
+                out=grouped[:].rearrange("p (c i j) -> p c j i", i=4, j=PACK),
+                in_=planes[:].rearrange("p j (c i) -> p c j i", i=4),
+            )
+            quantize(key, grouped)
+
+        slope = {}
+
+        def gather_slope(u):
+            for h in range(2):
+                slope[u, h] = held([P, HALF], F32, "slope%d%d" % (u, h))
+                nc.vector.tensor_copy(slope[u, h][:], s_win[u][:].indirect(lst[:, h * LCOLS : (h + 1) * LCOLS]))
+            for h in range(2):
+                m = slope[u, h]
+                nc.vector.scalar_tensor_tensor(out=m[:], in0=m[:], scalar=-1.0, in1=m[:], op0=ADD, op1=MULT)
+
+        v_w = {}
+        d_planes = {}
+
+        def make_d(u, h):
+            b, t = divmod(u, PACK)
+            if t == 0:
+                tag = "slope70" if (b, h) == (0, 1) else None
+                d_planes[b, h] = held([P, PACK, HALF], BF16, "d_planes%d%d" % (b, h), tag)
+            acc = psum.tile([P, HALF], F32, name="h%d%d" % (u, h), tag="bank%d" % h, bufs=(2, 6)[h])
+            cols = slice(h * HALF, (h + 1) * HALF)
+            for a in range(2):
+                key = "w1_%d%d" % (a, b)
+                nc.tensor.matmul_mx(
+                    out=acc[:],
+                    lhsT=codes[key][:, t * P : (t + 1) * P].bitcast(E4M3),
+                    lhsT_scale=scales[key][:, t * P : (t + 1) * P],
+                    rhs=v_w[a][:, cols].bitcast(E5M2),
+                    rhs_scale=v_sc[a][:, cols],
+                    start=(a == 0),
+                    stop=(a == 1),
+                )
+            nc.vector.scalar_tensor_tensor(
+                out=d_planes[b, h][:, t, :], in0=acc[:], scalar=-1.0, in1=slope[u, h][:], op0=MULT, op1=MULT
+            )
+            if t == PACK - 1:
+                interleave_and_quantize("d_%d%d" % (b, h), d_planes[b, h])
+
+        def w1_rows(a, b):
+            return w1[a * PASS : (a + 1) * PASS, b * HALF : (b + 1) * HALF]
+
+        nc.sync.dma_start(lst[:], offs)
+        load_s(0)
+        load_scale_rows(nc.scalar, tab_sc, tab_scales)
+        load_tab(0)
+        load_tab(1)
+        load_weight("w1_00", w1_rows(0, 0))
+        load_weight("w1_10", w1_rows(1, 0))
+
+        nc.vector.tensor_copy(v_sc[0][:], tab_sc[:].indirect(lst[:]))
+        nc.scalar.dma_start(out=v_sc[1][0 : P - 4, :].bitcast(I32), in_=v_sc[0][4:P, :].bitcast(I32))
+        gather_slope(0)
+        for a in range(2):
+            v_w[a] = held([P, S], U32, "v_w%d" % a)
+            nc.vector.tensor_copy(v_w[a][:], tab_w[a][:].indirect(lst[:]))
+        quantize_w1(0, 0)
+        quantize_w1(1, 0)
+        for u in (1, 2, 3):
+            load_s(u)
+            if u > 1:
+                load_weight("w1_%d1" % (u - 2), w1_rows(u - 2, 1))
+            gather_slope(u)
+            make_d(u - 1, 0)
+        make_d(3, 0)
+        quantize_w1(0, 1)
+        quantize_w1(1, 1)
+        for u in (4, 5, 6, 7):
+            load_s(u)
+            gather_slope(u)
+            make_d(u, 0)
+
+        for b in range(2):
+            load_weight("wg_%d" % b, wg[b * PASS : (b + 1) * PASS, :])
+            interleave_and_quantize("wg_%d" % b, raw["wg_%d" % b])
+        wv_w = held([P, 2, N], U32, "wv_w")
+        nc.sync.dma_start(
+            out=wv_w[:].bitcast(I32), in_=wv_words.rearrange("b p c i -> p b (c i)").bitcast(I32)
+        )
+        load_scale_rows(nc.sync, wv_sc, wv_scales)
+        wgo_sb = held([P, S], F32, "wgo_sb")
+        nc.sync.dma_start(out=wgo_sb[:], in_=wgo)
+        nc.sync.dma_start(lst2[:], offs2)
+
+        for u in range(2 * PACK):
+            make_d(u, 1)
+
+        def second_product(acc, h, lhsT, lhsT_scale):
+            for b in range(2):
+                key = "d_%d%d" % (b, h)
+                nc.tensor.matmul_mx(
+                    out=acc[:],
+                    lhsT=lhsT[b].bitcast(E4M3),
+                    lhsT_scale=lhsT_scale[b],
+                    rhs=codes[key][:].bitcast(E4M3),
+                    rhs_scale=scales[key][:],
+                    start=(b == 0),
+                    stop=(b == 1),
+                )
+
+        y = {}
+
+        def make_y(h, c):
+            cols = slice(c * P, (c + 1) * P)
+            gate = psum.tile([P, HALF], F32, name="gate%d%d" % (h, c), tag="bank0", bufs=2)
+            second_product(
+                gate, h, [codes["wg_%d" % b][:, cols] for b in range(2)], [scales["wg_%d" % b][:, cols] for b in range(2)]
+            )
+            val = psum.tile([P, HALF], F32, name="val%d%d" % (h, c), tag="bank1", bufs=6)
+            second_product(val, h, [wv_w[:, b, cols] for b in range(2)], [wv_sc[4 * b :, cols] for b in range(2)])
+            sig = ring.tile([P, HALF], F32, name="sig%d%d" % (h, c), tag="sig", bufs=3)
+            nc.scalar.activation(out=sig[:], in_=gate[:], func=SIGMOID)
+            y[h, c] = ring.tile([P, HALF], F32, name="y%d%d" % (h, c), tag="y", bufs=3)
+            nc.vector.tensor_tensor(y[h, c][:], val[:], sig[:], MULT)
+
+        def scatter(h, c):
+            nc.vector.tensor_tensor(
+                page[c][:].indirect(lst2[:, h * LCOLS : (h + 1) * LCOLS]),
+                y[h, c][:],
+                wgo_sb[:, h * HALF : (h + 1) * HALF],
+                MULT,
+            )
+            if h == 1:
+                nc.sync.dma_start(out=out[c * P : (c + 1) * P, :], in_=page[c][:])
+
+        steps = [(h, c) for h in range(2) for c in range(N // P)]
+        make_y(*steps[0])
+        for i, step in enumerate(steps):
+            if i + 1 < len(steps):
+                make_y(*steps[i + 1])
+            scatter(*step)

@@ -14,7 +14,7 @@ U8 = mybir.dt.uint8
 E4M3 = mybir.dt.float8_e4m3fn_x4
 E5M2 = mybir.dt.float8_e5m2_x4
 MULT = mybir.AluOpType.mult
-ADD = mybir.AluOpType.add
+COPY = mybir.ActivationFunctionType.Copy
 SIGMOID = mybir.ActivationFunctionType.Sigmoid
 
 P = 128
@@ -43,17 +43,23 @@ def tile_list_botnet_gated_gradients_kernel(
         wv_sc = held([P, N], U8, "wv_sc")
         page = [held([P, T2], F32, "page%d" % c) for c in range(N // P)]
 
-        nc.vector.memset(tab_sc[:].bitcast(I32), 0)
-        nc.vector.memset(v_sc[1][:].bitcast(I32), 0)
-        nc.vector.memset(wv_sc[:].bitcast(I32), 0)
+        nc.gpsimd.memset(tab_sc[:].bitcast(I32), 0)
+        nc.gpsimd.memset(v_sc[1][:].bitcast(I32), 0)
+        nc.gpsimd.memset(wv_sc[:].bitcast(I32), 0)
         for c in range(N // P):
-            nc.vector.memset(page[c][:].bitcast(I32), 0)
+            nc.gpsimd.memset(page[c][:], 0.0)
+
+        slot_of = {}
+
+        def staged(shape, dtype, name):
+            slot_of[name] = "slot%d" % (len(slot_of) % 8)
+            return held(shape, dtype, name, slot_of[name])
 
         s_rows = sT.rearrange("(b p t) c -> b t p c", p=P, t=PACK)
         s_win = {}
 
         def load_s(u):
-            s_win[u] = ring.tile([P, T], F32, name="s_win%d" % u, tag="s_win", bufs=3)
+            s_win[u] = staged([P, T], F32, "s_win%d" % u)
             nc.sync.dma_start(out=s_win[u][:], in_=s_rows[u // PACK, u % PACK])
 
         def load_scale_rows(queue, tile, scales):
@@ -66,7 +72,7 @@ def tile_list_botnet_gated_gradients_kernel(
         tab_w = {}
 
         def load_tab(a):
-            tab_w[a] = held([P, T], U32, "tab_w%d" % a)
+            tab_w[a] = staged([P, T], U32, "tab_w%d" % a)
             nc.sync.dma_start(
                 out=tab_w[a][:].bitcast(I32),
                 in_=tab_words[a].rearrange("p t i -> p (t i)").bitcast(I32),
@@ -75,35 +81,31 @@ def tile_list_botnet_gated_gradients_kernel(
         raw = {}
 
         def load_weight(key, rows):
-            raw[key] = ring.tile([P, PACK, HALF], F32, name="raw_%s" % key, tag="raw", bufs=3)
+            raw[key] = staged([P, PACK, HALF], F32, "raw_%s" % key)
             nc.sync.dma_start(out=raw[key][:], in_=rows.rearrange("(p j) c -> p j c", j=PACK))
 
         codes, scales = {}, {}
 
-        def quantize(key, grouped):
-            codes[key] = held([P, HALF], U32, "codes_%s" % key)
-            scales[key] = held([P, HALF], U8, "scales_%s" % key)
-            nc.vector.quantize_mx(out=codes[key][:].bitcast(E4M3), scales=scales[key][:], in_=grouped[:])
+        grouped = {}
 
-        def grouped_tile(key):
-            return ring.tile([P, PACK * HALF], BF16, name="grouped_%s" % key, tag="grouped", bufs=3, align_bytes=64)
+        def quantize(key, tag=None):
+            words = grouped[key].shape[1] // PACK
+            codes[key] = held([P, words], U32, "codes_%s" % key, tag)
+            scales[key] = held([P, words], U8, "scales_%s" % key)
+            nc.vector.quantize_mx(out=codes[key][:].bitcast(E4M3), scales=scales[key][:], in_=grouped[key][:])
 
-        def quantize_w1(a, b):
-            key = "w1_%d%d" % (a, b)
-            grouped = grouped_tile(key)
+        def grouped_pass(key, passes, a):
+            if a == 0:
+                grouped[key] = ring.tile(
+                    [P, passes * PACK * HALF], BF16, name="grouped_%s" % key, tag="grouped%d" % passes, align_bytes=64
+                )
+            return grouped[key][:, a * PACK * HALF : (a + 1) * PACK * HALF]
+
+        def interleave(dst, planes):
             nc.scalar.copy(
-                out=grouped[:].rearrange("p (t m j) -> p m j t", t=PACK, j=PACK),
-                in_=raw[key][:].rearrange("p j (m t) -> p m j t", t=PACK),
-            )
-            quantize(key, grouped)
-
-        def interleave_and_quantize(key, planes):
-            grouped = grouped_tile(key)
-            nc.scalar.copy(
-                out=grouped[:].rearrange("p (c i j) -> p c j i", i=4, j=PACK),
+                out=dst.rearrange("p (c i j) -> p c j i", i=4, j=PACK),
                 in_=planes[:].rearrange("p j (c i) -> p c j i", i=4),
             )
-            quantize(key, grouped)
 
         slope = {}
 
@@ -111,9 +113,10 @@ def tile_list_botnet_gated_gradients_kernel(
             for h in range(2):
                 slope[u, h] = held([P, HALF], F32, "slope%d%d" % (u, h))
                 nc.vector.tensor_copy(slope[u, h][:], s_win[u][:].indirect(lst[:, h * LCOLS : (h + 1) * LCOLS]))
-            for h in range(2):
                 m = slope[u, h]
-                nc.vector.scalar_tensor_tensor(out=m[:], in0=m[:], scalar=-1.0, in1=m[:], op0=ADD, op1=MULT)
+                rest = ring.tile([P, HALF], F32, name="rest%d%d" % (u, h), tag="rest", bufs=3)
+                nc.scalar.activation(out=rest[:], in_=m[:], func=COPY, scale=-1.0, bias=1.0)
+                nc.gpsimd.tensor_tensor(m[:], m[:], rest[:], MULT)
 
         v_w = {}
         d_planes = {}
@@ -121,63 +124,80 @@ def tile_list_botnet_gated_gradients_kernel(
         def make_d(u, h):
             b, t = divmod(u, PACK)
             if t == 0:
-                tag = "slope70" if (b, h) == (0, 1) else None
+                tag = {(0, 0): slot_of["s_win5"], (1, 0): slot_of.get("s_win7"), (0, 1): "slope70"}.get((b, h))
                 d_planes[b, h] = held([P, PACK, HALF], BF16, "d_planes%d%d" % (b, h), tag)
-            acc = psum.tile([P, HALF], F32, name="h%d%d" % (u, h), tag="bank%d" % h, bufs=(2, 6)[h])
+            acc = psum.tile([P, HALF], F32, name="h%d%d" % (u, h), tag="bank", bufs=8)
             cols = slice(h * HALF, (h + 1) * HALF)
             for a in range(2):
-                key = "w1_%d%d" % (a, b)
+                key = "w1_%d" % b
+                rows = slice(a * HALF + t * P, a * HALF + (t + 1) * P)
                 nc.tensor.matmul_mx(
                     out=acc[:],
-                    lhsT=codes[key][:, t * P : (t + 1) * P].bitcast(E4M3),
-                    lhsT_scale=scales[key][:, t * P : (t + 1) * P],
+                    lhsT=codes[key][:, rows].bitcast(E4M3),
+                    lhsT_scale=scales[key][:, rows],
                     rhs=v_w[a][:, cols].bitcast(E5M2),
                     rhs_scale=v_sc[a][:, cols],
                     start=(a == 0),
                     stop=(a == 1),
                 )
-            nc.vector.scalar_tensor_tensor(
-                out=d_planes[b, h][:, t, :], in0=acc[:], scalar=-1.0, in1=slope[u, h][:], op0=MULT, op1=MULT
-            )
+            nc.vector.tensor_tensor(d_planes[b, h][:, t, :], acc[:], slope[u, h][:], MULT)
             if t == PACK - 1:
-                interleave_and_quantize("d_%d%d" % (b, h), d_planes[b, h])
+                interleave(grouped_pass("d_%d%d" % (b, h), 1, 0), d_planes[b, h])
 
         def w1_rows(a, b):
             return w1[a * PASS : (a + 1) * PASS, b * HALF : (b + 1) * HALF]
 
-        nc.sync.dma_start(lst[:], offs)
-        load_s(0)
-        load_scale_rows(nc.scalar, tab_sc, tab_scales)
-        load_tab(0)
-        load_tab(1)
-        load_weight("w1_00", w1_rows(0, 0))
-        load_weight("w1_10", w1_rows(1, 0))
-
-        nc.vector.tensor_copy(v_sc[0][:], tab_sc[:].indirect(lst[:]))
-        nc.scalar.dma_start(out=v_sc[1][0 : P - 4, :].bitcast(I32), in_=v_sc[0][4:P, :].bitcast(I32))
-        gather_slope(0)
-        for a in range(2):
+        def gather_words(a):
             v_w[a] = held([P, S], U32, "v_w%d" % a)
             nc.vector.tensor_copy(v_w[a][:], tab_w[a][:].indirect(lst[:]))
-        quantize_w1(0, 0)
-        quantize_w1(1, 0)
-        for u in (1, 2, 3):
-            load_s(u)
-            if u > 1:
-                load_weight("w1_%d1" % (u - 2), w1_rows(u - 2, 1))
-            gather_slope(u)
-            make_d(u - 1, 0)
-        make_d(3, 0)
-        quantize_w1(0, 1)
-        quantize_w1(1, 1)
-        for u in (4, 5, 6, 7):
-            load_s(u)
-            gather_slope(u)
-            make_d(u, 0)
 
-        for b in range(2):
+        def first_weight(a, b):
+            load_weight("w1_%d%d" % (a, b), w1_rows(a, b))
+            nc.scalar.copy(
+                out=grouped_pass("w1_%d" % b, 2, a).rearrange("p (t m j) -> p m j t", t=PACK, j=PACK),
+                in_=raw["w1_%d%d" % (a, b)][:].rearrange("p j (m t) -> p m j t", t=PACK),
+            )
+
+        def gate_weight(b):
             load_weight("wg_%d" % b, wg[b * PASS : (b + 1) * PASS, :])
-            interleave_and_quantize("wg_%d" % b, raw["wg_%d" % b])
+            interleave(grouped_pass("wg", 2, b), raw["wg_%d" % b])
+
+        def slope_rows(u):
+            load_s(u)
+            gather_slope(u)
+
+        nc.sync.dma_start(lst[:], offs)
+        load_scale_rows(nc.scalar, tab_sc, tab_scales)
+        nc.vector.tensor_copy(v_sc[0][:], tab_sc[:].indirect(lst[:]))
+        nc.gpsimd.dma_start(out=v_sc[1][0 : P - 4, :].bitcast(I32), in_=v_sc[0][4:P, :].bitcast(I32))
+        load_tab(0)
+        gather_words(0)
+        slope_rows(0)
+        load_tab(1)
+        gather_words(1)
+        first_weight(0, 0)
+        slope_rows(1)
+        first_weight(1, 0)
+        slope_rows(2)
+        first_weight(0, 1)
+        slope_rows(3)
+        quantize("w1_0", slot_of["s_win3"])
+        first_weight(1, 1)
+        slope_rows(4)
+        slope_rows(5)
+        for u in range(PACK):
+            make_d(u, 0)
+        quantize("w1_1", slot_of["s_win4"])
+        gate_weight(0)
+        slope_rows(6)
+        quantize("d_00", slot_of["s_win6"])
+        gate_weight(1)
+        slope_rows(7)
+        for u in range(PACK, 2 * PACK):
+            make_d(u, 0)
+        quantize("wg", "slope60")
+        quantize("d_10")
+
         wv_w = held([P, 2, N], U32, "wv_w")
         nc.sync.dma_start(
             out=wv_w[:].bitcast(I32), in_=wv_words.rearrange("b p c i -> p b (c i)").bitcast(I32)
@@ -189,6 +209,8 @@ def tile_list_botnet_gated_gradients_kernel(
 
         for u in range(2 * PACK):
             make_d(u, 1)
+            if u % PACK == PACK - 1:
+                quantize("d_%d1" % (u // PACK))
 
         def second_product(acc, h, lhsT, lhsT_scale):
             for b in range(2):
@@ -207,11 +229,10 @@ def tile_list_botnet_gated_gradients_kernel(
 
         def make_y(h, c):
             cols = slice(c * P, (c + 1) * P)
-            gate = psum.tile([P, HALF], F32, name="gate%d%d" % (h, c), tag="bank0", bufs=2)
-            second_product(
-                gate, h, [codes["wg_%d" % b][:, cols] for b in range(2)], [scales["wg_%d" % b][:, cols] for b in range(2)]
-            )
-            val = psum.tile([P, HALF], F32, name="val%d%d" % (h, c), tag="bank1", bufs=6)
+            gate = psum.tile([P, HALF], F32, name="gate%d%d" % (h, c), tag="bank", bufs=8)
+            wg_cols = [slice(b * N + c * P, b * N + (c + 1) * P) for b in range(2)]
+            second_product(gate, h, [codes["wg"][:, w] for w in wg_cols], [scales["wg"][:, w] for w in wg_cols])
+            val = psum.tile([P, HALF], F32, name="val%d%d" % (h, c), tag="bank", bufs=8)
             second_product(val, h, [wv_w[:, b, cols] for b in range(2)], [wv_sc[4 * b :, cols] for b in range(2)])
             sig = ring.tile([P, HALF], F32, name="sig%d%d" % (h, c), tag="sig", bufs=3)
             nc.scalar.activation(out=sig[:], in_=gate[:], func=SIGMOID)

@@ -14,14 +14,22 @@ U8 = mybir.dt.uint8
 E4M3 = mybir.dt.float8_e4m3fn_x4
 E5M2 = mybir.dt.float8_e5m2_x4
 MULT = mybir.AluOpType.mult
+ADD = mybir.AluOpType.add
 COPY = mybir.ActivationFunctionType.Copy
 SIGMOID = mybir.ActivationFunctionType.Sigmoid
 
 P = 128
 PACK = 4
 PASS = P * PACK
+PASSES = 2
 HALF = 512
-LCOLS = HALF // 16
+LIST_COLS = HALF // 16
+ROW_TILES = H // P
+LAST = ROW_TILES - 1
+PAGES = N // P
+RUN = 4
+SLOTS = 8
+BANKS = 8
 
 
 def tile_list_botnet_gated_gradients_kernel(
@@ -33,225 +41,249 @@ def tile_list_botnet_gated_gradients_kernel(
         ring = ctx.enter_context(tc.tile_pool(name="ring", bufs=2))
         psum = ctx.enter_context(tc.psum_pool(name="psum", bufs=1))
 
-        def held(shape, dtype, name, tag=None):
-            return keep.tile(shape, dtype, name=name, tag=tag or name, align_bytes=64)
+        tag_of = {}
 
-        lst = held([P, S // 16], U16, "lst")
-        lst2 = held([P, S // 16], U16, "lst2")
+        def held(shape, dtype, name, follows=None):
+            tag_of.setdefault(name, tag_of[follows] if follows else name)
+            return keep.tile(shape, dtype, name=name, tag=tag_of[name], align_bytes=64)
+
+        staged_names = []
+
+        def staged(shape, dtype, name):
+            tag_of[name] = "slot%d" % (len(staged_names) % SLOTS)
+            staged_names.append(name)
+            return held(shape, dtype, name)
+
+        def bank(name):
+            return psum.tile([P, HALF], F32, name=name, tag="bank", bufs=BANKS)
+
+        idx = held([P, S // 16], U16, "idx")
+        idx2 = held([P, S // 16], U16, "idx2")
         tab_sc = held([P, T], U8, "tab_sc")
-        v_sc = [held([P, S], U8, "v_sc%d" % a) for a in range(2)]
+        v_sc = {1: held([P, S], U8, "v_sc1")}
         wv_sc = held([P, N], U8, "wv_sc")
-        page = [held([P, T2], F32, "page%d" % c) for c in range(N // P)]
+        page = [held([P, T2], F32, "page%d" % c) for c in range(PAGES)]
 
         nc.gpsimd.memset(tab_sc[:].bitcast(I32), 0)
         nc.gpsimd.memset(v_sc[1][:].bitcast(I32), 0)
         nc.gpsimd.memset(wv_sc[:].bitcast(I32), 0)
-        for c in range(N // P):
+        for c in range(PAGES):
             nc.gpsimd.memset(page[c][:], 0.0)
 
-        slot_of = {}
-
-        def staged(shape, dtype, name):
-            slot_of[name] = "slot%d" % (len(slot_of) % 8)
-            return held(shape, dtype, name, slot_of[name])
-
-        s_rows = sT.rearrange("(b p t) c -> b t p c", p=P, t=PACK)
-        s_win = {}
-
-        def load_s(u):
-            s_win[u] = staged([P, T], F32, "s_win%d" % u)
-            nc.sync.dma_start(out=s_win[u][:], in_=s_rows[u // PACK, u % PACK])
-
-        def load_scale_rows(queue, tile, scales):
-            for q in range(4):
+        def load_scale_rows(queue, tile, scale_rows):
+            for quad in range(4):
                 queue.dma_start(
-                    out=tile[32 * q : 32 * q + 8, :].bitcast(I32),
-                    in_=scales[:, 4 * q : 4 * q + 4, :].bitcast(I32),
+                    out=tile[32 * quad : 32 * quad + 8, :].bitcast(I32),
+                    in_=scale_rows[:, 4 * quad : 4 * quad + 4, :].bitcast(I32),
                 )
-
-        tab_w = {}
-
-        def load_tab(a):
-            tab_w[a] = staged([P, T], U32, "tab_w%d" % a)
-            nc.sync.dma_start(
-                out=tab_w[a][:].bitcast(I32),
-                in_=tab_words[a].rearrange("p t i -> p (t i)").bitcast(I32),
-            )
-
-        raw = {}
-
-        def load_weight(key, rows):
-            raw[key] = staged([P, PACK, HALF], F32, "raw_%s" % key)
-            nc.sync.dma_start(out=raw[key][:], in_=rows.rearrange("(p j) c -> p j c", j=PACK))
-
-        codes, scales = {}, {}
-
-        grouped = {}
-
-        def quantize(key, tag=None):
-            words = grouped[key].shape[1] // PACK
-            codes[key] = held([P, words], U32, "codes_%s" % key, tag)
-            scales[key] = held([P, words], U8, "scales_%s" % key)
-            nc.vector.quantize_mx(out=codes[key][:].bitcast(E4M3), scales=scales[key][:], in_=grouped[key][:])
-
-        def grouped_pass(key, passes, a):
-            if a == 0:
-                grouped[key] = ring.tile(
-                    [P, passes * PACK * HALF], BF16, name="grouped_%s" % key, tag="grouped%d" % passes, align_bytes=64
-                )
-            return grouped[key][:, a * PACK * HALF : (a + 1) * PACK * HALF]
-
-        def interleave(dst, planes):
-            nc.scalar.copy(
-                out=dst.rearrange("p (c i j) -> p c j i", i=4, j=PACK),
-                in_=planes[:].rearrange("p j (c i) -> p c j i", i=4),
-            )
-
-        slope = {}
-
-        def gather_slope(u):
-            for h in range(2):
-                slope[u, h] = held([P, HALF], F32, "slope%d%d" % (u, h))
-                nc.vector.tensor_copy(slope[u, h][:], s_win[u][:].indirect(lst[:, h * LCOLS : (h + 1) * LCOLS]))
-                m = slope[u, h]
-                rest = ring.tile([P, HALF], F32, name="rest%d%d" % (u, h), tag="rest", bufs=3)
-                nc.scalar.activation(out=rest[:], in_=m[:], func=COPY, scale=-1.0, bias=1.0)
-                nc.gpsimd.tensor_tensor(m[:], m[:], rest[:], MULT)
 
         v_w = {}
-        d_planes = {}
 
-        def make_d(u, h):
-            b, t = divmod(u, PACK)
-            if t == 0:
-                tag = {(0, 0): slot_of["s_win5"], (1, 0): slot_of.get("s_win7"), (0, 1): "slope70"}.get((b, h))
-                d_planes[b, h] = held([P, PACK, HALF], BF16, "d_planes%d%d" % (b, h), tag)
-            acc = psum.tile([P, HALF], F32, name="h%d%d" % (u, h), tag="bank", bufs=8)
-            cols = slice(h * HALF, (h + 1) * HALF)
-            for a in range(2):
-                key = "w1_%d" % b
-                rows = slice(a * HALF + t * P, a * HALF + (t + 1) * P)
-                nc.tensor.matmul_mx(
-                    out=acc[:],
-                    lhsT=codes[key][:, rows].bitcast(E4M3),
-                    lhsT_scale=scales[key][:, rows],
-                    rhs=v_w[a][:, cols].bitcast(E5M2),
-                    rhs_scale=v_sc[a][:, cols],
-                    start=(a == 0),
-                    stop=(a == 1),
-                )
-            nc.vector.tensor_tensor(d_planes[b, h][:, t, :], acc[:], slope[u, h][:], MULT)
-            if t == PACK - 1:
-                interleave(grouped_pass("d_%d%d" % (b, h), 1, 0), d_planes[b, h])
-
-        def w1_rows(a, b):
-            return w1[a * PASS : (a + 1) * PASS, b * HALF : (b + 1) * HALF]
-
-        def gather_words(a):
+        def table_pass(a):
+            window = staged([P, T], U32, "tab_w%d" % a)
+            nc.sync.dma_start(
+                out=window[:].bitcast(I32), in_=tab_words[a].rearrange("p t i -> p (t i)").bitcast(I32)
+            )
             v_w[a] = held([P, S], U32, "v_w%d" % a)
-            nc.vector.tensor_copy(v_w[a][:], tab_w[a][:].indirect(lst[:]))
+            nc.vector.tensor_copy(v_w[a][:], window[:].indirect(idx[:]))
 
-        def first_weight(a, b):
-            load_weight("w1_%d%d" % (a, b), w1_rows(a, b))
-            nc.scalar.copy(
-                out=grouped_pass("w1_%d" % b, 2, a).rearrange("p (t m j) -> p m j t", t=PACK, j=PACK),
-                in_=raw["w1_%d%d" % (a, b)][:].rearrange("p j (m t) -> p m j t", t=PACK),
+        grouped, codes, scales = {}, {}, {}
+
+        def new_grouped_weight(key):
+            grouped[key] = ring.tile(
+                [P, PASSES * PACK * HALF], BF16, name="grouped_" + key, tag="grouped_weight", align_bytes=64
             )
 
-        def gate_weight(b):
-            load_weight("wg_%d" % b, wg[b * PASS : (b + 1) * PASS, :])
-            interleave(grouped_pass("wg", 2, b), raw["wg_%d" % b])
+        def grouped_pass(key, a):
+            return grouped[key][:, a * PACK * HALF : (a + 1) * PACK * HALF]
 
-        def slope_rows(u):
-            load_s(u)
-            gather_slope(u)
+        def group(dst, planes):
+            nc.scalar.copy(
+                out=dst.rearrange("p (c x i) -> p c i x", x=RUN, i=PACK),
+                in_=planes.rearrange("p i (c x) -> p c i x", x=RUN),
+            )
 
-        nc.sync.dma_start(lst[:], offs)
+        def quantize(key, follows=None):
+            words = grouped[key].shape[1] // PACK
+            codes[key] = held([P, words], U32, "codes_" + key, follows)
+            scales[key] = held([P, words], U8, "scales_" + key)
+            nc.vector.quantize_mx(out=codes[key][:].bitcast(E4M3), scales=scales[key][:], in_=grouped[key][:])
+
+        def load_weight(name, rows):
+            raw = staged([P, PACK, HALF], F32, name)
+            nc.sync.dma_start(out=raw[:], in_=rows.rearrange("(p i) c -> p i c", i=PACK))
+            return raw
+
+        def w1_piece(a, b):
+            raw = load_weight("raw_w1_%d%d" % (a, b), w1[a * PASS : (a + 1) * PASS, b * PASS : (b + 1) * PASS])
+            if a == 0:
+                new_grouped_weight("w1_%d" % b)
+            nc.scalar.copy(
+                out=grouped_pass("w1_%d" % b, a).rearrange("p (t m i) -> p m i t", t=PACK, i=PACK),
+                in_=raw[:].rearrange("p i (m t) -> p m i t", t=PACK),
+            )
+
+        def wg_pass(b):
+            raw = load_weight("raw_wg_%d" % b, wg[b * PASS : (b + 1) * PASS, :])
+            if b == 0:
+                new_grouped_weight("wg")
+            group(grouped_pass("wg", b), raw[:])
+
+        s_rows = sT.rearrange("(b p t) c -> b t p c", p=P, t=PACK)
+        slope = {}
+
+        def on_vector(u, half):
+            return (u, half) == (LAST, 0)
+
+        def make_slope(u, half):
+            s = slope[u, half]
+            if on_vector(u, half):
+                nc.vector.scalar_tensor_tensor(out=s[:], in0=s[:], scalar=-1.0, in1=s[:], op0=ADD, op1=MULT)
+                return
+            rest = ring.tile([P, HALF], F32, name="rest%d%d" % (u, half), tag="rest%d" % half)
+            if u == LAST:
+                nc.gpsimd.tensor_scalar(rest[:], s[:], -1.0, 1.0, MULT, ADD)
+            else:
+                nc.scalar.activation(out=rest[:], in_=s[:], func=COPY, scale=-1.0, bias=1.0)
+            nc.gpsimd.tensor_tensor(s[:], s[:], rest[:], MULT)
+
+        def s_tile(u):
+            window = (staged if u else held)([P, T], F32, "s_win%d" % u)
+            nc.sync.dma_start(out=window[:], in_=s_rows[u // PACK, u % PACK])
+            for half in range(2):
+                slope[u, half] = held([P, HALF], F32, "slope%d%d" % (u, half))
+                nc.vector.tensor_copy(
+                    slope[u, half][:], window[:].indirect(idx[:, half * LIST_COLS : (half + 1) * LIST_COLS])
+                )
+            make_slope(u, 0)
+
+        d_planes = {}
+
+        def make_d(u, half):
+            b, t = divmod(u, PACK)
+            h_bank = bank("h%d%d" % (u, half))
+            entries = slice(half * HALF, (half + 1) * HALF)
+            for a in range(PASSES):
+                words = slice(a * PASS + t * P, a * PASS + (t + 1) * P)
+                nc.tensor.matmul_mx(
+                    out=h_bank[:],
+                    lhsT=codes["w1_%d" % b][:, words].bitcast(E4M3),
+                    lhsT_scale=scales["w1_%d" % b][:, words],
+                    rhs=v_w[a][:, entries].bitcast(E5M2),
+                    rhs_scale=v_sc[a][:, entries],
+                    start=(a == 0),
+                    stop=(a == PASSES - 1),
+                )
+            nc.vector.scalar_tensor_tensor(
+                out=d_planes[b, half][:, t, :],
+                in0=h_bank[:],
+                scalar=-1.0 if on_vector(u, half) else 1.0,
+                in1=slope[u, half][:],
+                op0=MULT,
+                op1=MULT,
+            )
+
+        def first_half_of_d(b, follows, grouped_follows=None):
+            d_planes[b, 0] = held([P, PACK, HALF], BF16, "d_planes%d0" % b, follows)
+            for u in range(b * PACK, (b + 1) * PACK):
+                make_d(u, 0)
+            grouped["d_%d0" % b] = held([P, PACK * HALF], BF16, "grouped_d_%d0" % b, grouped_follows)
+            group(grouped_pass("d_%d0" % b, 0), d_planes[b, 0][:])
+
+        nc.sync.dma_start(idx[:], offs)
         load_scale_rows(nc.scalar, tab_sc, tab_scales)
-        nc.vector.tensor_copy(v_sc[0][:], tab_sc[:].indirect(lst[:]))
+        table_pass(0)
+        s_tile(0)
+        v_sc[0] = held([P, S], U8, "v_sc0", follows="s_win0")
+        nc.vector.tensor_copy(v_sc[0][:], tab_sc[:].indirect(idx[:]))
         nc.gpsimd.dma_start(out=v_sc[1][0 : P - 4, :].bitcast(I32), in_=v_sc[0][4:P, :].bitcast(I32))
-        load_tab(0)
-        gather_words(0)
-        slope_rows(0)
-        load_tab(1)
-        gather_words(1)
-        first_weight(0, 0)
-        slope_rows(1)
-        first_weight(1, 0)
-        slope_rows(2)
-        first_weight(0, 1)
-        slope_rows(3)
-        quantize("w1_0", slot_of["s_win3"])
-        first_weight(1, 1)
-        slope_rows(4)
-        slope_rows(5)
-        for u in range(PACK):
-            make_d(u, 0)
-        quantize("w1_1", slot_of["s_win4"])
-        gate_weight(0)
-        slope_rows(6)
-        quantize("d_00", slot_of["s_win6"])
-        gate_weight(1)
-        slope_rows(7)
-        for u in range(PACK, 2 * PACK):
-            make_d(u, 0)
-        quantize("wg", "slope60")
-        quantize("d_10")
+        table_pass(1)
+        w1_piece(0, 0)
+        s_tile(1)
+        s_tile(2)
+        w1_piece(1, 0)
+        s_tile(3)
+        s_tile(4)
+        quantize("w1_0", follows="s_win4")
+        w1_piece(0, 1)
+        s_tile(5)
+        first_half_of_d(0, follows="s_win5")
+        w1_piece(1, 1)
+        s_tile(6)
+        quantize("w1_1", follows="s_win6")
+        s_tile(LAST)
+        wg_pass(0)
+        wg_pass(1)
+        first_half_of_d(1, follows="s_win%d" % LAST, grouped_follows="raw_wg_1")
 
-        wv_w = held([P, 2, N], U32, "wv_w")
-        nc.sync.dma_start(
-            out=wv_w[:].bitcast(I32), in_=wv_words.rearrange("b p c i -> p b (c i)").bitcast(I32)
-        )
+        wv_w = held([P, PASSES, N], U32, "wv_w", follows="raw_w1_01")
+        nc.sync.dma_start(out=wv_w[:].bitcast(I32), in_=wv_words.rearrange("b p c i -> p b (c i)").bitcast(I32))
         load_scale_rows(nc.sync, wv_sc, wv_scales)
-        wgo_sb = held([P, S], F32, "wgo_sb")
+        wgo_sb = held([P, S], F32, "wgo_sb", follows="raw_w1_11")
         nc.sync.dma_start(out=wgo_sb[:], in_=wgo)
-        nc.sync.dma_start(lst2[:], offs2)
+        nc.sync.dma_start(idx2[:], offs2)
 
-        for u in range(2 * PACK):
+        both = held([P, PASSES, PACK, HALF], BF16, "d_planes1", follows="slope%d0" % LAST)
+        d_planes[0, 1], d_planes[1, 1] = both[:, 0], both[:, 1]
+        gate_operands = ("wg", "d_00", "d_10")
+        for u in range(ROW_TILES):
+            make_slope(u, 1)
             make_d(u, 1)
-            if u % PACK == PACK - 1:
-                quantize("d_%d1" % (u // PACK))
+            if u < len(gate_operands):
+                quantize(gate_operands[u], follows="slope%d1" % u)
 
-        def second_product(acc, h, lhsT, lhsT_scale):
-            for b in range(2):
-                key = "d_%d%d" % (b, h)
+        def second_product(acc, half, lhsT, lhsT_scale):
+            for b in range(PASSES):
+                key, words = ("d_%d0" % b, slice(0, HALF)) if half == 0 else ("d_1", slice(b * HALF, (b + 1) * HALF))
                 nc.tensor.matmul_mx(
                     out=acc[:],
                     lhsT=lhsT[b].bitcast(E4M3),
                     lhsT_scale=lhsT_scale[b],
-                    rhs=codes[key][:].bitcast(E4M3),
-                    rhs_scale=scales[key][:],
+                    rhs=codes[key][:, words].bitcast(E4M3),
+                    rhs_scale=scales[key][:, words],
                     start=(b == 0),
-                    stop=(b == 1),
+                    stop=(b == PASSES - 1),
                 )
 
+        steps = [(half, c) for half in range(2) for c in range(PAGES)]
         y = {}
 
-        def make_y(h, c):
-            cols = slice(c * P, (c + 1) * P)
-            gate = psum.tile([P, HALF], F32, name="gate%d%d" % (h, c), tag="bank", bufs=8)
-            wg_cols = [slice(b * N + c * P, b * N + (c + 1) * P) for b in range(2)]
-            second_product(gate, h, [codes["wg"][:, w] for w in wg_cols], [scales["wg"][:, w] for w in wg_cols])
-            val = psum.tile([P, HALF], F32, name="val%d%d" % (h, c), tag="bank", bufs=8)
-            second_product(val, h, [wv_w[:, b, cols] for b in range(2)], [wv_sc[4 * b :, cols] for b in range(2)])
-            sig = ring.tile([P, HALF], F32, name="sig%d%d" % (h, c), tag="sig", bufs=3)
-            nc.scalar.activation(out=sig[:], in_=gate[:], func=SIGMOID)
-            y[h, c] = ring.tile([P, HALF], F32, name="y%d%d" % (h, c), tag="y", bufs=3)
-            nc.vector.tensor_tensor(y[h, c][:], val[:], sig[:], MULT)
+        def ring_f32(kind, i):
+            return ring.tile([P, HALF], F32, name="%s%d" % (kind, i), tag=kind, bufs=3)
 
-        def scatter(h, c):
+        def make_y(i):
+            half, c = steps[i]
+            cols = slice(c * P, (c + 1) * P)
+            gate = bank("gate%d" % i)
+            wg_words = [slice(b * N + c * P, b * N + (c + 1) * P) for b in range(PASSES)]
+            second_product(gate, half, [codes["wg"][:, w] for w in wg_words], [scales["wg"][:, w] for w in wg_words])
+            val = bank("val%d" % i)
+            second_product(
+                val, half, [wv_w[:, b, cols] for b in range(PASSES)], [wv_sc[4 * b :, cols] for b in range(PASSES)]
+            )
+            sig = held([P, HALF], F32, "first_sig") if i == 0 else ring_f32("sig", i)
+            nc.scalar.activation(out=sig[:], in_=gate[:], func=SIGMOID)
+            y[i] = held([P, HALF], F32, "third_y", follows="d_planes1") if i == 2 else ring_f32("y", i)
+            nc.vector.tensor_tensor(y[i][:], val[:], sig[:], MULT)
+
+        def scatter(i):
+            half, c = steps[i]
             nc.vector.tensor_tensor(
-                page[c][:].indirect(lst2[:, h * LCOLS : (h + 1) * LCOLS]),
-                y[h, c][:],
-                wgo_sb[:, h * HALF : (h + 1) * HALF],
+                page[c][:].indirect(idx2[:, half * LIST_COLS : (half + 1) * LIST_COLS]),
+                y[i][:],
+                wgo_sb[:, half * HALF : (half + 1) * HALF],
                 MULT,
             )
-            if h == 1:
+            if half == 1:
                 nc.sync.dma_start(out=out[c * P : (c + 1) * P, :], in_=page[c][:])
 
-        steps = [(h, c) for h in range(2) for c in range(N // P)]
-        make_y(*steps[0])
-        for i, step in enumerate(steps):
-            if i + 1 < len(steps):
-                make_y(*steps[i + 1])
-            scatter(*step)
+        make_y(0)
+        make_y(1)
+        grouped["d_1"] = held([P, PASSES * PACK * HALF], BF16, "grouped_d_1", follows="first_sig")
+        for b in range(PASSES):
+            group(grouped_pass("d_1", b), d_planes[b, 1])
+        quantize("d_1")
+        for i in range(len(steps)):
+            scatter(i)
+            if i + 2 < len(steps):
+                make_y(i + 2)

@@ -28,8 +28,9 @@ ROW_TILES = H // P
 LAST = ROW_TILES - 1
 PAGES = N // P
 RUN = 4
-SLOTS = 8
 BANKS = 8
+EARLY = 2
+DIRECT = 2
 
 
 def tile_list_botnet_gated_gradients_kernel(
@@ -44,15 +45,8 @@ def tile_list_botnet_gated_gradients_kernel(
         tag_of = {}
 
         def held(shape, dtype, name, follows=None):
-            tag_of.setdefault(name, tag_of[follows] if follows else name)
+            tag_of[name] = tag_of[follows] if follows else name
             return keep.tile(shape, dtype, name=name, tag=tag_of[name], align_bytes=64)
-
-        staged_names = []
-
-        def staged(shape, dtype, name):
-            tag_of[name] = "slot%d" % (len(staged_names) % SLOTS)
-            staged_names.append(name)
-            return held(shape, dtype, name)
 
         def bank(name):
             return psum.tile([P, HALF], F32, name=name, tag="bank", bufs=BANKS)
@@ -60,187 +54,228 @@ def tile_list_botnet_gated_gradients_kernel(
         idx = held([P, S // 16], U16, "idx")
         idx2 = held([P, S // 16], U16, "idx2")
         tab_sc = held([P, T], U8, "tab_sc")
-        v_sc = {1: held([P, S], U8, "v_sc1")}
+        v_sc = {a: held([P, S], U8, "v_sc%d" % a) for a in range(PASSES)}
         wv_sc = held([P, N], U8, "wv_sc")
         page = [held([P, T2], F32, "page%d" % c) for c in range(PAGES)]
 
-        nc.gpsimd.memset(tab_sc[:].bitcast(I32), 0)
-        nc.gpsimd.memset(v_sc[1][:].bitcast(I32), 0)
+        for quad in range(4):
+            nc.gpsimd.memset(tab_sc[32 * quad : 32 * quad + 24, :].bitcast(I32), 0)
+        for a in range(PASSES):
+            nc.gpsimd.memset(v_sc[a][:].bitcast(I32), 0)
         nc.gpsimd.memset(wv_sc[:].bitcast(I32), 0)
         for c in range(PAGES):
             nc.gpsimd.memset(page[c][:], 0.0)
 
-        def load_scale_rows(queue, tile, scale_rows):
+        def load_scale_rows(queue, tile, scale_rows, first=0):
             for quad in range(4):
                 queue.dma_start(
-                    out=tile[32 * quad : 32 * quad + 8, :].bitcast(I32),
+                    out=tile[32 * quad + first : 32 * quad + first + 8, :].bitcast(I32),
                     in_=scale_rows[:, 4 * quad : 4 * quad + 4, :].bitcast(I32),
                 )
 
         v_w = {}
 
         def table_pass(a):
-            window = staged([P, T], U32, "tab_w%d" % a)
+            window = held([P, T], U32, "tab_w%d" % a)
             nc.sync.dma_start(
                 out=window[:].bitcast(I32), in_=tab_words[a].rearrange("p t i -> p (t i)").bitcast(I32)
             )
             v_w[a] = held([P, S], U32, "v_w%d" % a)
             nc.vector.tensor_copy(v_w[a][:], window[:].indirect(idx[:]))
 
-        grouped, codes, scales = {}, {}, {}
-
-        def new_grouped_weight(key):
-            grouped[key] = ring.tile(
-                [P, PASSES * PACK * HALF], BF16, name="grouped_" + key, tag="grouped_weight", align_bytes=64
-            )
-
-        def grouped_pass(key, a):
-            return grouped[key][:, a * PACK * HALF : (a + 1) * PACK * HALF]
-
-        def group(dst, planes):
+        def group(dst, planes, first=0):
+            count = planes.shape[1]
             nc.scalar.copy(
-                out=dst.rearrange("p (c x i) -> p c i x", x=RUN, i=PACK),
+                out=dst.rearrange("p (c x i) -> p c i x", x=RUN, i=PACK)[:, :, first : first + count, :],
                 in_=planes.rearrange("p i (c x) -> p c i x", x=RUN),
             )
 
-        def quantize(key, follows=None):
-            words = grouped[key].shape[1] // PACK
-            codes[key] = held([P, words], U32, "codes_" + key, follows)
-            scales[key] = held([P, words], U8, "scales_" + key)
-            nc.vector.quantize_mx(out=codes[key][:].bitcast(E4M3), scales=scales[key][:], in_=grouped[key][:])
+        def quantize(codes, scales, grouped):
+            nc.vector.quantize_mx(out=codes.bitcast(E4M3), scales=scales, in_=grouped)
 
-        def load_weight(name, rows):
-            raw = staged([P, PACK, HALF], F32, name)
+        def load_weight(name, rows, follows):
+            raw = held([P, PACK, HALF], F32, name, follows)
             nc.sync.dma_start(out=raw[:], in_=rows.rearrange("(p i) c -> p i c", i=PACK))
             return raw
 
-        def w1_piece(a, b):
-            raw = load_weight("raw_w1_%d%d" % (a, b), w1[a * PASS : (a + 1) * PASS, b * PASS : (b + 1) * PASS])
-            if a == 0:
-                new_grouped_weight("w1_%d" % b)
+        def w1_piece(a, b, dst, follows=None):
+            raw = load_weight(
+                "raw_w1_%d%d" % (a, b), w1[a * PASS : (a + 1) * PASS, b * PASS : (b + 1) * PASS], follows
+            )
             nc.scalar.copy(
-                out=grouped_pass("w1_%d" % b, a).rearrange("p (t m i) -> p m i t", t=PACK, i=PACK),
+                out=dst.rearrange("p (t m i) -> p m i t", t=PACK, i=PACK),
                 in_=raw[:].rearrange("p i (m t) -> p m i t", t=PACK),
             )
 
-        def wg_pass(b):
-            raw = load_weight("raw_wg_%d" % b, wg[b * PASS : (b + 1) * PASS, :])
-            if b == 0:
-                new_grouped_weight("wg")
-            group(grouped_pass("wg", b), raw[:])
-
         s_rows = sT.rearrange("(b p t) c -> b t p c", p=P, t=PACK)
-        slope = {}
+        s_win, s = {}, {}
 
-        def on_vector(u, half):
-            return (u, half) == (LAST, 0)
+        def load_s(u, follows=None):
+            s_win[u] = held([P, T], F32, "s_win%d" % u, follows)
+            nc.sync.dma_start(out=s_win[u][:], in_=s_rows[u // PACK, u % PACK])
 
-        def make_slope(u, half):
-            s = slope[u, half]
-            if on_vector(u, half):
-                nc.vector.scalar_tensor_tensor(out=s[:], in0=s[:], scalar=-1.0, in1=s[:], op0=ADD, op1=MULT)
-                return
-            rest = ring.tile([P, HALF], F32, name="rest%d%d" % (u, half), tag="rest%d" % half)
-            if u == LAST:
-                nc.gpsimd.tensor_scalar(rest[:], s[:], -1.0, 1.0, MULT, ADD)
-            else:
-                nc.scalar.activation(out=rest[:], in_=s[:], func=COPY, scale=-1.0, bias=1.0)
-            nc.gpsimd.tensor_tensor(s[:], s[:], rest[:], MULT)
+        def gather_s(u, half):
+            s[u, half] = held([P, HALF], F32, "s%d%d" % (u, half))
+            nc.vector.tensor_copy(
+                s[u, half][:], s_win[u][:].indirect(idx[:, half * LIST_COLS : (half + 1) * LIST_COLS])
+            )
 
-        def s_tile(u):
-            window = (staged if u else held)([P, T], F32, "s_win%d" % u)
-            nc.sync.dma_start(out=window[:], in_=s_rows[u // PACK, u % PACK])
-            for half in range(2):
-                slope[u, half] = held([P, HALF], F32, "slope%d%d" % (u, half))
-                nc.vector.tensor_copy(
-                    slope[u, half][:], window[:].indirect(idx[:, half * LIST_COLS : (half + 1) * LIST_COLS])
-                )
-            make_slope(u, 0)
+        def early_slope(u, half):
+            rest = ring.tile([P, HALF], F32, name="rest%d%d" % (u, half), tag="t", bufs=6)
+            nc.scalar.activation(out=rest[:], in_=s[u, half][:], func=COPY, scale=1.0, bias=-1.0)
+            nc.gpsimd.tensor_tensor(s[u, half][:], s[u, half][:], rest[:], MULT)
 
-        d_planes = {}
+        w1_codes, w1_scales, plane, parts = {}, {}, {}, {}
 
-        def make_d(u, half):
+        def make_d(u, half, follows=None, finish=True):
             b, t = divmod(u, PACK)
             h_bank = bank("h%d%d" % (u, half))
             entries = slice(half * HALF, (half + 1) * HALF)
+            words = slice(t * P, (t + 1) * P)
             for a in range(PASSES):
-                words = slice(a * PASS + t * P, a * PASS + (t + 1) * P)
                 nc.tensor.matmul_mx(
                     out=h_bank[:],
-                    lhsT=codes["w1_%d" % b][:, words].bitcast(E4M3),
-                    lhsT_scale=scales["w1_%d" % b][:, words],
+                    lhsT=w1_codes[a, b][:, words].bitcast(E4M3),
+                    lhsT_scale=w1_scales[a, b][:, words],
                     rhs=v_w[a][:, entries].bitcast(E5M2),
                     rhs_scale=v_sc[a][:, entries],
                     start=(a == 0),
                     stop=(a == PASSES - 1),
                 )
+            if u < EARLY:
+                nc.vector.tensor_tensor(plane[u, half], h_bank[:], s[u, half][:], MULT)
+                return
+            if follows:
+                part = held([P, HALF], F32, "part%d%d" % (u, half), follows)
+            else:
+                part = ring.tile([P, HALF], F32, name="part%d%d" % (u, half), tag="t", bufs=6)
             nc.vector.scalar_tensor_tensor(
-                out=d_planes[b, half][:, t, :],
-                in0=h_bank[:],
-                scalar=-1.0 if on_vector(u, half) else 1.0,
-                in1=slope[u, half][:],
-                op0=MULT,
-                op1=MULT,
+                out=part[:], in0=s[u, half][:], scalar=-1.0, in1=h_bank[:], op0=ADD, op1=MULT
             )
+            parts[u, half] = part
+            if finish:
+                finish_d(u, half)
 
-        def first_half_of_d(b, follows, grouped_follows=None):
-            d_planes[b, 0] = held([P, PACK, HALF], BF16, "d_planes%d0" % b, follows)
-            for u in range(b * PACK, (b + 1) * PACK):
-                make_d(u, 0)
-            grouped["d_%d0" % b] = held([P, PACK * HALF], BF16, "grouped_d_%d0" % b, grouped_follows)
-            group(grouped_pass("d_%d0" % b, 0), d_planes[b, 0][:])
+        def finish_d(u, half):
+            nc.gpsimd.tensor_tensor(plane[u, half], parts[u, half][:], s[u, half][:], MULT)
+
+        W = PACK * HALF
+
+        area_a = held([P, 2 * W + 3 * S], BF16, "area_a")
+        planes0 = area_a[:, 2 * W - S :].rearrange("p (i c) -> p i c", i=PACK)
+        for u in range(PACK):
+            for half in range(2):
+                plane[u, half] = planes0[:, u, half * HALF : (half + 1) * HALF]
+        area_b = held([P, 3 * HALF + W], BF16, "area_b")
+        planes11 = area_b[:, :W].rearrange("p (i c) -> p i c", i=PACK)
+        grouped_d10 = area_b[:, 3 * HALF :]
+        planes10 = held([P, PACK - DIRECT, HALF], BF16, "planes10")
+        for t in range(PACK):
+            plane[PACK + t, 1] = planes11[:, t, :]
+            if t < PACK - DIRECT:
+                plane[PACK + t, 0] = planes10[:, t, :]
+            else:
+                plane[PACK + t, 0] = grouped_d10.rearrange("p (c i) -> p c i", i=PACK)[:, :, t]
+
+        def w1_operand(a, b, grouped, follows):
+            w1_codes[a, b] = held([P, HALF], U32, "w1_codes%d%d" % (a, b), follows)
+            w1_scales[a, b] = held([P, HALF], U8, "w1_scales%d%d" % (a, b))
+            quantize(w1_codes[a, b][:], w1_scales[a, b][:], grouped)
 
         nc.sync.dma_start(idx[:], offs)
-        load_scale_rows(nc.scalar, tab_sc, tab_scales)
+        load_scale_rows(nc.sync, tab_sc, tab_scales, first=24)
+        picked_sc = held([P, S], U8, "picked_sc")
+        nc.vector.tensor_copy(picked_sc[:], tab_sc[:].indirect(idx[:]))
+        for a in range(PASSES):
+            shift = 24 + 4 * a
+            nc.scalar.dma_start(out=v_sc[a][0 : P - shift, :].bitcast(I32), in_=picked_sc[shift:P, :].bitcast(I32))
         table_pass(0)
-        s_tile(0)
-        v_sc[0] = held([P, S], U8, "v_sc0", follows="s_win0")
-        nc.vector.tensor_copy(v_sc[0][:], tab_sc[:].indirect(idx[:]))
-        nc.gpsimd.dma_start(out=v_sc[1][0 : P - 4, :].bitcast(I32), in_=v_sc[0][4:P, :].bitcast(I32))
         table_pass(1)
-        w1_piece(0, 0)
-        s_tile(1)
-        s_tile(2)
-        w1_piece(1, 0)
-        s_tile(3)
-        s_tile(4)
-        quantize("w1_0", follows="s_win4")
-        w1_piece(0, 1)
-        s_tile(5)
-        first_half_of_d(0, follows="s_win5")
-        w1_piece(1, 1)
-        s_tile(6)
-        quantize("w1_1", follows="s_win6")
-        s_tile(LAST)
-        wg_pass(0)
-        wg_pass(1)
-        first_half_of_d(1, follows="s_win%d" % LAST, grouped_follows="raw_wg_1")
-
-        wv_w = held([P, PASSES, N], U32, "wv_w", follows="raw_w1_01")
+        grouped_w = held([P, 2 * W], BF16, "grouped_w")
+        for a in range(PASSES):
+            load_s(a)
+            for half in range(2):
+                gather_s(a, half)
+            for half in range(2):
+                early_slope(a, half)
+            if a == 1:
+                w1_operand(0, 0, grouped_w[:, :W], follows="s_win1")
+            w1_piece(a, 0, grouped_w[:, a * W : (a + 1) * W])
+        load_s(2)
+        gather_s(2, 0)
+        gather_s(2, 1)
+        w1_operand(1, 0, grouped_w[:, W:], follows="s_win2")
+        load_s(3)
+        gather_s(3, 0)
+        gather_s(3, 1)
+        make_d(2, 0, follows="s_win3")
+        make_d(2, 1)
+        make_d(3, 0)
+        make_d(3, 1)
+        make_d(1, 0)
+        make_d(1, 1)
+        w1_piece(0, 1, area_a[:, :W], follows="tab_w0")
+        w1_piece(1, 1, area_a[:, W : 2 * W], follows="tab_w1")
+        load_s(4, follows="s_win0")
+        gather_s(4, 0)
+        gather_s(4, 1)
+        both = held([P, 2 * HALF], U32, "w1_codes_1", follows="s_win4")
+        both_sc = held([P, 2 * HALF], U8, "w1_scales_1")
+        for a in range(PASSES):
+            w1_codes[a, 1] = both[:, a * HALF : (a + 1) * HALF]
+            w1_scales[a, 1] = both_sc[:, a * HALF : (a + 1) * HALF]
+        quantize(both[:], both_sc[:], area_a[:, : 2 * W])
+        make_d(0, 0)
+        make_d(0, 1)
+        grouped_d00 = held([P, W], BF16, "grouped_d00")
+        group(grouped_d00[:], planes0[:, :, :HALF])
+        make_d(4, 0)
+        make_d(4, 1)
+        load_s(5, follows="raw_w1_00")
+        gather_s(5, 0)
+        gather_s(5, 1)
+        make_d(5, 0)
+        make_d(5, 1)
+        grouped_wg = held([P, 2 * W], BF16, "grouped_wg", follows="grouped_w")
+        raw = load_weight("raw_wg0", wg[:PASS, :], follows="raw_w1_10")
+        group(grouped_wg[:, :W], raw[:])
+        load_s(6, follows="part20")
+        gather_s(6, 0)
+        gather_s(6, 1)
+        make_d(6, 0)
+        make_d(6, 1)
+        raw = load_weight("raw_wg1", wg[PASS:, :], follows="raw_w1_01")
+        group(grouped_wg[:, W:], raw[:])
+        group(grouped_d10, planes10[:])
+        load_s(LAST, follows="raw_w1_11")
+        wv_w = held([P, PASSES, N], U32, "wv_w", follows="raw_wg0")
         nc.sync.dma_start(out=wv_w[:].bitcast(I32), in_=wv_words.rearrange("b p c i -> p b (c i)").bitcast(I32))
         load_scale_rows(nc.sync, wv_sc, wv_scales)
-        wgo_sb = held([P, S], F32, "wgo_sb", follows="raw_w1_11")
+        wgo_sb = held([P, S], F32, "wgo_sb", follows="s_win5")
         nc.sync.dma_start(out=wgo_sb[:], in_=wgo)
         nc.sync.dma_start(idx2[:], offs2)
 
-        both = held([P, PASSES, PACK, HALF], BF16, "d_planes1", follows="slope%d0" % LAST)
-        d_planes[0, 1], d_planes[1, 1] = both[:, 0], both[:, 1]
-        gate_operands = ("wg", "d_00", "d_10")
-        for u in range(ROW_TILES):
-            make_slope(u, 1)
-            make_d(u, 1)
-            if u < len(gate_operands):
-                quantize(gate_operands[u], follows="slope%d1" % u)
+        gather_s(LAST, 0)
+        make_d(LAST, 0)
+        gather_s(LAST, 1)
+        make_d(LAST, 1, finish=False)
+        late = held([P, 2 * N + HALF], U32, "late_codes", follows="s_win%d" % LAST)
+        wg_codes, wg_scales = late[:, : 2 * N], held([P, 2 * N], U8, "wg_scales")
+        d_codes = {(0, 0): late[:, 2 * N :], (1, 0): held([P, HALF], U32, "d_codes10")[:]}
+        d_scales = {(b, 0): held([P, HALF], U8, "d_scales%d0" % b)[:] for b in range(PASSES)}
+        quantize(wg_codes, wg_scales[:], grouped_wg[:])
+        quantize(d_codes[0, 0], d_scales[0, 0], grouped_d00[:])
+        quantize(d_codes[1, 0], d_scales[1, 0], grouped_d10)
+        finish_d(LAST, 1)
 
         def second_product(acc, half, lhsT, lhsT_scale):
             for b in range(PASSES):
-                key, words = ("d_%d0" % b, slice(0, HALF)) if half == 0 else ("d_1", slice(b * HALF, (b + 1) * HALF))
                 nc.tensor.matmul_mx(
                     out=acc[:],
                     lhsT=lhsT[b].bitcast(E4M3),
                     lhsT_scale=lhsT_scale[b],
-                    rhs=codes[key][:, words].bitcast(E4M3),
-                    rhs_scale=scales[key][:, words],
+                    rhs=d_codes[b, half].bitcast(E4M3),
+                    rhs_scale=d_scales[b, half],
                     start=(b == 0),
                     stop=(b == PASSES - 1),
                 )
@@ -256,15 +291,15 @@ def tile_list_botnet_gated_gradients_kernel(
             cols = slice(c * P, (c + 1) * P)
             gate = bank("gate%d" % i)
             wg_words = [slice(b * N + c * P, b * N + (c + 1) * P) for b in range(PASSES)]
-            second_product(gate, half, [codes["wg"][:, w] for w in wg_words], [scales["wg"][:, w] for w in wg_words])
+            second_product(gate, half, [wg_codes[:, w] for w in wg_words], [wg_scales[:, w] for w in wg_words])
             val = bank("val%d" % i)
             second_product(
                 val, half, [wv_w[:, b, cols] for b in range(PASSES)], [wv_sc[4 * b :, cols] for b in range(PASSES)]
             )
             sig = held([P, HALF], F32, "first_sig") if i == 0 else ring_f32("sig", i)
-            nc.scalar.activation(out=sig[:], in_=gate[:], func=SIGMOID)
-            y[i] = held([P, HALF], F32, "third_y", follows="d_planes1") if i == 2 else ring_f32("y", i)
-            nc.vector.tensor_tensor(y[i][:], val[:], sig[:], MULT)
+            nc.scalar.activation(out=sig[:], in_=gate[:], func=SIGMOID, scale=-1.0)
+            y[i] = held([P, HALF], F32, "second_y") if i == 1 else ring_f32("y", i)
+            nc.vector.scalar_tensor_tensor(out=y[i][:], in0=val[:], scalar=-1.0, in1=sig[:], op0=MULT, op1=MULT)
 
         def scatter(i):
             half, c = steps[i]
@@ -279,11 +314,20 @@ def tile_list_botnet_gated_gradients_kernel(
 
         make_y(0)
         make_y(1)
-        grouped["d_1"] = held([P, PASSES * PACK * HALF], BF16, "grouped_d_1", follows="first_sig")
+        grouped_d1 = held([P, 2 * W], BF16, "grouped_d1", follows="first_sig")
+        group(grouped_d1[:, :W], planes0[:, :, HALF:])
+        group(grouped_d1[:, W:], planes11)
+        scatter(0)
+        make_y(2)
+        scatter(1)
+        d1_codes = held([P, 2 * HALF], U32, "d1_codes", follows="second_y")
+        d1_scales = held([P, 2 * HALF], U8, "d1_scales")
         for b in range(PASSES):
-            group(grouped_pass("d_1", b), d_planes[b, 1])
-        quantize("d_1")
-        for i in range(len(steps)):
+            d_codes[b, 1] = d1_codes[:, b * HALF : (b + 1) * HALF]
+            d_scales[b, 1] = d1_scales[:, b * HALF : (b + 1) * HALF]
+        quantize(d1_codes[:], d1_scales[:], grouped_d1[:])
+        make_y(3)
+        for i in range(2, len(steps)):
             scatter(i)
             if i + 2 < len(steps):
                 make_y(i + 2)

@@ -30,7 +30,6 @@ PAGES = N // P
 RUN = 4
 BANKS = 8
 EARLY = 2
-DIRECT = 2
 
 
 def tile_list_botnet_gated_gradients_kernel(
@@ -58,13 +57,11 @@ def tile_list_botnet_gated_gradients_kernel(
         wv_sc = held([P, N], U8, "wv_sc")
         page = [held([P, T2], F32, "page%d" % c) for c in range(PAGES)]
 
+        nc.gpsimd.memset(wv_sc[:].bitcast(I32), 0)
         for quad in range(4):
             nc.gpsimd.memset(tab_sc[32 * quad : 32 * quad + 24, :].bitcast(I32), 0)
         for a in range(PASSES):
             nc.gpsimd.memset(v_sc[a][:].bitcast(I32), 0)
-        nc.gpsimd.memset(wv_sc[:].bitcast(I32), 0)
-        for c in range(PAGES):
-            nc.gpsimd.memset(page[c][:], 0.0)
 
         def load_scale_rows(queue, tile, scale_rows, first=0):
             for quad in range(4):
@@ -114,16 +111,29 @@ def tile_list_botnet_gated_gradients_kernel(
             s_win[u] = held([P, T], F32, "s_win%d" % u, follows)
             nc.sync.dma_start(out=s_win[u][:], in_=s_rows[u // PACK, u % PACK])
 
-        def gather_s(u, half):
-            s[u, half] = held([P, HALF], F32, "s%d%d" % (u, half))
+        def gather_s(u, half, follows=None):
+            s[u, half] = held([P, HALF], F32, "s%d%d" % (u, half), follows)
             nc.vector.tensor_copy(
                 s[u, half][:], s_win[u][:].indirect(idx[:, half * LIST_COLS : (half + 1) * LIST_COLS])
             )
 
-        def early_slope(u, half):
-            rest = ring.tile([P, HALF], F32, name="rest%d%d" % (u, half), tag="t", bufs=6)
+        slope = {}
+
+        def gather_both(u):
+            both_halves = held([P, S], F32, "s%d" % u)
+            nc.vector.tensor_copy(both_halves[:], s_win[u][:].indirect(idx[:]))
+            s[u, 0], s[u, 1] = both_halves[:, :HALF], both_halves[:, HALF:]
+
+        def early_slope(u, half, follows=None, rest_follows=None, rest=None):
+            if rest is not None:
+                pass
+            elif rest_follows:
+                rest = held([P, HALF], F32, "rest%d%d" % (u, half), rest_follows)
+            else:
+                rest = ring.tile([P, HALF], F32, name="rest%d%d" % (u, half), tag="t", bufs=6)
             nc.scalar.activation(out=rest[:], in_=s[u, half][:], func=COPY, scale=1.0, bias=-1.0)
-            nc.gpsimd.tensor_tensor(s[u, half][:], s[u, half][:], rest[:], MULT)
+            slope[u, half] = held([P, HALF], F32, "slope%d%d" % (u, half), follows) if follows else s[u, half]
+            nc.gpsimd.tensor_tensor(slope[u, half][:], s[u, half][:], rest[:], MULT)
 
         w1_codes, w1_scales, plane, parts = {}, {}, {}, {}
 
@@ -142,10 +152,12 @@ def tile_list_botnet_gated_gradients_kernel(
                     start=(a == 0),
                     stop=(a == PASSES - 1),
                 )
-            if u < EARLY:
-                nc.vector.tensor_tensor(plane[u, half], h_bank[:], s[u, half][:], MULT)
+            if (u, half) in slope:
+                nc.vector.tensor_tensor(plane[u, half], h_bank[:], slope[u, half][:], MULT)
                 return
-            if follows:
+            if (u, half) in parts:
+                part = parts[u, half]
+            elif follows:
                 part = held([P, HALF], F32, "part%d%d" % (u, half), follows)
             else:
                 part = ring.tile([P, HALF], F32, name="part%d%d" % (u, half), tag="t", bufs=6)
@@ -161,21 +173,13 @@ def tile_list_botnet_gated_gradients_kernel(
 
         W = PACK * HALF
 
-        area_a = held([P, 2 * W + 3 * S], BF16, "area_a")
-        planes0 = area_a[:, 2 * W - S :].rearrange("p (i c) -> p i c", i=PACK)
-        for u in range(PACK):
-            for half in range(2):
-                plane[u, half] = planes0[:, u, half * HALF : (half + 1) * HALF]
-        area_b = held([P, 3 * HALF + W], BF16, "area_b")
-        planes11 = area_b[:, :W].rearrange("p (i c) -> p i c", i=PACK)
-        grouped_d10 = area_b[:, 3 * HALF :]
-        planes10 = held([P, PACK - DIRECT, HALF], BF16, "planes10")
-        for t in range(PACK):
-            plane[PACK + t, 1] = planes11[:, t, :]
-            if t < PACK - DIRECT:
-                plane[PACK + t, 0] = planes10[:, t, :]
-            else:
-                plane[PACK + t, 0] = grouped_d10.rearrange("p (c i) -> p c i", i=PACK)[:, :, t]
+        def new_planes(b, half, follows=None):
+            tile = held([P, PACK, HALF], BF16, "planes%d%d" % (b, half), follows)
+            for t in range(PACK):
+                plane[b * PACK + t, half] = tile[:, t, :]
+            return tile
+
+        planes = {(0, half): new_planes(0, half) for half in range(2)}
 
         def w1_operand(a, b, grouped, follows):
             w1_codes[a, b] = held([P, HALF], U32, "w1_codes%d%d" % (a, b), follows)
@@ -183,151 +187,163 @@ def tile_list_botnet_gated_gradients_kernel(
             quantize(w1_codes[a, b][:], w1_scales[a, b][:], grouped)
 
         nc.sync.dma_start(idx[:], offs)
+        nc.sync.dma_start(idx2[:], offs2)
         load_scale_rows(nc.sync, tab_sc, tab_scales, first=24)
         picked_sc = held([P, S], U8, "picked_sc")
         nc.vector.tensor_copy(picked_sc[:], tab_sc[:].indirect(idx[:]))
         for a in range(PASSES):
             shift = 24 + 4 * a
             nc.scalar.dma_start(out=v_sc[a][0 : P - shift, :].bitcast(I32), in_=picked_sc[shift:P, :].bitcast(I32))
+        for c in range(PAGES):
+            nc.gpsimd.memset(page[c][:], 0.0)
         table_pass(0)
         table_pass(1)
+        load_scale_rows(nc.sync, wv_sc, wv_scales)
         grouped_w = held([P, 2 * W], BF16, "grouped_w")
         for a in range(PASSES):
             load_s(a)
-            for half in range(2):
-                gather_s(a, half)
+            gather_both(a)
             for half in range(2):
                 early_slope(a, half)
             if a == 1:
                 w1_operand(0, 0, grouped_w[:, :W], follows="s_win1")
             w1_piece(a, 0, grouped_w[:, a * W : (a + 1) * W])
         load_s(2)
-        gather_s(2, 0)
-        gather_s(2, 1)
+        gather_both(2)
         w1_operand(1, 0, grouped_w[:, W:], follows="s_win2")
         load_s(3)
-        gather_s(3, 0)
-        gather_s(3, 1)
-        make_d(2, 0, follows="s_win3")
+        gather_both(3)
+        part2 = held([P, S], F32, "part2", follows="s_win3")
+        parts[2, 0], parts[2, 1] = part2[:, :HALF], part2[:, HALF:]
+        make_d(2, 0)
         make_d(2, 1)
         make_d(3, 0)
         make_d(3, 1)
-        make_d(1, 0)
-        make_d(1, 1)
-        w1_piece(0, 1, area_a[:, :W], follows="tab_w0")
-        w1_piece(1, 1, area_a[:, W : 2 * W], follows="tab_w1")
+        for u in range(EARLY):
+            make_d(u, 0)
+            make_d(u, 1)
+        grouped_w1 = held([P, 2 * W], BF16, "grouped_w1")
+        w1_piece(0, 1, grouped_w1[:, :W], follows="tab_w0")
+        w1_piece(1, 1, grouped_w1[:, W:], follows="tab_w1")
+        grouped_d00 = held([P, W], BF16, "grouped_d00", follows="raw_w1_01")
+        group(grouped_d00[:], planes[0, 0][:])
         load_s(4, follows="s_win0")
-        gather_s(4, 0)
-        gather_s(4, 1)
+        gather_both(4)
         both = held([P, 2 * HALF], U32, "w1_codes_1", follows="s_win4")
         both_sc = held([P, 2 * HALF], U8, "w1_scales_1")
         for a in range(PASSES):
             w1_codes[a, 1] = both[:, a * HALF : (a + 1) * HALF]
             w1_scales[a, 1] = both_sc[:, a * HALF : (a + 1) * HALF]
-        quantize(both[:], both_sc[:], area_a[:, : 2 * W])
-        make_d(0, 0)
-        make_d(0, 1)
-        grouped_d00 = held([P, W], BF16, "grouped_d00")
-        group(grouped_d00[:], planes0[:, :, :HALF])
-        make_d(4, 0)
-        make_d(4, 1)
-        load_s(5, follows="raw_w1_00")
-        gather_s(5, 0)
-        gather_s(5, 1)
-        make_d(5, 0)
-        make_d(5, 1)
+        quantize(both[:], both_sc[:], grouped_w1[:])
+        early_slope(4, 1)
+        planes[1, 0] = new_planes(1, 0, follows="raw_w1_11")
+        load_s(5)
+        gather_both(5)
+        for u in (4, 5):
+            make_d(u, 0)
         grouped_wg = held([P, 2 * W], BF16, "grouped_wg", follows="grouped_w")
-        raw = load_weight("raw_wg0", wg[:PASS, :], follows="raw_w1_10")
+        raw = load_weight("raw_wg0", wg[:PASS, :], follows=None)
         group(grouped_wg[:, :W], raw[:])
-        load_s(6, follows="part20")
+        early_slope(5, 1, rest_follows="raw_wg0")
+        load_s(6, follows="raw_w1_00")
         gather_s(6, 0)
         gather_s(6, 1)
         make_d(6, 0)
-        make_d(6, 1)
-        raw = load_weight("raw_wg1", wg[PASS:, :], follows="raw_w1_01")
+
+        raw = load_weight("raw_wg1", wg[PASS:, :], follows=None)
         group(grouped_wg[:, W:], raw[:])
-        group(grouped_d10, planes10[:])
-        load_s(LAST, follows="raw_w1_11")
-        wv_w = held([P, PASSES, N], U32, "wv_w", follows="raw_wg0")
+        area = held([P, W + 2 * HALF], BF16, "grouped_d10", follows="raw_wg1")
+        grouped_d10 = area[:, :W]
+        group(grouped_d10[:], planes[1, 0][:, :2], 0)
+        load_s(LAST, follows="raw_w1_10")
+        wv_w = held([P, PASSES, N], U32, "wv_w", follows="w1_codes00")
         nc.sync.dma_start(out=wv_w[:].bitcast(I32), in_=wv_words.rearrange("b p c i -> p b (c i)").bitcast(I32))
-        load_scale_rows(nc.sync, wv_sc, wv_scales)
-        wgo_sb = held([P, S], F32, "wgo_sb", follows="s_win5")
-        nc.sync.dma_start(out=wgo_sb[:], in_=wgo)
-        nc.sync.dma_start(idx2[:], offs2)
 
         gather_s(LAST, 0)
-        make_d(LAST, 0)
-        gather_s(LAST, 1)
-        make_d(LAST, 1, finish=False)
-        late = held([P, 2 * N + HALF], U32, "late_codes", follows="s_win%d" % LAST)
-        wg_codes, wg_scales = late[:, : 2 * N], held([P, 2 * N], U8, "wg_scales")
-        d_codes = {(0, 0): late[:, 2 * N :], (1, 0): held([P, HALF], U32, "d_codes10")[:]}
+        parts[LAST, 0] = held([P, HALF], F32, "part%d0" % LAST)
+        make_d(LAST, 0, finish=False)
+        nc.vector.tensor_tensor(plane[LAST, 0], parts[LAST, 0][:], s[LAST, 0][:], MULT)
+        group(grouped_d10[:], planes[1, 0][:, 2:], 2)
+        wg_codes = held([P, PASSES * N], U32, "wg_codes", follows="part%d0" % LAST)
+        wg_scales = held([P, PASSES * N], U8, "wg_scales")
+        quantize(wg_codes[:], wg_scales[:], grouped_wg[:])
+        d_codes = {(0, 0): held([P, HALF], U32, "d_codes00", follows="s%d0" % LAST)[:]}
+        d_codes[1, 0] = held([P, HALF], U32, "d_codes10")[:]
         d_scales = {(b, 0): held([P, HALF], U8, "d_scales%d0" % b)[:] for b in range(PASSES)}
-        quantize(wg_codes, wg_scales[:], grouped_wg[:])
         quantize(d_codes[0, 0], d_scales[0, 0], grouped_d00[:])
-        quantize(d_codes[1, 0], d_scales[1, 0], grouped_d10)
-        finish_d(LAST, 1)
+        gather_s(LAST, 1, follows="grouped_wg")
+        early_slope(6, 1, follows="grouped_d00", rest=area[:, W:].bitcast(F32))
+        quantize(d_codes[1, 0], d_scales[1, 0], grouped_d10[:])
+        planes[1, 1] = new_planes(1, 1, follows="grouped_d10")
+        for u in (LAST, 4, 5, 6):
+            make_d(u, 1)
+        wgo_sb = held([P, S], F32, "wgo_sb", follows="w1_codes10")
+        nc.sync.dma_start(out=wgo_sb[:], in_=wgo)
 
-        def second_product(acc, half, lhsT, lhsT_scale):
-            for b in range(PASSES):
-                nc.tensor.matmul_mx(
-                    out=acc[:],
-                    lhsT=lhsT[b].bitcast(E4M3),
-                    lhsT_scale=lhsT_scale[b],
-                    rhs=d_codes[b, half].bitcast(E4M3),
-                    rhs_scale=d_scales[b, half],
-                    start=(b == 0),
-                    stop=(b == PASSES - 1),
-                )
+        def second_pass(acc, half, b, lhsT, lhsT_scale):
+            nc.tensor.matmul_mx(
+                out=acc[:],
+                lhsT=lhsT.bitcast(E4M3),
+                lhsT_scale=lhsT_scale,
+                rhs=d_codes[b, half].bitcast(E4M3),
+                rhs_scale=d_scales[b, half],
+                start=(b == 0),
+                stop=(b == PASSES - 1),
+            )
 
-        steps = [(half, c) for half in range(2) for c in range(PAGES)]
         y = {}
 
-        def ring_f32(kind, i):
-            return ring.tile([P, HALF], F32, name="%s%d" % (kind, i), tag=kind, bufs=3)
+        def make_y(half, k, follows=None):
+            pair = (2 * k, 2 * k + 1)
+            sig, val = {}, {}
+            for c in pair:
+                gate = bank("gate%d%d" % (half, c))
+                for b in range(PASSES):
+                    words = slice(b * N + c * P, b * N + (c + 1) * P)
+                    second_pass(gate, half, b, wg_codes[:, words], wg_scales[:, words])
+                sig[c] = held([P, HALF], F32, "sig%d%d" % (half, c), "sig0%d" % c if half else "s%d" % c)
+                nc.scalar.activation(out=sig[c][:], in_=gate[:], func=SIGMOID, scale=-1.0)
+            for c in pair:
+                val[c] = bank("val%d%d" % (half, c))
+            for b in range(PASSES):
+                for c in pair:
+                    cols = slice(c * P, (c + 1) * P)
+                    second_pass(val[c], half, b, wv_w[:, b, cols], wv_sc[4 * b :, cols])
+            both_y = held([P, 2, HALF], F32, "y%d%d" % (half, k), follows)
+            for c in pair:
+                y[half, c] = both_y[:, c % 2, :]
+                nc.vector.scalar_tensor_tensor(
+                    out=y[half, c], in0=val[c][:], scalar=-1.0, in1=sig[c][:], op0=MULT, op1=MULT
+                )
 
-        def make_y(i):
-            half, c = steps[i]
-            cols = slice(c * P, (c + 1) * P)
-            gate = bank("gate%d" % i)
-            wg_words = [slice(b * N + c * P, b * N + (c + 1) * P) for b in range(PASSES)]
-            second_product(gate, half, [wg_codes[:, w] for w in wg_words], [wg_scales[:, w] for w in wg_words])
-            val = bank("val%d" % i)
-            second_product(
-                val, half, [wv_w[:, b, cols] for b in range(PASSES)], [wv_sc[4 * b :, cols] for b in range(PASSES)]
-            )
-            sig = held([P, HALF], F32, "first_sig") if i == 0 else ring_f32("sig", i)
-            nc.scalar.activation(out=sig[:], in_=gate[:], func=SIGMOID, scale=-1.0)
-            y[i] = held([P, HALF], F32, "second_y") if i == 1 else ring_f32("y", i)
-            nc.vector.scalar_tensor_tensor(out=y[i][:], in0=val[:], scalar=-1.0, in1=sig[:], op0=MULT, op1=MULT)
-
-        def scatter(i):
-            half, c = steps[i]
+        def scatter(half, c):
             nc.vector.tensor_tensor(
                 page[c][:].indirect(idx2[:, half * LIST_COLS : (half + 1) * LIST_COLS]),
-                y[i][:],
+                y[half, c],
                 wgo_sb[:, half * HALF : (half + 1) * HALF],
                 MULT,
             )
             if half == 1:
                 nc.sync.dma_start(out=out[c * P : (c + 1) * P, :], in_=page[c][:])
 
-        make_y(0)
-        make_y(1)
-        grouped_d1 = held([P, 2 * W], BF16, "grouped_d1", follows="first_sig")
-        group(grouped_d1[:, :W], planes0[:, :, HALF:])
-        group(grouped_d1[:, W:], planes11)
-        scatter(0)
-        make_y(2)
-        scatter(1)
-        d1_codes = held([P, 2 * HALF], U32, "d1_codes", follows="second_y")
+        make_y(0, 0)
+        grouped_d1 = held([P, 2 * W], BF16, "grouped_d1", follows="s5")
+        group(grouped_d1[:, :W], planes[0, 1][:])
+        group(grouped_d1[:, W:], planes[1, 1][:])
+        scatter(0, 0)
+        scatter(0, 1)
+        d1_codes = held([P, 2 * HALF], U32, "d1_codes", follows="y00")
         d1_scales = held([P, 2 * HALF], U8, "d1_scales")
         for b in range(PASSES):
             d_codes[b, 1] = d1_codes[:, b * HALF : (b + 1) * HALF]
             d_scales[b, 1] = d1_scales[:, b * HALF : (b + 1) * HALF]
         quantize(d1_codes[:], d1_scales[:], grouped_d1[:])
-        make_y(3)
-        for i in range(2, len(steps)):
-            scatter(i)
-            if i + 2 < len(steps):
-                make_y(i + 2)
+        make_y(0, 1, follows="grouped_d1")
+        scatter(0, 2)
+        scatter(0, 3)
+        make_y(1, 0, follows="part2")
+        scatter(1, 0)
+        scatter(1, 1)
+        make_y(1, 1, follows="y01")
+        scatter(1, 2)
+        scatter(1, 3)

@@ -119,8 +119,8 @@ def tile_list_botnet_gated_gradients_kernel(
 
         slope = {}
 
-        def gather_both(u):
-            both_halves = held([P, S], F32, "s%d" % u)
+        def gather_both(u, follows=None):
+            both_halves = held([P, S], F32, "s%d" % u, follows)
             nc.vector.tensor_copy(both_halves[:], s_win[u][:].indirect(idx[:]))
             s[u, 0], s[u, 1] = both_halves[:, :HALF], both_halves[:, HALF:]
 
@@ -225,7 +225,7 @@ def tile_list_botnet_gated_gradients_kernel(
         grouped_w1 = held([P, 2 * W], BF16, "grouped_w1")
         w1_piece(0, 1, grouped_w1[:, :W], follows="tab_w0")
         w1_piece(1, 1, grouped_w1[:, W:], follows="tab_w1")
-        grouped_d00 = held([P, W], BF16, "grouped_d00", follows="raw_w1_01")
+        grouped_d00 = held([P, W], BF16, "grouped_d00", follows="raw_w1_11")
         group(grouped_d00[:], planes[0, 0][:])
         load_s(4, follows="s_win0")
         gather_both(4)
@@ -236,15 +236,16 @@ def tile_list_botnet_gated_gradients_kernel(
             w1_scales[a, 1] = both_sc[:, a * HALF : (a + 1) * HALF]
         quantize(both[:], both_sc[:], grouped_w1[:])
         early_slope(4, 1)
-        planes[1, 0] = new_planes(1, 0, follows="raw_w1_11")
+        planes[1, 0] = new_planes(1, 0, follows="raw_w1_01")
         load_s(5)
-        gather_both(5)
+        gather_both(5, follows="grouped_w1")
+        parts[5, 0] = held([P, HALF], F32, "part50")
         for u in (4, 5):
             make_d(u, 0)
         grouped_wg = held([P, 2 * W], BF16, "grouped_wg", follows="grouped_w")
         raw = load_weight("raw_wg0", wg[:PASS, :], follows=None)
         group(grouped_wg[:, :W], raw[:])
-        early_slope(5, 1, rest_follows="raw_wg0")
+        early_slope(5, 1, follows="part50", rest_follows="raw_wg0")
         load_s(6, follows="raw_w1_00")
         gather_s(6, 0)
         gather_s(6, 1)
@@ -256,7 +257,7 @@ def tile_list_botnet_gated_gradients_kernel(
         grouped_d10 = area[:, :W]
         group(grouped_d10[:], planes[1, 0][:, :2], 0)
         load_s(LAST, follows="raw_w1_10")
-        wv_w = held([P, PASSES, N], U32, "wv_w", follows="w1_codes00")
+        wv_w = held([P, PASSES, N], U32, "wv_w", follows="s_win5")
         nc.sync.dma_start(out=wv_w[:].bitcast(I32), in_=wv_words.rearrange("b p c i -> p b (c i)").bitcast(I32))
 
         gather_s(LAST, 0)
@@ -277,7 +278,7 @@ def tile_list_botnet_gated_gradients_kernel(
         planes[1, 1] = new_planes(1, 1, follows="grouped_d10")
         for u in (LAST, 4, 5, 6):
             make_d(u, 1)
-        wgo_sb = held([P, S], F32, "wgo_sb", follows="w1_codes10")
+        wgo_sb = held([P, S], F32, "wgo_sb", follows="s_win6")
         nc.sync.dma_start(out=wgo_sb[:], in_=wgo)
 
         def second_pass(acc, half, b, lhsT, lhsT_scale):
@@ -327,7 +328,7 @@ def tile_list_botnet_gated_gradients_kernel(
                 nc.sync.dma_start(out=out[c * P : (c + 1) * P, :], in_=page[c][:])
 
         make_y(0, 0)
-        grouped_d1 = held([P, 2 * W], BF16, "grouped_d1", follows="s5")
+        grouped_d1 = held([P, 2 * W], BF16, "grouped_d1", follows="slope51")
         group(grouped_d1[:, :W], planes[0, 1][:])
         group(grouped_d1[:, W:], planes[1, 1][:])
         scatter(0, 0)

@@ -294,7 +294,7 @@ def tile_list_botnet_gated_gradients_kernel(
 
         y = {}
 
-        def make_y(half, k, follows=None):
+        def products(half, k, sig_follows):
             pair = (2 * k, 2 * k + 1)
             sig, val = {}, {}
             for c in pair:
@@ -302,7 +302,7 @@ def tile_list_botnet_gated_gradients_kernel(
                 for b in range(PASSES):
                     words = slice(b * N + c * P, b * N + (c + 1) * P)
                     second_pass(gate, half, b, wg_codes[:, words], wg_scales[:, words])
-                sig[c] = held([P, HALF], F32, "sig%d%d" % (half, c), "sig0%d" % c if half else "s%d" % c)
+                sig[c] = held([P, HALF], F32, "sig%d%d" % (half, c), sig_follows[c % 2])
                 nc.scalar.activation(out=sig[c][:], in_=gate[:], func=SIGMOID, scale=-1.0)
             for c in pair:
                 val[c] = bank("val%d%d" % (half, c))
@@ -310,27 +310,37 @@ def tile_list_botnet_gated_gradients_kernel(
                 for c in pair:
                     cols = slice(c * P, (c + 1) * P)
                     second_pass(val[c], half, b, wv_w[:, b, cols], wv_sc[4 * b :, cols])
-            both_y = held([P, 2, HALF], F32, "y%d%d" % (half, k), follows)
+            return pair, sig, val
+
+        def y_on_vector(half, k):
+            pair, sig, val = products(half, k, ("s0", "s1"))
+            both_y = held([P, 2, HALF], F32, "y%d%d" % (half, k))
             for c in pair:
                 y[half, c] = both_y[:, c % 2, :]
                 nc.vector.scalar_tensor_tensor(
                     out=y[half, c], in0=val[c][:], scalar=-1.0, in1=sig[c][:], op0=MULT, op1=MULT
                 )
+            for c in pair:
+                nc.vector.tensor_tensor(y[half, c], y[half, c], wgo_sb[:, half * HALF : (half + 1) * HALF], MULT)
+
+        def y_on_gpsimd(half, k, sig_follows):
+            pair, sig, val = products(half, k, sig_follows)
+            for c in pair:
+                y[half, c] = ring.tile([P, HALF], F32, name="y%d%d" % (half, c), tag="y", bufs=4)[:]
+                nc.scalar.activation(out=y[half, c], in_=val[c][:], func=COPY, scale=-1.0)
+                nc.gpsimd.tensor_tensor(sig[c][:], sig[c][:], wgo_sb[:, half * HALF : (half + 1) * HALF], MULT)
+                nc.gpsimd.tensor_tensor(y[half, c], y[half, c], sig[c][:], MULT)
 
         def scatter(half, c):
-            nc.vector.tensor_tensor(
-                page[c][:].indirect(idx2[:, half * LIST_COLS : (half + 1) * LIST_COLS]),
-                y[half, c],
-                wgo_sb[:, half * HALF : (half + 1) * HALF],
-                MULT,
-            )
+            nc.vector.tensor_copy(page[c][:].indirect(idx2[:, half * LIST_COLS : (half + 1) * LIST_COLS]), y[half, c])
             if half == 1:
                 nc.sync.dma_start(out=out[c * P : (c + 1) * P, :], in_=page[c][:])
 
-        make_y(0, 0)
+        y_on_vector(0, 0)
         grouped_d1 = held([P, 2 * W], BF16, "grouped_d1", follows="slope51")
         group(grouped_d1[:, :W], planes[0, 1][:])
         group(grouped_d1[:, W:], planes[1, 1][:])
+        y_on_gpsimd(0, 1, ("planes11", "planes01"))
         scatter(0, 0)
         scatter(0, 1)
         d1_codes = held([P, 2 * HALF], U32, "d1_codes", follows="y00")
@@ -339,12 +349,9 @@ def tile_list_botnet_gated_gradients_kernel(
             d_codes[b, 1] = d1_codes[:, b * HALF : (b + 1) * HALF]
             d_scales[b, 1] = d1_scales[:, b * HALF : (b + 1) * HALF]
         quantize(d1_codes[:], d1_scales[:], grouped_d1[:])
-        make_y(0, 1, follows="grouped_d1")
         scatter(0, 2)
         scatter(0, 3)
-        make_y(1, 0, follows="part2")
-        scatter(1, 0)
-        scatter(1, 1)
-        make_y(1, 1, follows="y01")
-        scatter(1, 2)
-        scatter(1, 3)
+        for k in range(2):
+            y_on_gpsimd(1, k, ("s2", "s3") if k == 0 else ("sig00", "sig01"))
+            scatter(1, 2 * k)
+            scatter(1, 2 * k + 1)

@@ -52,31 +52,31 @@ def tile_list_botnet_gated_gradients_kernel(
 
         idx = held([P, S // 16], U16, "idx")
         idx2 = held([P, S // 16], U16, "idx2")
-        tab_sc = held([P, T], U8, "tab_sc")
+        tab_sc = held([P, PASSES * T], U8, "tab_sc")
         v_sc = {a: held([P, S], U8, "v_sc%d" % a) for a in range(PASSES)}
-        wv_sc = held([P, N], U8, "wv_sc")
+        wv_sc = held([P, PASSES * N], U8, "wv_sc")
         page = [held([P, T2], F32, "page%d" % c) for c in range(PAGES)]
 
+        nc.gpsimd.memset(tab_sc[:].bitcast(I32), 0)
         nc.gpsimd.memset(wv_sc[:].bitcast(I32), 0)
-        for quad in range(4):
-            nc.gpsimd.memset(tab_sc[32 * quad : 32 * quad + 24, :].bitcast(I32), 0)
-        for a in range(PASSES):
-            nc.gpsimd.memset(v_sc[a][:].bitcast(I32), 0)
 
-        def load_scale_rows(queue, tile, scale_rows, first=0):
+        def load_scale_rows(tile, scale_rows):
             for quad in range(4):
-                queue.dma_start(
-                    out=tile[32 * quad + first : 32 * quad + first + 8, :].bitcast(I32),
-                    in_=scale_rows[:, 4 * quad : 4 * quad + 4, :].bitcast(I32),
+                nc.sync.dma_start(
+                    out=tile[32 * quad : 32 * quad + 4, :].bitcast(I32).rearrange("x (a c) -> x a c", a=PASSES),
+                    in_=scale_rows[:, 4 * quad : 4 * quad + 4, :].bitcast(I32).rearrange("a x c -> x a c"),
                 )
+
+        def load_in_halves(window, rows):
+            for half in range(2):
+                cols = slice(half * T // 2, (half + 1) * T // 2)
+                nc.sync.dma_start(out=window[:, cols], in_=rows[:, cols])
 
         v_w = {}
 
         def table_pass(a):
             window = held([P, T], U32, "tab_w%d" % a)
-            nc.sync.dma_start(
-                out=window[:].bitcast(I32), in_=tab_words[a].rearrange("p t i -> p (t i)").bitcast(I32)
-            )
+            load_in_halves(window[:].bitcast(I32), tab_words[a].rearrange("p t i -> p (t i)").bitcast(I32))
             v_w[a] = held([P, S], U32, "v_w%d" % a)
             nc.vector.tensor_copy(v_w[a][:], window[:].indirect(idx[:]))
 
@@ -109,7 +109,10 @@ def tile_list_botnet_gated_gradients_kernel(
 
         def load_s(u, follows=None):
             s_win[u] = held([P, T], F32, "s_win%d" % u, follows)
-            nc.sync.dma_start(out=s_win[u][:], in_=s_rows[u // PACK, u % PACK])
+            if u == 0:
+                load_in_halves(s_win[u][:], s_rows[0, 0])
+            else:
+                nc.sync.dma_start(out=s_win[u][:], in_=s_rows[u // PACK, u % PACK])
 
         def gather_s(u, half, follows=None):
             s[u, half] = held([P, HALF], F32, "s%d%d" % (u, half), follows)
@@ -188,26 +191,27 @@ def tile_list_botnet_gated_gradients_kernel(
 
         nc.sync.dma_start(idx[:], offs)
         nc.sync.dma_start(idx2[:], offs2)
-        load_scale_rows(nc.sync, tab_sc, tab_scales, first=24)
-        picked_sc = held([P, S], U8, "picked_sc")
-        nc.vector.tensor_copy(picked_sc[:], tab_sc[:].indirect(idx[:]))
-        for a in range(PASSES):
-            shift = 24 + 4 * a
-            nc.scalar.dma_start(out=v_sc[a][0 : P - shift, :].bitcast(I32), in_=picked_sc[shift:P, :].bitcast(I32))
         for c in range(PAGES):
             nc.gpsimd.memset(page[c][:], 0.0)
         table_pass(0)
         table_pass(1)
-        load_scale_rows(nc.sync, wv_sc, wv_scales)
         grouped_w = held([P, 2 * W], BF16, "grouped_w")
         for a in range(PASSES):
             load_s(a)
             gather_both(a)
-            for half in range(2):
-                early_slope(a, half)
+            if a == 0:
+                load_scale_rows(tab_sc, tab_scales)
+                for b in range(PASSES):
+                    nc.vector.tensor_copy(v_sc[b][:], tab_sc[:, b * T : (b + 1) * T].indirect(idx[:]))
+            if a == 0:
+                for half in range(2):
+                    early_slope(a, half)
             if a == 1:
                 w1_operand(0, 0, grouped_w[:, :W], follows="s_win1")
             w1_piece(a, 0, grouped_w[:, a * W : (a + 1) * W])
+        rest1 = held([P, S], F32, "rest1", follows="raw_w1_10")
+        for half in range(2):
+            early_slope(1, half, rest=rest1[:, half * HALF : (half + 1) * HALF])
         load_s(2)
         gather_both(2)
         w1_operand(1, 0, grouped_w[:, W:], follows="s_win2")
@@ -227,7 +231,7 @@ def tile_list_botnet_gated_gradients_kernel(
         w1_piece(1, 1, grouped_w1[:, W:], follows="tab_w1")
         grouped_d00 = held([P, W], BF16, "grouped_d00", follows="raw_w1_11")
         group(grouped_d00[:], planes[0, 0][:])
-        load_s(4, follows="s_win0")
+        load_s(4)
         gather_both(4)
         both = held([P, 2 * HALF], U32, "w1_codes_1", follows="s_win4")
         both_sc = held([P, 2 * HALF], U8, "w1_scales_1")
@@ -237,7 +241,7 @@ def tile_list_botnet_gated_gradients_kernel(
         quantize(both[:], both_sc[:], grouped_w1[:])
         early_slope(4, 1)
         planes[1, 0] = new_planes(1, 0, follows="raw_w1_01")
-        load_s(5)
+        load_s(5, follows="s_win0")
         gather_both(5, follows="grouped_w1")
         parts[5, 0] = held([P, HALF], F32, "part50")
         for u in (4, 5):
@@ -256,7 +260,7 @@ def tile_list_botnet_gated_gradients_kernel(
         area = held([P, W + 2 * HALF], BF16, "grouped_d10", follows="raw_wg1")
         grouped_d10 = area[:, :W]
         group(grouped_d10[:], planes[1, 0][:, :2], 0)
-        load_s(LAST, follows="raw_w1_10")
+        load_s(LAST, follows="rest1")
         wv_w = held([P, PASSES, N], U32, "wv_w", follows="s_win5")
         nc.sync.dma_start(out=wv_w[:].bitcast(I32), in_=wv_words.rearrange("b p c i -> p b (c i)").bitcast(I32))
 
@@ -278,6 +282,7 @@ def tile_list_botnet_gated_gradients_kernel(
         planes[1, 1] = new_planes(1, 1, follows="grouped_d10")
         for u in (LAST, 4, 5, 6):
             make_d(u, 1)
+        load_scale_rows(wv_sc, wv_scales)
         wgo_sb = held([P, S], F32, "wgo_sb", follows="s_win6")
         nc.sync.dma_start(out=wgo_sb[:], in_=wgo)
 
@@ -309,7 +314,7 @@ def tile_list_botnet_gated_gradients_kernel(
             for b in range(PASSES):
                 for c in pair:
                     cols = slice(c * P, (c + 1) * P)
-                    second_pass(val[c], half, b, wv_w[:, b, cols], wv_sc[4 * b :, cols])
+                    second_pass(val[c], half, b, wv_w[:, b, cols], wv_sc[:, b * N + c * P : b * N + (c + 1) * P])
             return pair, sig, val
 
         def y_on_vector(half, k):

@@ -127,7 +127,7 @@ def tile_list_botnet_gated_gradients_kernel(
             nc.vector.tensor_copy(both_halves[:], s_win[u][:].indirect(idx[:]))
             s[u, 0], s[u, 1] = both_halves[:, :HALF], both_halves[:, HALF:]
 
-        def early_slope(u, half, follows=None, rest_follows=None, rest=None):
+        def early_slope(u, half, follows=None, rest_follows=None, rest=None, dst=None):
             if rest is not None:
                 pass
             elif rest_follows:
@@ -136,6 +136,8 @@ def tile_list_botnet_gated_gradients_kernel(
                 rest = ring.tile([P, HALF], F32, name="rest%d%d" % (u, half), tag="t", bufs=6)
             nc.scalar.activation(out=rest[:], in_=s[u, half][:], func=COPY, scale=1.0, bias=-1.0)
             slope[u, half] = held([P, HALF], F32, "slope%d%d" % (u, half), follows) if follows else s[u, half]
+            if dst is not None:
+                slope[u, half] = dst
             nc.gpsimd.tensor_tensor(slope[u, half][:], s[u, half][:], rest[:], MULT)
 
         w1_codes, w1_scales, plane, parts = {}, {}, {}, {}
@@ -240,16 +242,20 @@ def tile_list_botnet_gated_gradients_kernel(
             w1_scales[a, 1] = both_sc[:, a * HALF : (a + 1) * HALF]
         quantize(both[:], both_sc[:], grouped_w1[:])
         early_slope(4, 1)
-        planes[1, 0] = new_planes(1, 0, follows="raw_w1_01")
+        area_d = held([P, 5 * W // 2], BF16, "area_d", follows="raw_w1_01")
+        planes[1, 0] = area_d[:, :W].rearrange("p (i c) -> p i c", i=PACK)
+        for t in range(PACK):
+            plane[PACK + t, 0] = planes[1, 0][:, t, :]
+        grouped_d1 = area_d[:, W // 2 :]
         load_s(5, follows="s_win0")
         gather_both(5, follows="grouped_w1")
-        parts[5, 0] = held([P, HALF], F32, "part50")
+        parts[5, 0] = area_d[:, W : 3 * W // 2].bitcast(F32)
         for u in (4, 5):
             make_d(u, 0)
         grouped_wg = held([P, 2 * W], BF16, "grouped_wg", follows="grouped_w")
         raw = load_weight("raw_wg0", wg[:PASS, :], follows=None)
         group(grouped_wg[:, :W], raw[:])
-        early_slope(5, 1, follows="part50", rest_follows="raw_wg0")
+        early_slope(5, 1, rest_follows="raw_wg0", dst=parts[5, 0])
         load_s(6, follows="raw_w1_00")
         gather_s(6, 0)
         gather_s(6, 1)
@@ -299,64 +305,72 @@ def tile_list_botnet_gated_gradients_kernel(
 
         y = {}
 
-        def products(half, k, sig_follows):
-            pair = (2 * k, 2 * k + 1)
-            sig, val = {}, {}
+        def gate_sigmoid(half, c, sig):
+            gate = bank("gate%d%d" % (half, c))
+            for b in range(PASSES):
+                words = slice(b * N + c * P, b * N + (c + 1) * P)
+                second_pass(gate, half, b, wg_codes[:, words], wg_scales[:, words])
+            nc.scalar.activation(out=sig, in_=gate[:], func=SIGMOID, scale=-1.0)
+
+        def val_pass(val, half, c, b):
+            second_pass(val, half, b, wv_w[:, b, c * P : (c + 1) * P], wv_sc[:, b * N + c * P : b * N + (c + 1) * P])
+
+        def y_on_vector(half, pair):
+            sig = held([P, 2, HALF], F32, "sig_first", follows="s0")
+            both_y = held([P, 2, HALF], F32, "y_first", follows="s1")
             for c in pair:
-                gate = bank("gate%d%d" % (half, c))
-                for b in range(PASSES):
-                    words = slice(b * N + c * P, b * N + (c + 1) * P)
-                    second_pass(gate, half, b, wg_codes[:, words], wg_scales[:, words])
-                sig[c] = held([P, HALF], F32, "sig%d%d" % (half, c), sig_follows[c % 2])
-                nc.scalar.activation(out=sig[c][:], in_=gate[:], func=SIGMOID, scale=-1.0)
-            for c in pair:
-                val[c] = bank("val%d%d" % (half, c))
+                gate_sigmoid(half, c, sig[:, c, :])
+            val = [bank("val%d%d" % (half, c)) for c in pair]
             for b in range(PASSES):
                 for c in pair:
-                    cols = slice(c * P, (c + 1) * P)
-                    second_pass(val[c], half, b, wv_w[:, b, cols], wv_sc[:, b * N + c * P : b * N + (c + 1) * P])
-            return pair, sig, val
-
-        def y_on_vector(half, k):
-            pair, sig, val = products(half, k, ("s0", "s1"))
-            both_y = held([P, 2, HALF], F32, "y%d%d" % (half, k))
+                    val_pass(val[c], half, c, b)
             for c in pair:
-                y[half, c] = both_y[:, c % 2, :]
+                y[half, c] = both_y[:, c, :]
                 nc.vector.scalar_tensor_tensor(
-                    out=y[half, c], in0=val[c][:], scalar=-1.0, in1=sig[c][:], op0=MULT, op1=MULT
+                    out=y[half, c], in0=val[c][:], scalar=-1.0, in1=sig[:, c, :], op0=MULT, op1=MULT
                 )
             for c in pair:
                 nc.vector.tensor_tensor(y[half, c], y[half, c], wgo_sb[:, half * HALF : (half + 1) * HALF], MULT)
 
-        def y_on_gpsimd(half, k, sig_follows):
-            pair, sig, val = products(half, k, sig_follows)
+        def y_on_gpsimd(half, pair, sig_follows, shared=None):
+            sig = held([P, 2 if half else 4, HALF], F32, "sig%d%d" % (half, pair[0]), sig_follows)
             for c in pair:
-                y[half, c] = ring.tile([P, HALF], F32, name="y%d%d" % (half, c), tag="y", bufs=4)[:]
-                nc.scalar.activation(out=y[half, c], in_=val[c][:], func=COPY, scale=-1.0)
-                nc.gpsimd.tensor_tensor(sig[c][:], sig[c][:], wgo_sb[:, half * HALF : (half + 1) * HALF], MULT)
-                nc.gpsimd.tensor_tensor(y[half, c], y[half, c], sig[c][:], MULT)
+                weight = sig[:, 0, :] if (half, c) == (0, 2) else shared[:]
+                raw_sig = sig[:, c % 2, :]
+                gate_sigmoid(half, c, raw_sig)
+                val = bank("val%d%d" % (half, c))
+                for b in range(PASSES):
+                    val_pass(val, half, c, b)
+                y[half, c] = ring.tile([P, HALF], F32, name="y%d%d" % (half, c), tag="y", bufs=4)[:] if half else sig[:, c, :]
+                nc.scalar.activation(out=y[half, c], in_=val[:], func=COPY, scale=-1.0)
+                nc.gpsimd.tensor_tensor(weight, raw_sig, wgo_sb[:, half * HALF : (half + 1) * HALF], MULT)
+                copied = y[half, c]
+                if (half, c) == (0, 3):
+                    y[half, c] = held([P, HALF], F32, "y03", follows="area_d")[:]
+                nc.gpsimd.tensor_tensor(y[half, c], copied, weight, MULT)
 
         def scatter(half, c):
             nc.vector.tensor_copy(page[c][:].indirect(idx2[:, half * LIST_COLS : (half + 1) * LIST_COLS]), y[half, c])
             if half == 1:
                 nc.sync.dma_start(out=out[c * P : (c + 1) * P, :], in_=page[c][:])
 
-        y_on_vector(0, 0)
-        grouped_d1 = held([P, 2 * W], BF16, "grouped_d1", follows="slope51")
-        group(grouped_d1[:, :W], planes[0, 1][:])
+        group(grouped_d1[:, : W // 2], planes[0, 1][:, :, : HALF // 2])
+        y_on_vector(0, (0, 1))
+        group(grouped_d1[:, W // 2 : W], planes[0, 1][:, :, HALF // 2 :])
         group(grouped_d1[:, W:], planes[1, 1][:])
-        y_on_gpsimd(0, 1, ("planes11", "planes01"))
         scatter(0, 0)
         scatter(0, 1)
-        d1_codes = held([P, 2 * HALF], U32, "d1_codes", follows="y00")
+        d1_codes = held([P, 2 * HALF], U32, "d1_codes", follows="y_first")
         d1_scales = held([P, 2 * HALF], U8, "d1_scales")
         for b in range(PASSES):
             d_codes[b, 1] = d1_codes[:, b * HALF : (b + 1) * HALF]
             d_scales[b, 1] = d1_scales[:, b * HALF : (b + 1) * HALF]
         quantize(d1_codes[:], d1_scales[:], grouped_d1[:])
+        shared = held([P, HALF], F32, "weight", follows="sig_first")
+        y_on_gpsimd(0, (2, 3), "planes11", shared)
         scatter(0, 2)
         scatter(0, 3)
-        for k in range(2):
-            y_on_gpsimd(1, k, ("s2", "s3") if k == 0 else ("sig00", "sig01"))
-            scatter(1, 2 * k)
-            scatter(1, 2 * k + 1)
+        for pair, sig_follows in (((0, 1), "s2"), ((2, 3), "s3")):
+            y_on_gpsimd(1, pair, sig_follows, shared)
+            for c in pair:
+                scatter(1, c)

@@ -122,8 +122,8 @@ def tile_list_botnet_gated_gradients_kernel(
 
         slope = {}
 
-        def gather_both(u, follows=None):
-            both_halves = held([P, S], F32, "s%d" % u, follows)
+        def gather_both(u, dst=None):
+            both_halves = held([P, S], F32, "s%d" % u) if dst is None else dst
             nc.vector.tensor_copy(both_halves[:], s_win[u][:].indirect(idx[:]))
             s[u, 0], s[u, 1] = both_halves[:, :HALF], both_halves[:, HALF:]
 
@@ -184,7 +184,12 @@ def tile_list_botnet_gated_gradients_kernel(
                 plane[b * PACK + t, half] = tile[:, t, :]
             return tile
 
-        planes = {(0, half): new_planes(0, half) for half in range(2)}
+        planes = {(0, 0): new_planes(0, 0)}
+        area_w = held([P, 3 * HALF + 2 * W], BF16, "area_w")
+        planes[0, 1] = area_w[:, :W].rearrange("p (i c) -> p i c", i=PACK)
+        for t in range(PACK):
+            plane[t, 1] = planes[0, 1][:, t, :]
+        grouped_w1 = area_w[:, 3 * HALF :]
 
         def w1_operand(a, b, grouped, follows):
             w1_codes[a, b] = held([P, HALF], U32, "w1_codes%d%d" % (a, b), follows)
@@ -205,18 +210,20 @@ def tile_list_botnet_gated_gradients_kernel(
                 load_scale_rows(tab_sc, tab_scales)
                 for b in range(PASSES):
                     nc.vector.tensor_copy(v_sc[b][:], tab_sc[:, b * T : (b + 1) * T].indirect(idx[:]))
-            if a == 0:
-                for half in range(2):
-                    early_slope(a, half)
-            if a == 1:
-                w1_operand(0, 0, grouped_w[:, :W], follows="s_win1")
             w1_piece(a, 0, grouped_w[:, a * W : (a + 1) * W])
+            if a == 0:
+                w1_operand(0, 0, grouped_w[:, :W], follows=None)
+                rest0 = held([P, S], F32, "rest0", follows="raw_w1_00")
+                for half in range(2):
+                    cols = slice(half * HALF, (half + 1) * HALF)
+                    early_slope(0, half, rest=rest0[:, cols], dst=grouped_w[:, :W].bitcast(F32)[:, cols])
         rest1 = held([P, S], F32, "rest1", follows="raw_w1_10")
-        for half in range(2):
-            early_slope(1, half, rest=rest1[:, half * HALF : (half + 1) * HALF])
         load_s(2)
         gather_both(2)
         w1_operand(1, 0, grouped_w[:, W:], follows="s_win2")
+        for half in range(2):
+            cols = slice(half * HALF, (half + 1) * HALF)
+            early_slope(1, half, rest=rest1[:, cols], dst=grouped_w[:, W:].bitcast(F32)[:, cols])
         load_s(3)
         gather_both(3)
         part2 = held([P, S], F32, "part2", follows="s_win3")
@@ -224,14 +231,14 @@ def tile_list_botnet_gated_gradients_kernel(
         make_d(2, 0)
         make_d(2, 1)
         make_d(3, 0)
-        make_d(3, 1)
+        make_d(3, 1, finish=False)
         for u in range(EARLY):
             make_d(u, 0)
             make_d(u, 1)
-        grouped_w1 = held([P, 2 * W], BF16, "grouped_w1")
         w1_piece(0, 1, grouped_w1[:, :W], follows="tab_w0")
         w1_piece(1, 1, grouped_w1[:, W:], follows="tab_w1")
-        grouped_d00 = held([P, W], BF16, "grouped_d00", follows="raw_w1_11")
+        area_d = held([P, 5 * W // 2], BF16, "area_d", follows="raw_w1_11")
+        grouped_d00 = area_d[:, W : 2 * W]
         group(grouped_d00[:], planes[0, 0][:])
         load_s(4)
         gather_both(4)
@@ -241,22 +248,20 @@ def tile_list_botnet_gated_gradients_kernel(
             w1_codes[a, 1] = both[:, a * HALF : (a + 1) * HALF]
             w1_scales[a, 1] = both_sc[:, a * HALF : (a + 1) * HALF]
         quantize(both[:], both_sc[:], grouped_w1[:])
-        early_slope(4, 1)
-        area_d = held([P, 5 * W // 2], BF16, "area_d", follows="raw_w1_01")
+        finish_d(3, 1)
+        early_slope(4, 1, rest_follows="planes00")
         planes[1, 0] = area_d[:, :W].rearrange("p (i c) -> p i c", i=PACK)
         for t in range(PACK):
             plane[PACK + t, 0] = planes[1, 0][:, t, :]
         grouped_d1 = area_d[:, W // 2 :]
         load_s(5, follows="s_win0")
-        gather_both(5, follows="grouped_w1")
-        parts[5, 0] = area_d[:, W : 3 * W // 2].bitcast(F32)
+        gather_both(5, dst=grouped_w1[:, W:].bitcast(F32))
         for u in (4, 5):
             make_d(u, 0)
         grouped_wg = held([P, 2 * W], BF16, "grouped_wg", follows="grouped_w")
         raw = load_weight("raw_wg0", wg[:PASS, :], follows=None)
         group(grouped_wg[:, :W], raw[:])
-        early_slope(5, 1, rest_follows="raw_wg0", dst=parts[5, 0])
-        load_s(6, follows="raw_w1_00")
+        load_s(6, follows="s_win1")
         gather_s(6, 0)
         gather_s(6, 1)
         make_d(6, 0)
@@ -283,10 +288,14 @@ def tile_list_botnet_gated_gradients_kernel(
         d_scales = {(b, 0): held([P, HALF], U8, "d_scales%d0" % b)[:] for b in range(PASSES)}
         quantize(d_codes[0, 0], d_scales[0, 0], grouped_d00[:])
         gather_s(LAST, 1, follows="grouped_wg")
-        early_slope(6, 1, follows="grouped_d00", rest=area[:, W:].bitcast(F32))
+        early_slope(6, 1, rest=area[:, W:].bitcast(F32), dst=area_d[:, 5 * W // 4 : 7 * W // 4].bitcast(F32))
         quantize(d_codes[1, 0], d_scales[1, 0], grouped_d10[:])
-        planes[1, 1] = new_planes(1, 1, follows="grouped_d10")
-        for u in (LAST, 4, 5, 6):
+        area_p = held([P, W + 2 * HALF], BF16, "planes11", follows="grouped_d10")
+        planes[1, 1] = area_p[:, :W].rearrange("p (i c) -> p i c", i=PACK)
+        for t in range(PACK):
+            plane[PACK + t, 1] = planes[1, 1][:, t, :]
+        early_slope(5, 1, rest_follows="raw_wg0", dst=area_p[:, W:].bitcast(F32))
+        for u in (LAST, 4, 6, 5):
             make_d(u, 1)
         load_scale_rows(wv_sc, wv_scales)
         wgo_sb = held([P, S], F32, "wgo_sb", follows="s_win6")
@@ -315,62 +324,54 @@ def tile_list_botnet_gated_gradients_kernel(
         def val_pass(val, half, c, b):
             second_pass(val, half, b, wv_w[:, b, c * P : (c + 1) * P], wv_sc[:, b * N + c * P : b * N + (c + 1) * P])
 
-        def y_on_vector(half, pair):
-            sig = held([P, 2, HALF], F32, "sig_first", follows="s0")
-            both_y = held([P, 2, HALF], F32, "y_first", follows="s1")
-            for c in pair:
-                gate_sigmoid(half, c, sig[:, c, :])
-            val = [bank("val%d%d" % (half, c)) for c in pair]
-            for b in range(PASSES):
-                for c in pair:
-                    val_pass(val[c], half, c, b)
-            for c in pair:
-                y[half, c] = both_y[:, c, :]
-                nc.vector.scalar_tensor_tensor(
-                    out=y[half, c], in0=val[c][:], scalar=-1.0, in1=sig[:, c, :], op0=MULT, op1=MULT
-                )
-            for c in pair:
-                nc.vector.tensor_tensor(y[half, c], y[half, c], wgo_sb[:, half * HALF : (half + 1) * HALF], MULT)
+        shared = held([P, HALF], F32, "weight")
 
-        def y_on_gpsimd(half, pair, sig_follows, shared=None):
-            sig = held([P, 2 if half else 4, HALF], F32, "sig%d%d" % (half, pair[0]), sig_follows)
-            for c in pair:
-                weight = sig[:, 0, :] if (half, c) == (0, 2) else shared[:]
-                raw_sig = sig[:, c % 2, :]
-                gate_sigmoid(half, c, raw_sig)
-                val = bank("val%d%d" % (half, c))
-                for b in range(PASSES):
-                    val_pass(val, half, c, b)
-                y[half, c] = ring.tile([P, HALF], F32, name="y%d%d" % (half, c), tag="y", bufs=4)[:] if half else sig[:, c, :]
-                nc.scalar.activation(out=y[half, c], in_=val[:], func=COPY, scale=-1.0)
-                nc.gpsimd.tensor_tensor(weight, raw_sig, wgo_sb[:, half * HALF : (half + 1) * HALF], MULT)
-                copied = y[half, c]
-                if (half, c) == (0, 3):
-                    y[half, c] = held([P, HALF], F32, "y03", follows="area_d")[:]
-                nc.gpsimd.tensor_tensor(y[half, c], copied, weight, MULT)
+        def first_y():
+            sig = area_d[:, 2 * W :].bitcast(F32)
+            gate_sigmoid(0, 0, sig[:])
+            val = bank("val00")
+            for b in range(PASSES):
+                val_pass(val, 0, 0, b)
+            nc.vector.scalar_tensor_tensor(out=shared[:], in0=val[:], scalar=-1.0, in1=sig[:], op0=MULT, op1=MULT)
+            y[0, 0] = held([P, HALF], F32, "y00", follows="s1")[:]
+            nc.vector.tensor_tensor(y[0, 0], shared[:], wgo_sb[:, :HALF], MULT)
+
+        def y_on_gpsimd(half, c, sig, copied, weight):
+            gate_sigmoid(half, c, sig)
+            val = bank("val%d%d" % (half, c))
+            for b in range(PASSES):
+                val_pass(val, half, c, b)
+            nc.scalar.activation(out=copied, in_=val[:], func=COPY, scale=-1.0)
+            nc.gpsimd.tensor_tensor(weight, sig, wgo_sb[:, half * HALF : (half + 1) * HALF], MULT)
+            y[half, c] = copied
+            nc.gpsimd.tensor_tensor(copied, copied, weight, MULT)
 
         def scatter(half, c):
             nc.vector.tensor_copy(page[c][:].indirect(idx2[:, half * LIST_COLS : (half + 1) * LIST_COLS]), y[half, c])
             if half == 1:
                 nc.sync.dma_start(out=out[c * P : (c + 1) * P, :], in_=page[c][:])
 
-        group(grouped_d1[:, : W // 2], planes[0, 1][:, :, : HALF // 2])
-        y_on_vector(0, (0, 1))
-        group(grouped_d1[:, W // 2 : W], planes[0, 1][:, :, HALF // 2 :])
+        group(grouped_d1[:, : 3 * W // 4], planes[0, 1][:, :, : 3 * HALF // 4])
+        first_y()
+        page1 = held([P, 2, HALF], F32, "in01", follows="s2")
+        y_on_gpsimd(0, 1, page1[:, 0, :], page1[:, 1, :], shared[:])
+        group(grouped_d1[:, 3 * W // 4 : W], planes[0, 1][:, :, 3 * HALF // 4 :])
         group(grouped_d1[:, W:], planes[1, 1][:])
         scatter(0, 0)
         scatter(0, 1)
-        d1_codes = held([P, 2 * HALF], U32, "d1_codes", follows="y_first")
+        d1_codes = held([P, 2 * HALF], U32, "d1_codes", follows="in01")
         d1_scales = held([P, 2 * HALF], U8, "d1_scales")
         for b in range(PASSES):
             d_codes[b, 1] = d1_codes[:, b * HALF : (b + 1) * HALF]
             d_scales[b, 1] = d1_scales[:, b * HALF : (b + 1) * HALF]
         quantize(d1_codes[:], d1_scales[:], grouped_d1[:])
-        shared = held([P, HALF], F32, "weight", follows="sig_first")
-        y_on_gpsimd(0, (2, 3), "planes11", shared)
+        pages23 = held([P, 4, HALF], F32, "in02", follows="planes11")
+        y_on_gpsimd(0, 2, pages23[:, 0, :], pages23[:, 1, :], shared[:])
+        late_weight = held([P, HALF], F32, "late_weight", follows="area_d")
+        y_on_gpsimd(0, 3, pages23[:, 2, :], pages23[:, 3, :], late_weight[:])
         scatter(0, 2)
         scatter(0, 3)
-        for pair, sig_follows in (((0, 1), "s2"), ((2, 3), "s3")):
-            y_on_gpsimd(1, pair, sig_follows, shared)
-            for c in pair:
-                scatter(1, c)
+        for c in range(PAGES):
+            both_in = ring.tile([P, 2, HALF], F32, name="in1%d" % c, tag="in1", bufs=3)
+            y_on_gpsimd(1, c, both_in[:, 0, :], both_in[:, 1, :], late_weight[:])
+            scatter(1, c)

@@ -29,7 +29,6 @@ LAST = ROW_TILES - 1
 PAGES = N // P
 RUN = 4
 BANKS = 8
-EARLY = 2
 
 
 def tile_list_botnet_gated_gradients_kernel(
@@ -105,7 +104,10 @@ def tile_list_botnet_gated_gradients_kernel(
             )
 
         s_rows = sT.rearrange("(b p t) c -> b t p c", p=P, t=PACK)
-        s_win, s = {}, {}
+        s_win, s, slope, part, plane = {}, {}, {}, {}, {}
+
+        def halves(ap):
+            return ap[:, :HALF], ap[:, HALF:]
 
         def load_s(u, follows=None):
             s_win[u] = held([P, T], F32, "s_win%d" % u, follows)
@@ -114,42 +116,29 @@ def tile_list_botnet_gated_gradients_kernel(
             else:
                 nc.sync.dma_start(out=s_win[u][:], in_=s_rows[u // PACK, u % PACK])
 
-        def gather_s(u, half, follows=None):
-            s[u, half] = held([P, HALF], F32, "s%d%d" % (u, half), follows)
-            nc.vector.tensor_copy(
-                s[u, half][:], s_win[u][:].indirect(idx[:, half * LIST_COLS : (half + 1) * LIST_COLS])
-            )
+        def gather_s(u, dst):
+            nc.vector.tensor_copy(dst, s_win[u][:].indirect(idx[:]))
+            s[u, 0], s[u, 1] = halves(dst)
 
-        slope = {}
+        def gather_s_half(u, half, dst):
+            nc.vector.tensor_copy(dst, s_win[u][:].indirect(idx[:, half * LIST_COLS : (half + 1) * LIST_COLS]))
+            s[u, half] = dst
 
-        def gather_both(u, dst=None):
-            both_halves = held([P, S], F32, "s%d" % u) if dst is None else dst
-            nc.vector.tensor_copy(both_halves[:], s_win[u][:].indirect(idx[:]))
-            s[u, 0], s[u, 1] = both_halves[:, :HALF], both_halves[:, HALF:]
+        def make_slope(u, half, rest, dst):
+            nc.scalar.activation(out=rest, in_=s[u, half], func=COPY, scale=1.0, bias=-1.0)
+            nc.gpsimd.tensor_tensor(dst, s[u, half], rest, MULT)
+            slope[u, half] = dst
 
-        def early_slope(u, half, follows=None, rest_follows=None, rest=None, dst=None):
-            if rest is not None:
-                pass
-            elif rest_follows:
-                rest = held([P, HALF], F32, "rest%d%d" % (u, half), rest_follows)
-            else:
-                rest = ring.tile([P, HALF], F32, name="rest%d%d" % (u, half), tag="t", bufs=6)
-            nc.scalar.activation(out=rest[:], in_=s[u, half][:], func=COPY, scale=1.0, bias=-1.0)
-            slope[u, half] = held([P, HALF], F32, "slope%d%d" % (u, half), follows) if follows else s[u, half]
-            if dst is not None:
-                slope[u, half] = dst
-            nc.gpsimd.tensor_tensor(slope[u, half][:], s[u, half][:], rest[:], MULT)
+        w1_codes, w1_scales = {}, {}
 
-        w1_codes, w1_scales, plane, parts = {}, {}, {}, {}
-
-        def make_d(u, half, follows=None, finish=True):
+        def h_bank(u, half):
             b, t = divmod(u, PACK)
-            h_bank = bank("h%d%d" % (u, half))
+            acc = bank("h%d%d" % (u, half))
             entries = slice(half * HALF, (half + 1) * HALF)
             words = slice(t * P, (t + 1) * P)
             for a in range(PASSES):
                 nc.tensor.matmul_mx(
-                    out=h_bank[:],
+                    out=acc[:],
                     lhsT=w1_codes[a, b][:, words].bitcast(E4M3),
                     lhsT_scale=w1_scales[a, b][:, words],
                     rhs=v_w[a][:, entries].bitcast(E5M2),
@@ -157,44 +146,53 @@ def tile_list_botnet_gated_gradients_kernel(
                     start=(a == 0),
                     stop=(a == PASSES - 1),
                 )
-            if (u, half) in slope:
-                nc.vector.tensor_tensor(plane[u, half], h_bank[:], slope[u, half][:], MULT)
-                return
-            if (u, half) in parts:
-                part = parts[u, half]
-            elif follows:
-                part = held([P, HALF], F32, "part%d%d" % (u, half), follows)
-            else:
-                part = ring.tile([P, HALF], F32, name="part%d%d" % (u, half), tag="t", bufs=6)
-            nc.vector.scalar_tensor_tensor(
-                out=part[:], in0=s[u, half][:], scalar=-1.0, in1=h_bank[:], op0=ADD, op1=MULT
-            )
-            parts[u, half] = part
-            if finish:
-                finish_d(u, half)
+            return acc
 
-        def finish_d(u, half):
-            nc.gpsimd.tensor_tensor(plane[u, half], parts[u, half][:], s[u, half][:], MULT)
+        def d_from_slope(u, half):
+            nc.vector.tensor_tensor(plane[u, half], h_bank(u, half)[:], slope[u, half], MULT)
+
+        def make_part(u, half, dst=None):
+            if dst is None:
+                dst = ring.tile([P, HALF], F32, name="part%d%d" % (u, half), tag="part", bufs=4)[:]
+            part[u, half] = dst
+            nc.vector.scalar_tensor_tensor(
+                out=dst, in0=s[u, half], scalar=-1.0, in1=h_bank(u, half)[:], op0=ADD, op1=MULT
+            )
+
+        def d_from_part(u, half, engine):
+            engine.tensor_tensor(plane[u, half], part[u, half], s[u, half], MULT)
 
         W = PACK * HALF
+        planes = {}
 
-        def new_planes(b, half, follows=None):
-            tile = held([P, PACK, HALF], BF16, "planes%d%d" % (b, half), follows)
+        def set_planes(b, half, flat):
+            planes[b, half] = flat.rearrange("p (i c) -> p i c", i=PACK)
             for t in range(PACK):
-                plane[b * PACK + t, half] = tile[:, t, :]
-            return tile
+                plane[b * PACK + t, half] = planes[b, half][:, t, :]
 
-        planes = {(0, 0): new_planes(0, 0)}
-        area_w = held([P, 3 * HALF + 2 * W], BF16, "area_w")
-        planes[0, 1] = area_w[:, :W].rearrange("p (i c) -> p i c", i=PACK)
-        for t in range(PACK):
-            plane[t, 1] = planes[0, 1][:, t, :]
-        grouped_w1 = area_w[:, 3 * HALF :]
+        def w1_operand(a, grouped, follows):
+            w1_codes[a, 0] = held([P, HALF], U32, "w1_codes%d0" % a, follows)
+            w1_scales[a, 0] = held([P, HALF], U8, "w1_scales%d0" % a)
+            quantize(w1_codes[a, 0][:], w1_scales[a, 0][:], grouped)
 
-        def w1_operand(a, b, grouped, follows):
-            w1_codes[a, b] = held([P, HALF], U32, "w1_codes%d%d" % (a, b), follows)
-            w1_scales[a, b] = held([P, HALF], U8, "w1_scales%d%d" % (a, b))
-            quantize(w1_codes[a, b][:], w1_scales[a, b][:], grouped)
+        NH = N // 2
+
+        def wg_columns(k, follows, dst):
+            raw = held([P, PASSES, PACK, NH], F32, "raw_wg%d" % k, follows)
+            for b in range(PASSES):
+                rows = wg[b * PASS : (b + 1) * PASS, k * NH : (k + 1) * NH]
+                nc.sync.dma_start(out=raw[:, b], in_=rows.rearrange("(p i) c -> p i c", i=PACK))
+                group(dst[:, b * W // 2 : (b + 1) * W // 2], raw[:, b])
+
+        area = held([P, 3 * HALF + 2 * W], BF16, "area")
+        set_planes(0, 0, held([P, W], BF16, "planes00")[:])
+        set_planes(0, 1, area[:, :W])
+        grouped_w1 = area[:, 3 * HALF :]
+        rest61 = area[:, : 2 * HALF].bitcast(F32)
+        grouped_d10 = area[:, 2 * HALF : 2 * HALF + W]
+        EDGE = 32
+        slope51 = area[:, EDGE : EDGE + 2 * HALF].bitcast(F32)
+        planes11_at = 2 * HALF + EDGE
 
         nc.sync.dma_start(idx[:], offs)
         nc.sync.dma_start(idx2[:], offs2)
@@ -202,176 +200,168 @@ def tile_list_botnet_gated_gradients_kernel(
             nc.gpsimd.memset(page[c][:], 0.0)
         table_pass(0)
         table_pass(1)
-        grouped_w = held([P, 2 * W], BF16, "grouped_w")
+        grouped_w0 = held([P, 2 * W], BF16, "grouped_w0")
+        load_s(0)
+        gather_s(0, held([P, S], F32, "s0")[:])
+        load_scale_rows(tab_sc, tab_scales)
         for a in range(PASSES):
-            load_s(a)
-            gather_both(a)
-            if a == 0:
-                load_scale_rows(tab_sc, tab_scales)
-                for b in range(PASSES):
-                    nc.vector.tensor_copy(v_sc[b][:], tab_sc[:, b * T : (b + 1) * T].indirect(idx[:]))
-            w1_piece(a, 0, grouped_w[:, a * W : (a + 1) * W])
-            if a == 0:
-                w1_operand(0, 0, grouped_w[:, :W], follows=None)
-                rest0 = held([P, S], F32, "rest0", follows="raw_w1_00")
-                for half in range(2):
-                    cols = slice(half * HALF, (half + 1) * HALF)
-                    early_slope(0, half, rest=rest0[:, cols], dst=grouped_w[:, :W].bitcast(F32)[:, cols])
-        rest1 = held([P, S], F32, "rest1", follows="raw_w1_10")
-        load_s(2)
-        gather_both(2)
-        w1_operand(1, 0, grouped_w[:, W:], follows="s_win2")
+            nc.vector.tensor_copy(v_sc[a][:], tab_sc[:, a * T : (a + 1) * T].indirect(idx[:]))
+        w1_piece(0, 0, grouped_w0[:, :W])
+        w1_operand(0, grouped_w0[:, :W], follows=None)
+        rest = held([P, S], F32, "rest0", follows="raw_w1_00")
         for half in range(2):
-            cols = slice(half * HALF, (half + 1) * HALF)
-            early_slope(1, half, rest=rest1[:, cols], dst=grouped_w[:, W:].bitcast(F32)[:, cols])
+            make_slope(0, half, halves(rest)[half], halves(grouped_w0[:, :W].bitcast(F32))[half])
+        load_s(1)
+        gather_s(1, held([P, S], F32, "s1")[:])
+        w1_piece(1, 0, grouped_w0[:, W:])
+        load_s(2)
+        gather_s(2, held([P, S], F32, "s2")[:])
+        w1_operand(1, grouped_w0[:, W:], follows="s_win2")
+        rest = held([P, S], F32, "rest1", follows="raw_w1_10")
+        for half in range(2):
+            make_slope(1, half, halves(rest)[half], halves(grouped_w0[:, W:].bitcast(F32))[half])
         load_s(3)
-        gather_both(3)
+        gather_s(3, held([P, S], F32, "s3")[:])
         part2 = held([P, S], F32, "part2", follows="s_win3")
-        parts[2, 0], parts[2, 1] = part2[:, :HALF], part2[:, HALF:]
-        make_d(2, 0)
-        make_d(2, 1)
-        make_d(3, 0)
-        make_d(3, 1, finish=False)
-        for u in range(EARLY):
-            make_d(u, 0)
-            make_d(u, 1)
+        for half in range(2):
+            make_part(2, half, halves(part2)[half])
+            d_from_part(2, half, nc.gpsimd)
+        make_part(3, 0)
+        d_from_part(3, 0, nc.gpsimd)
+        make_part(3, 1)
+        for u in range(2):
+            for half in range(2):
+                d_from_slope(u, half)
         w1_piece(0, 1, grouped_w1[:, :W], follows="tab_w0")
         w1_piece(1, 1, grouped_w1[:, W:], follows="tab_w1")
-        area_d = held([P, 5 * W // 2], BF16, "area_d", follows="raw_w1_11")
-        grouped_d00 = area_d[:, W : 2 * W]
-        group(grouped_d00[:], planes[0, 0][:])
+        grouped_first = held([P, 2 * W], BF16, "grouped_first", follows="raw_w1_11")
+        group(grouped_first[:, W:], planes[0, 0])
         load_s(4)
-        gather_both(4)
-        both = held([P, 2 * HALF], U32, "w1_codes_1", follows="s_win4")
-        both_sc = held([P, 2 * HALF], U8, "w1_scales_1")
+        gather_s(4, held([P, S], F32, "s4")[:])
+        codes = held([P, 2 * HALF], U32, "w1_codes1", follows="s_win4")
+        scales = held([P, 2 * HALF], U8, "w1_scales1")
         for a in range(PASSES):
-            w1_codes[a, 1] = both[:, a * HALF : (a + 1) * HALF]
-            w1_scales[a, 1] = both_sc[:, a * HALF : (a + 1) * HALF]
-        quantize(both[:], both_sc[:], grouped_w1[:])
-        finish_d(3, 1)
-        early_slope(4, 1, rest_follows="planes00")
-        planes[1, 0] = area_d[:, :W].rearrange("p (i c) -> p i c", i=PACK)
-        for t in range(PACK):
-            plane[PACK + t, 0] = planes[1, 0][:, t, :]
-        grouped_d1 = area_d[:, W // 2 :]
+            w1_codes[a, 1], w1_scales[a, 1] = halves(codes)[a], halves(scales)[a]
+        quantize(codes[:], scales[:], grouped_w1)
+        d_from_part(3, 1, nc.gpsimd)
+        make_slope(4, 1, held([P, HALF], F32, "rest41", follows="planes00")[:], s[4, 1])
+        set_planes(1, 0, held([P, W], BF16, "planes10", follows="raw_w1_01")[:])
         load_s(5, follows="s_win0")
-        gather_both(5, dst=grouped_w1[:, W:].bitcast(F32))
+        gather_s(5, grouped_w1[:, W:].bitcast(F32))
         for u in (4, 5):
-            make_d(u, 0)
-        grouped_wg = held([P, 2 * W], BF16, "grouped_wg", follows="grouped_w")
-        raw = load_weight("raw_wg0", wg[:PASS, :], follows=None)
-        group(grouped_wg[:, :W], raw[:])
+            make_part(u, 0)
+            d_from_part(u, 0, nc.gpsimd)
+        wg_columns(0, None, grouped_first[:, :W])
+        second = held([P, 2 * W + 2 * HALF], BF16, "grouped_d1", follows="raw_wg0")
+        grouped_d1 = second[:, : 2 * W]
+        rest51 = second[:, 2 * W :].bitcast(F32)
+        nc.scalar.activation(out=rest51, in_=s[5, 1], func=COPY, scale=1.0, bias=-1.0)
+        group(grouped_d1[:, :W], planes[0, 1])
         load_s(6, follows="s_win1")
-        gather_s(6, 0)
-        gather_s(6, 1)
-        make_d(6, 0)
-
-        raw = load_weight("raw_wg1", wg[PASS:, :], follows=None)
-        group(grouped_wg[:, W:], raw[:])
-        area = held([P, W + 2 * HALF], BF16, "grouped_d10", follows="raw_wg1")
-        grouped_d10 = area[:, :W]
-        group(grouped_d10[:], planes[1, 0][:, :2], 0)
-        load_s(LAST, follows="rest1")
-        wv_w = held([P, PASSES, N], U32, "wv_w", follows="s_win5")
+        for half in range(2):
+            gather_s_half(6, half, held([P, HALF], F32, "s6%d" % half)[:])
+        make_part(6, 0)
+        d_from_part(6, 0, nc.gpsimd)
+        nc.scalar.activation(out=rest61, in_=s[6, 1], func=COPY, scale=1.0, bias=-1.0)
+        group(grouped_d10, planes[1, 0][:, :2], 0)
+        load_s(LAST)
+        load_scale_rows(wv_sc, wv_scales)
+        wv_w = held([P, PASSES, N], U32, "wv_w", follows="rest1")
         nc.sync.dma_start(out=wv_w[:].bitcast(I32), in_=wv_words.rearrange("b p c i -> p b (c i)").bitcast(I32))
 
-        gather_s(LAST, 0)
-        parts[LAST, 0] = held([P, HALF], F32, "part%d0" % LAST)
-        make_d(LAST, 0, finish=False)
-        nc.vector.tensor_tensor(plane[LAST, 0], parts[LAST, 0][:], s[LAST, 0][:], MULT)
-        group(grouped_d10[:], planes[1, 0][:, 2:], 2)
-        wg_codes = held([P, PASSES * N], U32, "wg_codes", follows="part%d0" % LAST)
-        wg_scales = held([P, PASSES * N], U8, "wg_scales")
-        quantize(wg_codes[:], wg_scales[:], grouped_wg[:])
-        d_codes = {(0, 0): held([P, HALF], U32, "d_codes00", follows="s%d0" % LAST)[:]}
-        d_codes[1, 0] = held([P, HALF], U32, "d_codes10")[:]
-        d_scales = {(b, 0): held([P, HALF], U8, "d_scales%d0" % b)[:] for b in range(PASSES)}
-        quantize(d_codes[0, 0], d_scales[0, 0], grouped_d00[:])
-        gather_s(LAST, 1, follows="grouped_wg")
-        early_slope(6, 1, rest=area[:, W:].bitcast(F32), dst=area_d[:, 5 * W // 4 : 7 * W // 4].bitcast(F32))
-        quantize(d_codes[1, 0], d_scales[1, 0], grouped_d10[:])
-        area_p = held([P, W + 2 * HALF], BF16, "planes11", follows="grouped_d10")
-        planes[1, 1] = area_p[:, :W].rearrange("p (i c) -> p i c", i=PACK)
-        for t in range(PACK):
-            plane[PACK + t, 1] = planes[1, 1][:, t, :]
-        early_slope(5, 1, rest_follows="raw_wg0", dst=area_p[:, W:].bitcast(F32))
-        for u in (LAST, 4, 6, 5):
-            make_d(u, 1)
-        load_scale_rows(wv_sc, wv_scales)
+        gather_s_half(LAST, 0, held([P, HALF], F32, "s70")[:])
+        make_part(LAST, 0, held([P, HALF], F32, "part70")[:])
+        d_from_part(LAST, 0, nc.vector)
+        group(grouped_d10, planes[1, 0][:, 2:], 2)
+        slope[6, 1] = held([P, HALF], F32, "slope61", follows="part70")[:]
+        nc.gpsimd.tensor_tensor(slope[6, 1], s[6, 1], rest61, MULT)
+        gather_s_half(LAST, 1, held([P, HALF], F32, "s71", follows="s70")[:])
+        codes = held([P, 2 * HALF], U32, "first_codes", follows="s_win7")
+        scales = held([P, 2 * HALF], U8, "first_scales")
+        quantize(codes[:], scales[:], grouped_first[:])
+        wg_codes, wg_scales = {0: codes[:, :HALF]}, {0: scales[:, :HALF]}
+        d_codes = {(0, 0): codes[:, HALF:], (1, 0): held([P, HALF], U32, "d_codes10")[:]}
+        d_scales = {(0, 0): scales[:, HALF:], (1, 0): held([P, HALF], U8, "d_scales10")[:]}
+        quantize(d_codes[1, 0], d_scales[1, 0], grouped_d10)
+        grouped_wg1 = held([P, W], BF16, "grouped_wg1", follows="planes10")
+        wg_columns(1, "s_win5", grouped_wg1[:])
         wgo_sb = held([P, S], F32, "wgo_sb", follows="s_win6")
         nc.sync.dma_start(out=wgo_sb[:], in_=wgo)
+        set_planes(1, 1, area[:, planes11_at : planes11_at + W])
+        nc.gpsimd.tensor_tensor(slope51, s[5, 1], rest51, MULT)
+        slope[5, 1] = slope51
+        make_part(LAST, 1)
+        d_from_part(LAST, 1, nc.gpsimd)
+        for u in (4, 6, 5):
+            d_from_slope(u, 1)
 
-        def second_pass(acc, half, b, lhsT, lhsT_scale):
-            nc.tensor.matmul_mx(
-                out=acc[:],
-                lhsT=lhsT.bitcast(E4M3),
-                lhsT_scale=lhsT_scale,
-                rhs=d_codes[b, half].bitcast(E4M3),
-                rhs_scale=d_scales[b, half],
-                start=(b == 0),
-                stop=(b == PASSES - 1),
-            )
+        def product(name, half, lhsT, lhsT_scale):
+            acc = bank(name)
+            for b in range(PASSES):
+                nc.tensor.matmul_mx(
+                    out=acc[:],
+                    lhsT=lhsT[b].bitcast(E4M3),
+                    lhsT_scale=lhsT_scale[b],
+                    rhs=d_codes[b, half].bitcast(E4M3),
+                    rhs_scale=d_scales[b, half],
+                    start=(b == 0),
+                    stop=(b == PASSES - 1),
+                )
+            return acc
+
+        def sigmoid_of_gate(half, c, sig):
+            k, first = divmod(c * P, NH)
+            words = [slice(b * NH + first, b * NH + first + P) for b in range(PASSES)]
+            gate = product("gate%d%d" % (half, c), half, [wg_codes[k][:, w] for w in words], [wg_scales[k][:, w] for w in words])
+            nc.scalar.activation(out=sig, in_=gate[:], func=SIGMOID, scale=-1.0)
+
+        def val_bank(half, c):
+            words = [wv_w[:, b, c * P : (c + 1) * P] for b in range(PASSES)]
+            return product("val%d%d" % (half, c), half, words, [wv_sc[:, b * N + c * P : b * N + (c + 1) * P] for b in range(PASSES)])
 
         y = {}
 
-        def gate_sigmoid(half, c, sig):
-            gate = bank("gate%d%d" % (half, c))
-            for b in range(PASSES):
-                words = slice(b * N + c * P, b * N + (c + 1) * P)
-                second_pass(gate, half, b, wg_codes[:, words], wg_scales[:, words])
-            nc.scalar.activation(out=sig, in_=gate[:], func=SIGMOID, scale=-1.0)
-
-        def val_pass(val, half, c, b):
-            second_pass(val, half, b, wv_w[:, b, c * P : (c + 1) * P], wv_sc[:, b * N + c * P : b * N + (c + 1) * P])
-
-        shared = held([P, HALF], F32, "weight")
-
-        def first_y():
-            sig = area_d[:, 2 * W :].bitcast(F32)
-            gate_sigmoid(0, 0, sig[:])
-            val = bank("val00")
-            for b in range(PASSES):
-                val_pass(val, 0, 0, b)
-            nc.vector.scalar_tensor_tensor(out=shared[:], in0=val[:], scalar=-1.0, in1=sig[:], op0=MULT, op1=MULT)
-            y[0, 0] = held([P, HALF], F32, "y00", follows="s1")[:]
-            nc.vector.tensor_tensor(y[0, 0], shared[:], wgo_sb[:, :HALF], MULT)
-
-        def y_on_gpsimd(half, c, sig, copied, weight):
-            gate_sigmoid(half, c, sig)
-            val = bank("val%d%d" % (half, c))
-            for b in range(PASSES):
-                val_pass(val, half, c, b)
-            nc.scalar.activation(out=copied, in_=val[:], func=COPY, scale=-1.0)
-            nc.gpsimd.tensor_tensor(weight, sig, wgo_sb[:, half * HALF : (half + 1) * HALF], MULT)
-            y[half, c] = copied
-            nc.gpsimd.tensor_tensor(copied, copied, weight, MULT)
+        def y_on_gpsimd(half, c, sig, dst, weight):
+            sigmoid_of_gate(half, c, sig)
+            nc.scalar.activation(out=dst, in_=val_bank(half, c)[:], func=COPY, scale=-1.0)
+            nc.gpsimd.tensor_tensor(weight, sig, halves(wgo_sb)[half], MULT)
+            nc.gpsimd.tensor_tensor(dst, dst, weight, MULT)
+            y[half, c] = dst
 
         def scatter(half, c):
             nc.vector.tensor_copy(page[c][:].indirect(idx2[:, half * LIST_COLS : (half + 1) * LIST_COLS]), y[half, c])
             if half == 1:
                 nc.sync.dma_start(out=out[c * P : (c + 1) * P, :], in_=page[c][:])
 
-        group(grouped_d1[:, : 3 * W // 4], planes[0, 1][:, :, : 3 * HALF // 4])
-        first_y()
-        page1 = held([P, 2, HALF], F32, "in01", follows="s2")
-        y_on_gpsimd(0, 1, page1[:, 0, :], page1[:, 1, :], shared[:])
-        group(grouped_d1[:, 3 * W // 4 : W], planes[0, 1][:, :, 3 * HALF // 4 :])
-        group(grouped_d1[:, W:], planes[1, 1][:])
+        first_sig = grouped_d1[:, 3 * W // 2 :].bitcast(F32)
+        sigmoid_of_gate(0, 0, first_sig)
+        raw_y = held([P, HALF], F32, "raw_y", follows="s0")
+        nc.vector.scalar_tensor_tensor(out=raw_y[:], in0=val_bank(0, 0)[:], scalar=-1.0, in1=first_sig, op0=MULT, op1=MULT)
+        y[0, 0] = held([P, HALF], F32, "y00", follows="s1")[:]
+        nc.vector.tensor_tensor(y[0, 0], raw_y[:], halves(wgo_sb)[0], MULT)
+        wg_codes[1] = held([P, HALF], U32, "wg_codes1", follows="raw_y")[:]
+        wg_scales[1] = held([P, HALF], U8, "wg_scales1")[:]
+        quantize(wg_codes[1], wg_scales[1], grouped_wg1[:])
+        sig01 = held([P, HALF], F32, "sig01", follows="s2")[:]
+        y01 = held([P, HALF], F32, "y01", follows="s3")[:]
+        y_on_gpsimd(0, 1, sig01, y01, held([P, HALF], F32, "weight01", follows="grouped_wg1")[:])
+        group(grouped_d1[:, W:], planes[1, 1])
         scatter(0, 0)
         scatter(0, 1)
-        d1_codes = held([P, 2 * HALF], U32, "d1_codes", follows="in01")
-        d1_scales = held([P, 2 * HALF], U8, "d1_scales")
+        codes = held([P, 2 * HALF], U32, "d1_codes", follows="y01")
+        scales = held([P, 2 * HALF], U8, "d1_scales")
         for b in range(PASSES):
-            d_codes[b, 1] = d1_codes[:, b * HALF : (b + 1) * HALF]
-            d_scales[b, 1] = d1_scales[:, b * HALF : (b + 1) * HALF]
-        quantize(d1_codes[:], d1_scales[:], grouped_d1[:])
-        pages23 = held([P, 4, HALF], F32, "in02", follows="planes11")
-        y_on_gpsimd(0, 2, pages23[:, 0, :], pages23[:, 1, :], shared[:])
-        late_weight = held([P, HALF], F32, "late_weight", follows="area_d")
-        y_on_gpsimd(0, 3, pages23[:, 2, :], pages23[:, 3, :], late_weight[:])
+            d_codes[b, 1], d_scales[b, 1] = halves(codes)[b], halves(scales)[b]
+        quantize(codes[:], scales[:], grouped_d1)
+        sig02, y02, sig03 = [area[:, 2 * EDGE + 2 * HALF * i : 2 * EDGE + 2 * HALF * (i + 1)].bitcast(F32) for i in range(3)]
+        y_on_gpsimd(0, 2, sig02, y02, sig01)
+        y_on_gpsimd(0, 3, sig03, sig02, held([P, HALF], F32, "weight03", follows="grouped_d1")[:])
         scatter(0, 2)
         scatter(0, 3)
+        weight = sig03
         for c in range(PAGES):
-            both_in = ring.tile([P, 2, HALF], F32, name="in1%d" % c, tag="in1", bufs=3)
-            y_on_gpsimd(1, c, both_in[:, 0, :], both_in[:, 1, :], late_weight[:])
+            sig = ring.tile([P, HALF], F32, name="sig1%d" % c, tag="sig", bufs=3)[:]
+            dst = ring.tile([P, HALF], F32, name="y1%d" % c, tag="y", bufs=3)[:]
+            y_on_gpsimd(1, c, sig, dst, weight)
+            weight = sig
             scatter(1, c)

@@ -177,22 +177,22 @@ def tile_list_botnet_gated_gradients_kernel(
 
         NH = N // 2
 
-        def wg_columns(k, follows, dst):
+        def wg_columns(k, follows, dsts):
             raw = held([P, PASSES, PACK, NH], F32, "raw_wg%d" % k, follows)
             for b in range(PASSES):
                 rows = wg[b * PASS : (b + 1) * PASS, k * NH : (k + 1) * NH]
                 nc.sync.dma_start(out=raw[:, b], in_=rows.rearrange("(p i) c -> p i c", i=PACK))
-                group(dst[:, b * W // 2 : (b + 1) * W // 2], raw[:, b])
+                group(dsts[b], raw[:, b])
 
         area = held([P, 3 * HALF + 2 * W], BF16, "area")
         set_planes(0, 0, held([P, W], BF16, "planes00")[:])
         set_planes(0, 1, area[:, :W])
         grouped_w1 = area[:, 3 * HALF :]
         rest61 = area[:, : 2 * HALF].bitcast(F32)
-        grouped_d10 = area[:, 2 * HALF : 2 * HALF + W]
         EDGE = 32
-        slope51 = area[:, EDGE : EDGE + 2 * HALF].bitcast(F32)
         planes11_at = 2 * HALF + EDGE
+        grouped_d10 = area[:, planes11_at + EDGE : planes11_at + EDGE + W]
+        slope61_late = area[:, planes11_at + W : planes11_at + W + HALF].bitcast(F32)
 
         nc.sync.dma_start(idx[:], offs)
         nc.sync.dma_start(idx2[:], offs2)
@@ -234,8 +234,8 @@ def tile_list_botnet_gated_gradients_kernel(
                 d_from_slope(u, half)
         w1_piece(0, 1, grouped_w1[:, :W], follows="tab_w0")
         w1_piece(1, 1, grouped_w1[:, W:], follows="tab_w1")
-        grouped_first = held([P, 2 * W], BF16, "grouped_first", follows="raw_w1_11")
-        group(grouped_first[:, W:], planes[0, 0])
+        grouped_d00 = held([P, W], BF16, "grouped_d00", follows="raw_w1_11")
+        group(grouped_d00[:], planes[0, 0])
         load_s(4)
         gather_s(4, held([P, S], F32, "s4")[:])
         codes = held([P, 2 * HALF], U32, "w1_codes1", follows="s_win4")
@@ -245,17 +245,17 @@ def tile_list_botnet_gated_gradients_kernel(
         quantize(codes[:], scales[:], grouped_w1)
         d_from_part(3, 1, nc.gpsimd)
         make_slope(4, 1, held([P, HALF], F32, "rest41", follows="planes00")[:], s[4, 1])
-        set_planes(1, 0, held([P, W], BF16, "planes10", follows="raw_w1_01")[:])
         load_s(5, follows="s_win0")
         gather_s(5, grouped_w1[:, W:].bitcast(F32))
+        grouped_wg0 = held([P, W], BF16, "grouped_wg0", follows="raw_w1_01")
+        wg_columns(0, None, [grouped_wg0[:, : W // 2], grouped_wg0[:, W // 2 :]])
+        second = held([P, 5 * W // 2], BF16, "grouped_d1", follows="raw_wg0")
+        set_planes(1, 0, second[:, 3 * W // 2 :])
+        grouped_d1 = second[:, : 2 * W]
         for u in (4, 5):
             make_part(u, 0)
             d_from_part(u, 0, nc.gpsimd)
-        wg_columns(0, None, grouped_first[:, :W])
-        second = held([P, 2 * W + 2 * HALF], BF16, "grouped_d1", follows="raw_wg0")
-        grouped_d1 = second[:, : 2 * W]
-        rest51 = second[:, 2 * W :].bitcast(F32)
-        nc.scalar.activation(out=rest51, in_=s[5, 1], func=COPY, scale=1.0, bias=-1.0)
+        make_slope(5, 1, second[:, 2 * W :].bitcast(F32), s[5, 1])
         group(grouped_d1[:, :W], planes[0, 1])
         load_s(6, follows="s_win1")
         for half in range(2):
@@ -273,27 +273,31 @@ def tile_list_botnet_gated_gradients_kernel(
         make_part(LAST, 0, held([P, HALF], F32, "part70")[:])
         d_from_part(LAST, 0, nc.vector)
         group(grouped_d10, planes[1, 0][:, 2:], 2)
-        slope[6, 1] = held([P, HALF], F32, "slope61", follows="part70")[:]
-        nc.gpsimd.tensor_tensor(slope[6, 1], s[6, 1], rest61, MULT)
-        gather_s_half(LAST, 1, held([P, HALF], F32, "s71", follows="s70")[:])
-        codes = held([P, 2 * HALF], U32, "first_codes", follows="s_win7")
-        scales = held([P, 2 * HALF], U8, "first_scales")
-        quantize(codes[:], scales[:], grouped_first[:])
-        wg_codes, wg_scales = {0: codes[:, :HALF]}, {0: scales[:, :HALF]}
-        d_codes = {(0, 0): codes[:, HALF:], (1, 0): held([P, HALF], U32, "d_codes10")[:]}
-        d_scales = {(0, 0): scales[:, HALF:], (1, 0): held([P, HALF], U8, "d_scales10")[:]}
+        wg_codes = {0: held([P, HALF], U32, "wg_codes0", follows="part70")[:]}
+        wg_scales = {0: held([P, HALF], U8, "wg_scales0")[:]}
+        quantize(wg_codes[0], wg_scales[0], grouped_wg0[:])
+        d_codes = {(0, 0): held([P, HALF], U32, "d_codes00", follows="s70")[:]}
+        d_codes[1, 0] = held([P, HALF], U32, "d_codes10")[:]
+        d_scales = {(b, 0): held([P, HALF], U8, "d_scales%d0" % b)[:] for b in range(PASSES)}
+        quantize(d_codes[0, 0], d_scales[0, 0], grouped_d00[:])
+        gather_s_half(LAST, 1, held([P, HALF], F32, "s71", follows="grouped_wg0")[:])
+        left, right = slice(0, HALF // 2), slice(HALF // 2, HALF)
+        slope61_early = held([P, HALF // 2], F32, "slope61_early", follows="grouped_d00")[:]
+        nc.gpsimd.tensor_tensor(slope61_early, s[6, 1][:, left], rest61[:, left], MULT)
         quantize(d_codes[1, 0], d_scales[1, 0], grouped_d10)
-        grouped_wg1 = held([P, W], BF16, "grouped_wg1", follows="planes10")
-        wg_columns(1, "s_win5", grouped_wg1[:])
+        grouped_wg1 = [second[:, 7 * W // 4 : 9 * W // 4], held([P, W // 2], BF16, "grouped_wg11", follows="s4")[:]]
+        wg_columns(1, "s_win5", grouped_wg1)
         wgo_sb = held([P, S], F32, "wgo_sb", follows="s_win6")
         nc.sync.dma_start(out=wgo_sb[:], in_=wgo)
         set_planes(1, 1, area[:, planes11_at : planes11_at + W])
-        nc.gpsimd.tensor_tensor(slope51, s[5, 1], rest51, MULT)
-        slope[5, 1] = slope51
+        nc.gpsimd.tensor_tensor(slope61_late, s[6, 1][:, right], rest61[:, right], MULT)
         make_part(LAST, 1)
         d_from_part(LAST, 1, nc.gpsimd)
-        for u in (4, 6, 5):
+        for u in (4, 5):
             d_from_slope(u, 1)
+        h61 = h_bank(6, 1)
+        for cols, part_slope in ((left, slope61_early), (right, slope61_late)):
+            nc.vector.tensor_tensor(plane[6, 1][:, cols], h61[:, cols], part_slope, MULT)
 
         def product(name, half, lhsT, lhsT_scale):
             acc = bank(name)
@@ -321,10 +325,11 @@ def tile_list_botnet_gated_gradients_kernel(
 
         y = {}
 
-        def y_on_gpsimd(half, c, sig, dst, weight):
+        def y_on_gpsimd(half, c, sig, dst, weight, pieces=(slice(0, HALF),)):
             sigmoid_of_gate(half, c, sig)
             nc.scalar.activation(out=dst, in_=val_bank(half, c)[:], func=COPY, scale=-1.0)
-            nc.gpsimd.tensor_tensor(weight, sig, halves(wgo_sb)[half], MULT)
+            for cols in pieces:
+                nc.gpsimd.tensor_tensor(weight[:, cols], sig[:, cols], halves(wgo_sb)[half][:, cols], MULT)
             nc.gpsimd.tensor_tensor(dst, dst, weight, MULT)
             y[half, c] = dst
 
@@ -333,18 +338,20 @@ def tile_list_botnet_gated_gradients_kernel(
             if half == 1:
                 nc.sync.dma_start(out=out[c * P : (c + 1) * P, :], in_=page[c][:])
 
-        first_sig = grouped_d1[:, 3 * W // 2 :].bitcast(F32)
+        first_sig = held([P, HALF], F32, "sig00", follows="s60")[:]
         sigmoid_of_gate(0, 0, first_sig)
         raw_y = held([P, HALF], F32, "raw_y", follows="s0")
         nc.vector.scalar_tensor_tensor(out=raw_y[:], in0=val_bank(0, 0)[:], scalar=-1.0, in1=first_sig, op0=MULT, op1=MULT)
+        wg_codes[1] = held([P, HALF], U32, "wg_codes1", follows="sig00")[:]
+        wg_scales[1] = held([P, HALF], U8, "wg_scales1")[:]
+        for b in range(PASSES):
+            words = slice(b * NH, (b + 1) * NH)
+            quantize(wg_codes[1][:, words], wg_scales[1][:, words], grouped_wg1[b])
         y[0, 0] = held([P, HALF], F32, "y00", follows="s1")[:]
         nc.vector.tensor_tensor(y[0, 0], raw_y[:], halves(wgo_sb)[0], MULT)
-        wg_codes[1] = held([P, HALF], U32, "wg_codes1", follows="raw_y")[:]
-        wg_scales[1] = held([P, HALF], U8, "wg_scales1")[:]
-        quantize(wg_codes[1], wg_scales[1], grouped_wg1[:])
         sig01 = held([P, HALF], F32, "sig01", follows="s2")[:]
         y01 = held([P, HALF], F32, "y01", follows="s3")[:]
-        y_on_gpsimd(0, 1, sig01, y01, held([P, HALF], F32, "weight01", follows="grouped_wg1")[:])
+        y_on_gpsimd(0, 1, sig01, y01, held([P, HALF], F32, "weight01", follows="raw_y")[:])
         group(grouped_d1[:, W:], planes[1, 1])
         scatter(0, 0)
         scatter(0, 1)
@@ -355,7 +362,7 @@ def tile_list_botnet_gated_gradients_kernel(
         quantize(codes[:], scales[:], grouped_d1)
         sig02, y02, sig03 = [area[:, 2 * EDGE + 2 * HALF * i : 2 * EDGE + 2 * HALF * (i + 1)].bitcast(F32) for i in range(3)]
         y_on_gpsimd(0, 2, sig02, y02, sig01)
-        y_on_gpsimd(0, 3, sig03, sig02, held([P, HALF], F32, "weight03", follows="grouped_d1")[:])
+        y_on_gpsimd(0, 3, sig03, sig02, second[:, 2 * W - HALF : 2 * W + HALF].bitcast(F32), (right, left))
         scatter(0, 2)
         scatter(0, 3)
         weight = sig03

@@ -75,7 +75,9 @@ def tile_list_botnet_gated_gradients_kernel(
 
         def table_pass(a):
             window = held([P, T], U32, "tab_w%d" % a)
-            load_in_halves(window[:].bitcast(I32), tab_words[a].rearrange("p t i -> p (t i)").bitcast(I32))
+            nc.sync.dma_start(
+                out=window[:].bitcast(I32), in_=tab_words[a].rearrange("p t i -> p (t i)").bitcast(I32)
+            )
             v_w[a] = held([P, S], U32, "v_w%d" % a)
             nc.vector.tensor_copy(v_w[a][:], window[:].indirect(idx[:]))
 
@@ -192,7 +194,7 @@ def tile_list_botnet_gated_gradients_kernel(
         EDGE = 32
         planes11_at = 2 * HALF + EDGE
         grouped_d10 = area[:, planes11_at + EDGE : planes11_at + EDGE + W]
-        slope61_late = area[:, planes11_at + W : planes11_at + W + HALF].bitcast(F32)
+        slope61 = area[:, planes11_at + W : planes11_at + W + 2 * HALF].bitcast(F32)
 
         nc.sync.dma_start(idx[:], offs)
         nc.sync.dma_start(idx2[:], offs2)
@@ -203,10 +205,18 @@ def tile_list_botnet_gated_gradients_kernel(
         grouped_w0 = held([P, 2 * W], BF16, "grouped_w0")
         load_s(0)
         gather_s(0, held([P, S], F32, "s0")[:])
-        load_scale_rows(tab_sc, tab_scales)
+        raw = held([P, PACK, HALF], F32, "raw_w1_00")
+        rows = w1[:PASS, :PASS].rearrange("(p i) c -> p i c", i=PACK)
+        for i in range(PACK):
+            if i == 2:
+                load_scale_rows(tab_sc, tab_scales)
+            nc.sync.dma_start(out=raw[:, i], in_=rows[:, i])
         for a in range(PASSES):
             nc.vector.tensor_copy(v_sc[a][:], tab_sc[:, a * T : (a + 1) * T].indirect(idx[:]))
-        w1_piece(0, 0, grouped_w0[:, :W])
+        nc.scalar.copy(
+            out=grouped_w0[:, :W].rearrange("p (t m i) -> p m i t", t=PACK, i=PACK),
+            in_=raw[:].rearrange("p i (m t) -> p m i t", t=PACK),
+        )
         w1_operand(0, grouped_w0[:, :W], follows=None)
         rest = held([P, S], F32, "rest0", follows="raw_w1_00")
         for half in range(2):
@@ -249,13 +259,17 @@ def tile_list_botnet_gated_gradients_kernel(
         gather_s(5, grouped_w1[:, W:].bitcast(F32))
         grouped_wg0 = held([P, W], BF16, "grouped_wg0", follows="raw_w1_01")
         wg_columns(0, None, [grouped_wg0[:, : W // 2], grouped_wg0[:, W // 2 :]])
-        second = held([P, 5 * W // 2], BF16, "grouped_d1", follows="raw_wg0")
-        set_planes(1, 0, second[:, 3 * W // 2 :])
+        second = held([P, 11 * W // 4], BF16, "grouped_d1", follows="raw_wg0")
+        set_planes(1, 0, second[:, 3 * W // 2 : 5 * W // 2])
         grouped_d1 = second[:, : 2 * W]
         for u in (4, 5):
             make_part(u, 0)
             d_from_part(u, 0, nc.gpsimd)
-        make_slope(5, 1, second[:, 2 * W :].bitcast(F32), s[5, 1])
+        left, right = slice(0, HALF // 2), slice(HALF // 2, HALF)
+        rest51 = [second[:, 2 * W : 9 * W // 4].bitcast(F32), second[:, 5 * W // 2 :].bitcast(F32)]
+        for cols, dst in zip((left, right), rest51):
+            nc.scalar.activation(out=dst, in_=s[5, 1][:, cols], func=COPY, scale=1.0, bias=-1.0)
+        nc.gpsimd.tensor_tensor(s[5, 1][:, left], s[5, 1][:, left], rest51[0], MULT)
         group(grouped_d1[:, :W], planes[0, 1])
         load_s(6, follows="s_win1")
         for half in range(2):
@@ -281,23 +295,23 @@ def tile_list_botnet_gated_gradients_kernel(
         d_scales = {(b, 0): held([P, HALF], U8, "d_scales%d0" % b)[:] for b in range(PASSES)}
         quantize(d_codes[0, 0], d_scales[0, 0], grouped_d00[:])
         gather_s_half(LAST, 1, held([P, HALF], F32, "s71", follows="grouped_wg0")[:])
-        left, right = slice(0, HALF // 2), slice(HALF // 2, HALF)
-        slope61_early = held([P, HALF // 2], F32, "slope61_early", follows="grouped_d00")[:]
-        nc.gpsimd.tensor_tensor(slope61_early, s[6, 1][:, left], rest61[:, left], MULT)
+        slope51_right = held([P, HALF // 2], F32, "slope51_right", follows="grouped_d00")[:]
+        nc.gpsimd.tensor_tensor(slope51_right, s[5, 1][:, right], rest51[1], MULT)
         quantize(d_codes[1, 0], d_scales[1, 0], grouped_d10)
         grouped_wg1 = [second[:, 7 * W // 4 : 9 * W // 4], held([P, W // 2], BF16, "grouped_wg11", follows="s4")[:]]
         wg_columns(1, "s_win5", grouped_wg1)
         wgo_sb = held([P, S], F32, "wgo_sb", follows="s_win6")
         nc.sync.dma_start(out=wgo_sb[:], in_=wgo)
         set_planes(1, 1, area[:, planes11_at : planes11_at + W])
-        nc.gpsimd.tensor_tensor(slope61_late, s[6, 1][:, right], rest61[:, right], MULT)
+        nc.gpsimd.tensor_tensor(slope61, s[6, 1], rest61, MULT)
+        slope[6, 1] = slope61
         make_part(LAST, 1)
         d_from_part(LAST, 1, nc.gpsimd)
-        for u in (4, 5):
-            d_from_slope(u, 1)
-        h61 = h_bank(6, 1)
-        for cols, part_slope in ((left, slope61_early), (right, slope61_late)):
-            nc.vector.tensor_tensor(plane[6, 1][:, cols], h61[:, cols], part_slope, MULT)
+        d_from_slope(4, 1)
+        h51 = h_bank(5, 1)
+        for cols, part_slope in ((left, s[5, 1][:, left]), (right, slope51_right)):
+            nc.vector.tensor_tensor(plane[5, 1][:, cols], h51[:, cols], part_slope, MULT)
+        d_from_slope(6, 1)
 
         def product(name, half, lhsT, lhsT_scale):
             acc = bank(name)

@@ -75,9 +75,7 @@ def tile_list_botnet_gated_gradients_kernel(
 
         def table_pass(a):
             window = held([P, T], U32, "tab_w%d" % a)
-            nc.sync.dma_start(
-                out=window[:].bitcast(I32), in_=tab_words[a].rearrange("p t i -> p (t i)").bitcast(I32)
-            )
+            load_in_halves(window[:].bitcast(I32), tab_words[a].rearrange("p t i -> p (t i)").bitcast(I32))
             v_w[a] = held([P, S], U32, "v_w%d" % a)
             nc.vector.tensor_copy(v_w[a][:], window[:].indirect(idx[:]))
 
@@ -186,15 +184,15 @@ def tile_list_botnet_gated_gradients_kernel(
                 nc.sync.dma_start(out=raw[:, b], in_=rows.rearrange("(p i) c -> p i c", i=PACK))
                 group(dsts[b], raw[:, b])
 
-        area = held([P, 3 * HALF + 2 * W], BF16, "area")
+        area = held([P, 3 * HALF + 3 * W + 2 * HALF], BF16, "area")
         set_planes(0, 0, held([P, W], BF16, "planes00")[:])
         set_planes(0, 1, area[:, :W])
-        grouped_w1 = area[:, 3 * HALF :]
+        grouped_w1 = area[:, 3 * HALF : 3 * HALF + 2 * W]
         rest61 = area[:, : 2 * HALF].bitcast(F32)
         EDGE = 32
-        planes11_at = 2 * HALF + EDGE
+        planes11_at = 3 * HALF + 2 * W
         grouped_d10 = area[:, planes11_at + EDGE : planes11_at + EDGE + W]
-        slope61 = area[:, planes11_at + W : planes11_at + W + 2 * HALF].bitcast(F32)
+        slope51_right = area[:, planes11_at + W : planes11_at + W + HALF].bitcast(F32)
 
         nc.sync.dma_start(idx[:], offs)
         nc.sync.dma_start(idx2[:], offs2)
@@ -205,18 +203,10 @@ def tile_list_botnet_gated_gradients_kernel(
         grouped_w0 = held([P, 2 * W], BF16, "grouped_w0")
         load_s(0)
         gather_s(0, held([P, S], F32, "s0")[:])
-        raw = held([P, PACK, HALF], F32, "raw_w1_00")
-        rows = w1[:PASS, :PASS].rearrange("(p i) c -> p i c", i=PACK)
-        for i in range(PACK):
-            if i == 2:
-                load_scale_rows(tab_sc, tab_scales)
-            nc.sync.dma_start(out=raw[:, i], in_=rows[:, i])
+        load_scale_rows(tab_sc, tab_scales)
         for a in range(PASSES):
             nc.vector.tensor_copy(v_sc[a][:], tab_sc[:, a * T : (a + 1) * T].indirect(idx[:]))
-        nc.scalar.copy(
-            out=grouped_w0[:, :W].rearrange("p (t m i) -> p m i t", t=PACK, i=PACK),
-            in_=raw[:].rearrange("p i (m t) -> p m i t", t=PACK),
-        )
+        w1_piece(0, 0, grouped_w0[:, :W])
         w1_operand(0, grouped_w0[:, :W], follows=None)
         rest = held([P, S], F32, "rest0", follows="raw_w1_00")
         for half in range(2):
@@ -259,17 +249,16 @@ def tile_list_botnet_gated_gradients_kernel(
         gather_s(5, grouped_w1[:, W:].bitcast(F32))
         grouped_wg0 = held([P, W], BF16, "grouped_wg0", follows="raw_w1_01")
         wg_columns(0, None, [grouped_wg0[:, : W // 2], grouped_wg0[:, W // 2 :]])
-        second = held([P, 11 * W // 4], BF16, "grouped_d1", follows="raw_wg0")
+        second = held([P, 3 * W], BF16, "grouped_d1", follows="raw_wg0")
         set_planes(1, 0, second[:, 3 * W // 2 : 5 * W // 2])
         grouped_d1 = second[:, : 2 * W]
         for u in (4, 5):
+            plane[u, 0] = grouped_d10.rearrange("p (c i) -> p c i", i=PACK)[:, :, u - PACK]
             make_part(u, 0)
             d_from_part(u, 0, nc.gpsimd)
         left, right = slice(0, HALF // 2), slice(HALF // 2, HALF)
-        rest51 = [second[:, 2 * W : 9 * W // 4].bitcast(F32), second[:, 5 * W // 2 :].bitcast(F32)]
-        for cols, dst in zip((left, right), rest51):
-            nc.scalar.activation(out=dst, in_=s[5, 1][:, cols], func=COPY, scale=1.0, bias=-1.0)
-        nc.gpsimd.tensor_tensor(s[5, 1][:, left], s[5, 1][:, left], rest51[0], MULT)
+        rest51 = second[:, 5 * W // 2 :].bitcast(F32)
+        nc.scalar.activation(out=rest51, in_=s[5, 1], func=COPY, scale=1.0, bias=-1.0)
         group(grouped_d1[:, :W], planes[0, 1])
         load_s(6, follows="s_win1")
         for half in range(2):
@@ -277,7 +266,6 @@ def tile_list_botnet_gated_gradients_kernel(
         make_part(6, 0)
         d_from_part(6, 0, nc.gpsimd)
         nc.scalar.activation(out=rest61, in_=s[6, 1], func=COPY, scale=1.0, bias=-1.0)
-        group(grouped_d10, planes[1, 0][:, :2], 0)
         load_s(LAST)
         load_scale_rows(wv_sc, wv_scales)
         wv_w = held([P, PASSES, N], U32, "wv_w", follows="rest1")
@@ -295,23 +283,23 @@ def tile_list_botnet_gated_gradients_kernel(
         d_scales = {(b, 0): held([P, HALF], U8, "d_scales%d0" % b)[:] for b in range(PASSES)}
         quantize(d_codes[0, 0], d_scales[0, 0], grouped_d00[:])
         gather_s_half(LAST, 1, held([P, HALF], F32, "s71", follows="grouped_wg0")[:])
-        slope51_right = held([P, HALF // 2], F32, "slope51_right", follows="grouped_d00")[:]
-        nc.gpsimd.tensor_tensor(slope51_right, s[5, 1][:, right], rest51[1], MULT)
+        slope51_left = held([P, HALF // 2], F32, "slope51_left", follows="grouped_d00")[:]
+        nc.gpsimd.tensor_tensor(slope51_left, s[5, 1][:, left], rest51[:, left], MULT)
         quantize(d_codes[1, 0], d_scales[1, 0], grouped_d10)
         grouped_wg1 = [second[:, 7 * W // 4 : 9 * W // 4], held([P, W // 2], BF16, "grouped_wg11", follows="s4")[:]]
         wg_columns(1, "s_win5", grouped_wg1)
         wgo_sb = held([P, S], F32, "wgo_sb", follows="s_win6")
         nc.sync.dma_start(out=wgo_sb[:], in_=wgo)
         set_planes(1, 1, area[:, planes11_at : planes11_at + W])
-        nc.gpsimd.tensor_tensor(slope61, s[6, 1], rest61, MULT)
-        slope[6, 1] = slope61
+        nc.gpsimd.tensor_tensor(slope51_right, s[5, 1][:, right], rest51[:, right], MULT)
+        slope[6, 1] = second[:, 5 * W // 2 :].bitcast(F32)
+        nc.gpsimd.tensor_tensor(slope[6, 1], s[6, 1], rest61, MULT)
         make_part(LAST, 1)
         d_from_part(LAST, 1, nc.gpsimd)
         d_from_slope(4, 1)
         h51 = h_bank(5, 1)
-        for cols, part_slope in ((left, s[5, 1][:, left]), (right, slope51_right)):
+        for cols, part_slope in ((left, slope51_left), (right, slope51_right)):
             nc.vector.tensor_tensor(plane[5, 1][:, cols], h51[:, cols], part_slope, MULT)
-        d_from_slope(6, 1)
 
         def product(name, half, lhsT, lhsT_scale):
             acc = bank(name)
@@ -356,6 +344,7 @@ def tile_list_botnet_gated_gradients_kernel(
         sigmoid_of_gate(0, 0, first_sig)
         raw_y = held([P, HALF], F32, "raw_y", follows="s0")
         nc.vector.scalar_tensor_tensor(out=raw_y[:], in0=val_bank(0, 0)[:], scalar=-1.0, in1=first_sig, op0=MULT, op1=MULT)
+        d_from_slope(6, 1)
         wg_codes[1] = held([P, HALF], U32, "wg_codes1", follows="sig00")[:]
         wg_scales[1] = held([P, HALF], U8, "wg_scales1")[:]
         for b in range(PASSES):
@@ -374,7 +363,7 @@ def tile_list_botnet_gated_gradients_kernel(
         for b in range(PASSES):
             d_codes[b, 1], d_scales[b, 1] = halves(codes)[b], halves(scales)[b]
         quantize(codes[:], scales[:], grouped_d1)
-        sig02, y02, sig03 = [area[:, 2 * EDGE + 2 * HALF * i : 2 * EDGE + 2 * HALF * (i + 1)].bitcast(F32) for i in range(3)]
+        sig02, y02, sig03 = [area[:, planes11_at + EDGE + 2 * HALF * (i - 1) : planes11_at + EDGE + 2 * HALF * i].bitcast(F32) for i in range(3)]
         y_on_gpsimd(0, 2, sig02, y02, sig01)
         y_on_gpsimd(0, 3, sig03, sig02, second[:, 2 * W - HALF : 2 * W + HALF].bitcast(F32), (right, left))
         scatter(0, 2)

@@ -18,6 +18,8 @@ ADD = mybir.AluOpType.add
 COPY = mybir.ActivationFunctionType.Copy
 SIGMOID = mybir.ActivationFunctionType.Sigmoid
 
+BYTES_OF = {F32: 4, BF16: 2, U32: 4, U16: 2, U8: 1}
+
 P = 128
 PACK = 4
 PASS = P * PACK
@@ -37,27 +39,93 @@ def tile_list_botnet_gated_gradients_kernel(
     nc = tc.nc
     with ExitStack() as ctx:
         keep = ctx.enter_context(tc.tile_pool(name="keep", bufs=1))
-        ring = ctx.enter_context(tc.tile_pool(name="ring", bufs=2))
         psum = ctx.enter_context(tc.psum_pool(name="psum", bufs=1))
 
-        tag_of = {}
+        place, top = {}, [0]
 
-        def held(shape, dtype, name, follows=None):
-            tag_of[name] = tag_of[follows] if follows else name
-            return keep.tile(shape, dtype, name=name, tag=tag_of[name], align_bytes=64)
+        def held(shape, dtype, name, follows=None, at=0, spare=0):
+            size = BYTES_OF[dtype]
+            for extent in shape[1:]:
+                size = size * extent
+            if follows:
+                place[name] = place[follows] + at
+            else:
+                place[name] = top[0]
+                top[0] = top[0] + (size + 63) // 64 * 64 + spare
+            return keep.tile(shape, dtype, name=name, align_bytes=64, offset=place[name])
 
         def bank(name):
             return psum.tile([P, HALF], F32, name=name, tag="bank", bufs=BANKS)
 
+        def halves(ap):
+            return ap[:, :HALF], ap[:, HALF:]
+
+        def group(dst, planes):
+            nc.scalar.copy(
+                out=dst.rearrange("p (c x i) -> p c i x", x=RUN, i=PACK),
+                in_=planes.rearrange("p i (c x) -> p c i x", x=RUN),
+            )
+
+        def quantize(codes, scales, grouped):
+            nc.vector.quantize_mx(out=codes.bitcast(E4M3), scales=scales, in_=grouped)
+
+        W = PACK * HALF
+        NH = N // 2
+        HB = HALF * 4
+        EDGE = 64
+
         idx = held([P, S // 16], U16, "idx")
         idx2 = held([P, S // 16], U16, "idx2")
         tab_sc = held([P, PASSES * T], U8, "tab_sc")
-        v_sc = {a: held([P, S], U8, "v_sc%d" % a) for a in range(PASSES)}
         wv_sc = held([P, PASSES * N], U8, "wv_sc")
-        page = [held([P, T2], F32, "page%d" % c) for c in range(PAGES)]
+        page = {}
+
+        def clear_page(c, follows=None):
+            page[c] = held([P, T2], F32, "page%d" % c, follows)
+            nc.gpsimd.memset(page[c][:], 0.0)
 
         nc.gpsimd.memset(tab_sc[:].bitcast(I32), 0)
         nc.gpsimd.memset(wv_sc[:].bitcast(I32), 0)
+        for c in range(PAGES - 1):
+            clear_page(c)
+
+        def load_columns(window, rows, pieces):
+            for k in range(pieces):
+                cols = slice(k * T // pieces, (k + 1) * T // pieces)
+                nc.sync.dma_start(out=window[:, cols], in_=rows[:, cols])
+
+        s_rows = sT.rearrange("(b p t) c -> b t p c", p=P, t=PACK)
+        s_win, s, tab_win, v_w, raw_w1 = {}, {}, {}, {}, {}
+
+        def load_s(u, follows=None, pieces=1, spare=0):
+            s_win[u] = held([P, T], F32, "s_win%d" % u, follows, spare=spare)
+            load_columns(s_win[u][:], s_rows[u // PACK, u % PACK], pieces)
+
+        def load_table(a, pieces=1):
+            tab_win[a] = held([P, T], U32, "tab_w%d" % a)
+            load_columns(tab_win[a][:].bitcast(I32), tab_words[a].rearrange("p t i -> p (t i)").bitcast(I32), pieces)
+
+        def load_w1(a, b, follows=None, rows_of_word=(slice(0, PACK),), at=0, spare=0):
+            if (a, b) not in raw_w1:
+                raw_w1[a, b] = held([P, PACK, HALF], F32, "raw_w1_%d%d" % (a, b), follows, at, spare)
+            rows = w1[a * PASS : (a + 1) * PASS, b * PASS : (b + 1) * PASS].rearrange("(p i) c -> p i c", i=PACK)
+            for part in rows_of_word:
+                nc.sync.dma_start(out=raw_w1[a, b][:, part], in_=rows[:, part])
+
+        def gather_s(u, follows=None):
+            dst = held([P, S], F32, "s%d" % u, follows)
+            nc.vector.tensor_copy(dst[:], s_win[u][:].indirect(idx[:]))
+            s[u, 0], s[u, 1] = halves(dst)
+
+        def gather_s_half(u, half, dst):
+            s[u, half] = dst
+            nc.vector.tensor_copy(s[u, half], s_win[u][:].indirect(idx[:, half * LIST_COLS : (half + 1) * LIST_COLS]))
+
+        v_sc = {}
+
+        def gather_scales(a, follows=None):
+            v_sc[a] = held([P, S], U8, "v_sc%d" % a, follows)
+            nc.vector.tensor_copy(v_sc[a][:], tab_sc[:, a * T : (a + 1) * T].indirect(idx[:]))
 
         def load_scale_rows(tile, scale_rows):
             for quad in range(4):
@@ -66,70 +134,24 @@ def tile_list_botnet_gated_gradients_kernel(
                     in_=scale_rows[:, 4 * quad : 4 * quad + 4, :].bitcast(I32).rearrange("a x c -> x a c"),
                 )
 
-        def load_in_halves(window, rows):
-            for half in range(2):
-                cols = slice(half * T // 2, (half + 1) * T // 2)
-                nc.sync.dma_start(out=window[:, cols], in_=rows[:, cols])
-
-        v_w = {}
-
-        def table_pass(a):
-            window = held([P, T], U32, "tab_w%d" % a)
-            load_in_halves(window[:].bitcast(I32), tab_words[a].rearrange("p t i -> p (t i)").bitcast(I32))
+        def gather_table(a):
             v_w[a] = held([P, S], U32, "v_w%d" % a)
-            nc.vector.tensor_copy(v_w[a][:], window[:].indirect(idx[:]))
+            nc.vector.tensor_copy(v_w[a][:], tab_win[a][:].indirect(idx[:]))
 
-        def group(dst, planes, first=0):
-            count = planes.shape[1]
-            nc.scalar.copy(
-                out=dst.rearrange("p (c x i) -> p c i x", x=RUN, i=PACK)[:, :, first : first + count, :],
-                in_=planes.rearrange("p i (c x) -> p c i x", x=RUN),
-            )
+        w1_q, d_q, wg_q = {}, {}, {}
 
-        def quantize(codes, scales, grouped):
-            nc.vector.quantize_mx(out=codes.bitcast(E4M3), scales=scales, in_=grouped)
-
-        def load_weight(name, rows, follows):
-            raw = held([P, PACK, HALF], F32, name, follows)
-            nc.sync.dma_start(out=raw[:], in_=rows.rearrange("(p i) c -> p i c", i=PACK))
-            return raw
-
-        def w1_piece(a, b, dst, follows=None):
-            raw = load_weight(
-                "raw_w1_%d%d" % (a, b), w1[a * PASS : (a + 1) * PASS, b * PASS : (b + 1) * PASS], follows
-            )
+        def round_w1(a, b, dst):
             nc.scalar.copy(
                 out=dst.rearrange("p (t m i) -> p m i t", t=PACK, i=PACK),
-                in_=raw[:].rearrange("p i (m t) -> p m i t", t=PACK),
+                in_=raw_w1[a, b][:].rearrange("p i (m t) -> p m i t", t=PACK),
             )
 
-        s_rows = sT.rearrange("(b p t) c -> b t p c", p=P, t=PACK)
-        s_win, s, slope, part, plane = {}, {}, {}, {}, {}
-
-        def halves(ap):
-            return ap[:, :HALF], ap[:, HALF:]
-
-        def load_s(u, follows=None):
-            s_win[u] = held([P, T], F32, "s_win%d" % u, follows)
-            if u == 0:
-                load_in_halves(s_win[u][:], s_rows[0, 0])
-            else:
-                nc.sync.dma_start(out=s_win[u][:], in_=s_rows[u // PACK, u % PACK])
-
-        def gather_s(u, dst):
-            nc.vector.tensor_copy(dst, s_win[u][:].indirect(idx[:]))
-            s[u, 0], s[u, 1] = halves(dst)
-
-        def gather_s_half(u, half, dst):
-            nc.vector.tensor_copy(dst, s_win[u][:].indirect(idx[:, half * LIST_COLS : (half + 1) * LIST_COLS]))
-            s[u, half] = dst
-
-        def make_slope(u, half, rest, dst):
-            nc.scalar.activation(out=rest, in_=s[u, half], func=COPY, scale=1.0, bias=-1.0)
-            nc.gpsimd.tensor_tensor(dst, s[u, half], rest, MULT)
-            slope[u, half] = dst
-
-        w1_codes, w1_scales = {}, {}
+        def quantize_pieces(name, grouped, follows=None):
+            words = grouped.shape[1] // PACK
+            codes = held([P, words], U32, name + "_codes", follows)
+            scales = held([P, words], U8, name + "_scales")
+            quantize(codes[:], scales[:], grouped)
+            return [(codes[:, k : k + HALF], scales[:, k : k + HALF]) for k in range(0, words, HALF)]
 
         def h_bank(u, half):
             b, t = divmod(u, PACK)
@@ -139,8 +161,8 @@ def tile_list_botnet_gated_gradients_kernel(
             for a in range(PASSES):
                 nc.tensor.matmul_mx(
                     out=acc[:],
-                    lhsT=w1_codes[a, b][:, words].bitcast(E4M3),
-                    lhsT_scale=w1_scales[a, b][:, words],
+                    lhsT=w1_q[a, b][0][:, words].bitcast(E4M3),
+                    lhsT_scale=w1_q[a, b][1][:, words],
                     rhs=v_w[a][:, entries].bitcast(E5M2),
                     rhs_scale=v_sc[a][:, entries],
                     start=(a == 0),
@@ -148,230 +170,249 @@ def tile_list_botnet_gated_gradients_kernel(
                 )
             return acc
 
-        def d_from_slope(u, half):
-            nc.vector.tensor_tensor(plane[u, half], h_bank(u, half)[:], slope[u, half], MULT)
-
-        def make_part(u, half, dst=None):
-            if dst is None:
-                dst = ring.tile([P, HALF], F32, name="part%d%d" % (u, half), tag="part", bufs=4)[:]
-            part[u, half] = dst
-            nc.vector.scalar_tensor_tensor(
-                out=dst, in0=s[u, half], scalar=-1.0, in1=h_bank(u, half)[:], op0=ADD, op1=MULT
-            )
-
-        def d_from_part(u, half, engine):
-            engine.tensor_tensor(plane[u, half], part[u, half], s[u, half], MULT)
-
-        W = PACK * HALF
         planes = {}
 
-        def set_planes(b, half, flat):
-            planes[b, half] = flat.rearrange("p (i c) -> p i c", i=PACK)
-            for t in range(PACK):
-                plane[b * PACK + t, half] = planes[b, half][:, t, :]
+        def plane(u, half):
+            return planes[u // PACK, half][:, u % PACK, :]
 
-        def w1_operand(a, grouped, follows):
-            w1_codes[a, 0] = held([P, HALF], U32, "w1_codes%d0" % a, follows)
-            w1_scales[a, 0] = held([P, HALF], U8, "w1_scales%d0" % a)
-            quantize(w1_codes[a, 0][:], w1_scales[a, 0][:], grouped)
+        slope, part = {}, {}
 
-        NH = N // 2
+        def less_one(u, half, dst):
+            slope[u, half] = dst
+            nc.scalar.activation(out=slope[u, half], in_=s[u, half], func=COPY, scale=1.0, bias=-1.0)
 
-        def wg_columns(k, follows, dsts):
-            raw = held([P, PASSES, PACK, NH], F32, "raw_wg%d" % k, follows)
-            for b in range(PASSES):
-                rows = wg[b * PASS : (b + 1) * PASS, k * NH : (k + 1) * NH]
-                nc.sync.dma_start(out=raw[:, b], in_=rows.rearrange("(p i) c -> p i c", i=PACK))
-                group(dsts[b], raw[:, b])
+        def make_slope(u, half):
+            nc.gpsimd.tensor_tensor(slope[u, half], s[u, half], slope[u, half], MULT)
 
-        area = held([P, 3 * HALF + 3 * W + 2 * HALF], BF16, "area")
-        set_planes(0, 0, held([P, W], BF16, "planes00")[:])
-        set_planes(0, 1, area[:, :W])
-        grouped_w1 = area[:, 3 * HALF : 3 * HALF + 2 * W]
-        rest61 = area[:, : 2 * HALF].bitcast(F32)
-        EDGE = 32
-        planes11_at = 3 * HALF + 2 * W
-        grouped_d10 = area[:, planes11_at + EDGE : planes11_at + EDGE + W]
-        slope51_right = area[:, planes11_at + W : planes11_at + W + HALF].bitcast(F32)
+        def copy_h(u, half, dst):
+            part[u, half] = dst
+            nc.scalar.copy(out=part[u, half], in_=h_bank(u, half)[:])
+
+        def d_on_gpsimd(u, half):
+            nc.gpsimd.tensor_tensor(plane(u, half), part[u, half], slope[u, half], MULT)
+
+        def d_on_vector(u, half):
+            nc.vector.tensor_tensor(plane(u, half), h_bank(u, half)[:], slope[u, half], MULT)
+
+        def make_part(u, half, dst):
+            part[u, half] = dst
+            nc.vector.scalar_tensor_tensor(
+                out=part[u, half], in0=s[u, half], scalar=-1.0, in1=h_bank(u, half)[:], op0=ADD, op1=MULT
+            )
+
+        def finish_part(u, half):
+            nc.gpsimd.tensor_tensor(plane(u, half), part[u, half], s[u, half], MULT)
+
+        raw_wg = {}
+
+        def load_wg(k, b, raw):
+            raw_wg[k, b] = raw
+            rows = wg[b * PASS : (b + 1) * PASS, k * NH : (k + 1) * NH]
+            nc.sync.dma_start(out=raw, in_=rows.rearrange("(p i) c -> p i c", i=PACK))
+
+        def round_wg(k, b, dst):
+            group(dst[:, b * W // 2 : (b + 1) * W // 2], raw_wg[k, b])
+
+        def half_tile(name, follows=None, at=0):
+            return held([P, HALF], F32, name, follows, at)[:]
 
         nc.sync.dma_start(idx[:], offs)
         nc.sync.dma_start(idx2[:], offs2)
-        for c in range(PAGES):
-            nc.gpsimd.memset(page[c][:], 0.0)
-        table_pass(0)
-        table_pass(1)
-        grouped_w0 = held([P, 2 * W], BF16, "grouped_w0")
-        load_s(0)
-        gather_s(0, held([P, S], F32, "s0")[:])
+        load_s(0, pieces=2, spare=4 * HB)
+        load_table(0, pieces=2)
+        load_w1(0, 0, rows_of_word=(slice(0, 1), slice(1, 2)))
         load_scale_rows(tab_sc, tab_scales)
-        for a in range(PASSES):
-            nc.vector.tensor_copy(v_sc[a][:], tab_sc[:, a * T : (a + 1) * T].indirect(idx[:]))
-        w1_piece(0, 0, grouped_w0[:, :W])
-        w1_operand(0, grouped_w0[:, :W], follows=None)
-        rest = held([P, S], F32, "rest0", follows="raw_w1_00")
-        for half in range(2):
-            make_slope(0, half, halves(rest)[half], halves(grouped_w0[:, :W].bitcast(F32))[half])
+        load_w1(0, 0, rows_of_word=(slice(2, 4),))
+        load_table(1)
+        load_w1(1, 0)
         load_s(1)
-        gather_s(1, held([P, S], F32, "s1")[:])
-        w1_piece(1, 0, grouped_w0[:, W:])
         load_s(2)
-        gather_s(2, held([P, S], F32, "s2")[:])
-        w1_operand(1, grouped_w0[:, W:], follows="s_win2")
-        rest = held([P, S], F32, "rest1", follows="raw_w1_10")
-        for half in range(2):
-            make_slope(1, half, halves(rest)[half], halves(grouped_w0[:, W:].bitcast(F32))[half])
-        load_s(3)
-        gather_s(3, held([P, S], F32, "s3")[:])
-        part2 = held([P, S], F32, "part2", follows="s_win3")
-        for half in range(2):
-            make_part(2, half, halves(part2)[half])
-            d_from_part(2, half, nc.gpsimd)
-        make_part(3, 0)
-        d_from_part(3, 0, nc.gpsimd)
-        make_part(3, 1)
-        for u in range(2):
-            for half in range(2):
-                d_from_slope(u, half)
-        w1_piece(0, 1, grouped_w1[:, :W], follows="tab_w0")
-        w1_piece(1, 1, grouped_w1[:, W:], follows="tab_w1")
-        grouped_d00 = held([P, W], BF16, "grouped_d00", follows="raw_w1_11")
-        group(grouped_d00[:], planes[0, 0])
-        load_s(4)
-        gather_s(4, held([P, S], F32, "s4")[:])
-        codes = held([P, 2 * HALF], U32, "w1_codes1", follows="s_win4")
-        scales = held([P, 2 * HALF], U8, "w1_scales1")
-        for a in range(PASSES):
-            w1_codes[a, 1], w1_scales[a, 1] = halves(codes)[a], halves(scales)[a]
-        quantize(codes[:], scales[:], grouped_w1)
-        d_from_part(3, 1, nc.gpsimd)
-        make_slope(4, 1, held([P, HALF], F32, "rest41", follows="planes00")[:], s[4, 1])
-        load_s(5, follows="s_win0")
-        gather_s(5, grouped_w1[:, W:].bitcast(F32))
-        grouped_wg0 = held([P, W], BF16, "grouped_wg0", follows="raw_w1_01")
-        wg_columns(0, None, [grouped_wg0[:, : W // 2], grouped_wg0[:, W // 2 :]])
-        second = held([P, 3 * W], BF16, "grouped_d1", follows="raw_wg0")
-        set_planes(1, 0, second[:, 3 * W // 2 : 5 * W // 2])
-        grouped_d1 = second[:, : 2 * W]
-        for u in (4, 5):
-            plane[u, 0] = grouped_d10.rearrange("p (c i) -> p c i", i=PACK)[:, :, u - PACK]
-            make_part(u, 0)
-            d_from_part(u, 0, nc.gpsimd)
-        left, right = slice(0, HALF // 2), slice(HALF // 2, HALF)
-        rest51 = second[:, 5 * W // 2 :].bitcast(F32)
-        nc.scalar.activation(out=rest51, in_=s[5, 1], func=COPY, scale=1.0, bias=-1.0)
-        group(grouped_d1[:, :W], planes[0, 1])
-        load_s(6, follows="s_win1")
-        for half in range(2):
-            gather_s_half(6, half, held([P, HALF], F32, "s6%d" % half)[:])
-        make_part(6, 0)
-        d_from_part(6, 0, nc.gpsimd)
-        nc.scalar.activation(out=rest61, in_=s[6, 1], func=COPY, scale=1.0, bias=-1.0)
-        load_s(LAST)
-        load_scale_rows(wv_sc, wv_scales)
-        wv_w = held([P, PASSES, N], U32, "wv_w", follows="rest1")
-        nc.sync.dma_start(out=wv_w[:].bitcast(I32), in_=wv_words.rearrange("b p c i -> p b (c i)").bitcast(I32))
+        load_w1(0, 1, spare=EDGE)
+        load_s(3, spare=10 * HB)
+        planes[0, 0] = held([P, PACK, HALF], BF16, "planes00")[:]
+        area0 = held([P, 3 * HALF + 2 * W], BF16, "area0")
+        planes[0, 1] = area0[:, :W].rearrange("p (i c) -> p i c", i=PACK)
+        w1_second = area0[:, 3 * HALF :]
 
-        gather_s_half(LAST, 0, held([P, HALF], F32, "s70")[:])
-        make_part(LAST, 0, held([P, HALF], F32, "part70")[:])
-        d_from_part(LAST, 0, nc.vector)
-        group(grouped_d10, planes[1, 0][:, 2:], 2)
-        wg_codes = {0: held([P, HALF], U32, "wg_codes0", follows="part70")[:]}
-        wg_scales = {0: held([P, HALF], U8, "wg_scales0")[:]}
-        quantize(wg_codes[0], wg_scales[0], grouped_wg0[:])
-        d_codes = {(0, 0): held([P, HALF], U32, "d_codes00", follows="s70")[:]}
-        d_codes[1, 0] = held([P, HALF], U32, "d_codes10")[:]
-        d_scales = {(b, 0): held([P, HALF], U8, "d_scales%d0" % b)[:] for b in range(PASSES)}
-        quantize(d_codes[0, 0], d_scales[0, 0], grouped_d00[:])
-        gather_s_half(LAST, 1, held([P, HALF], F32, "s71", follows="grouped_wg0")[:])
-        slope51_left = held([P, HALF // 2], F32, "slope51_left", follows="grouped_d00")[:]
-        nc.gpsimd.tensor_tensor(slope51_left, s[5, 1][:, left], rest51[:, left], MULT)
-        quantize(d_codes[1, 0], d_scales[1, 0], grouped_d10)
-        grouped_wg1 = [second[:, 7 * W // 4 : 9 * W // 4], held([P, W // 2], BF16, "grouped_wg11", follows="s4")[:]]
-        wg_columns(1, "s_win5", grouped_wg1)
-        wgo_sb = held([P, S], F32, "wgo_sb", follows="s_win6")
+        gather_s(0)
+        load_w1(1, 1, follows="s_win0", at=EDGE)
+        for half in range(2):
+            less_one(0, half, half_tile("slope0%d" % half))
+            make_slope(0, half)
+        gather_table(0)
+        load_s(4, follows="tab_w0")
+        for a in range(PASSES):
+            gather_scales(a)
+        w1_00 = held([P, T], F32, "w1_00")[:, : W // 2].bitcast(BF16)
+        round_w1(0, 0, w1_00)
+        load_s(5, follows="raw_w1_00")
+        (w1_q[0, 0],) = quantize_pieces("w1_00", w1_00)
+        clear_page(PAGES - 1, follows="w1_00")
+        gather_table(1)
+        load_s(6, follows="tab_w1")
+        w1_10 = held([P, W], BF16, "w1_10")
+        round_w1(1, 0, w1_10[:])
+        load_s(7, follows="raw_w1_10")
+        gather_s(1)
+        (w1_q[1, 0],) = quantize_pieces("w1_10", w1_10[:], follows="s_win1")
+        less_one(1, 0, half_tile("slope10"))
+        make_slope(1, 0)
+        for half in range(2):
+            copy_h(0, half, half_tile("h_sb0%d" % half, "s0", half * HB))
+            d_on_gpsimd(0, half)
+        copy_h(1, 0, half_tile("h_sb10", "s_win1", HB))
+        d_on_gpsimd(1, 0)
+        gather_s(2)
+        round_w1(0, 1, w1_second[:, :W])
+        for b in range(PASSES):
+            load_wg(0, b, held([P, PACK, NH], F32, "raw_wg0%d" % b, "raw_w1_01", EDGE + 2 * b * HB)[:])
+        make_part(2, 0, half_tile("part20", "s_win2"))
+        make_part(1, 1, half_tile("part11", "s_win2", HB))
+        finish_part(2, 0)
+        gather_s(3)
+        STEP = 5 * HALF
+        area1 = held([P, PACK * STEP], BF16, "area1", follows="s_win3", at=4 * HB - EDGE)
+        planes[1, 1] = area1[:].rearrange("p (i c) -> p i c", i=PACK)[:, :, :HALF]
+        d10_at = STEP + HALF - 32
+        WG1_AT = 2 * STEP + HALF - 64
+        d10_grouped = area1[:, d10_at : d10_at + W]
+        load_wg(1, 0, d10_grouped.bitcast(F32).rearrange("p (i c) -> p i c", i=PACK))
+        load_wg(1, 1, held([P, PACK, NH], F32, "raw_wg11", "s_win3")[:])
+        load_scale_rows(wv_sc, wv_scales)
+        make_part(2, 1, half_tile("part21", "s_win2", 2 * HB))
+        make_part(3, 0, half_tile("part30", "s_win2", 3 * HB))
+        make_part(3, 1, half_tile("part31", "s_win1", 2 * HB))
+        finish_part(1, 1)
+        finish_part(3, 0)
+        finish_part(2, 1)
+        round_w1(1, 1, w1_second[:, W:])
+        wv_w = held([P, PASSES, N], U32, "wv_w", follows="raw_w1_11", at=-EDGE)
+        nc.sync.dma_start(out=wv_w[:].bitcast(I32), in_=wv_words.rearrange("b p c i -> p b (c i)").bitcast(I32))
+        wgo_sb = held([P, S], F32, "wgo_sb", follows="raw_w1_11", at=2 * HB - EDGE)
         nc.sync.dma_start(out=wgo_sb[:], in_=wgo)
-        set_planes(1, 1, area[:, planes11_at : planes11_at + W])
-        nc.gpsimd.tensor_tensor(slope51_right, s[5, 1][:, right], rest51[:, right], MULT)
-        slope[6, 1] = second[:, 5 * W // 2 :].bitcast(F32)
-        nc.gpsimd.tensor_tensor(slope[6, 1], s[6, 1], rest61, MULT)
-        make_part(LAST, 1)
-        d_from_part(LAST, 1, nc.gpsimd)
-        d_from_slope(4, 1)
-        h51 = h_bank(5, 1)
-        for cols, part_slope in ((left, slope51_left), (right, slope51_right)):
-            nc.vector.tensor_tensor(plane[5, 1][:, cols], h51[:, cols], part_slope, MULT)
+        early = held([P, 2 * W], BF16, "early", follows="s_win0", at=4 * HB)[:]
+        group(early[:, :W], planes[0, 0])
+        gather_s(4)
+        w1_q[0, 1], w1_q[1, 1] = quantize_pieces("w1_1", w1_second, follows="s_win4")
+        finish_part(3, 1)
+        planes[1, 0] = held([P, PACK, HALF], BF16, "planes10", follows="w1_10")[:]
+        rest41 = half_tile("rest41", "part11")
+        less_one(4, 1, rest41)
+        slope[4, 1] = w1_second[:, W : W + 2 * HALF].bitcast(F32)
+        nc.gpsimd.tensor_tensor(slope[4, 1], s[4, 1], rest41, MULT)
+        second = held([P, 2 * W], BF16, "second")
+        group(second[:, :W], planes[0, 1])
+        gather_s_half(5, 0, half_tile("s50"))
+        for u in (4, 5):
+            make_part(u, 0, half_tile("part%d0" % u, "slope0%d" % (u - 4)))
+            finish_part(u, 0)
+        copy_h(4, 1, half_tile("h_sb41", "s_win4", 2 * HB))
+        gather_s_half(6, 0, half_tile("s60"))
+        make_part(6, 0, half_tile("part60", "slope10"))
+        finish_part(6, 0)
+        gather_s_half(7, 0, half_tile("s70"))
+        make_part(7, 0, area1[:, : 2 * HALF].bitcast(F32))
+        finish_part(7, 0)
+        d_on_gpsimd(4, 1)
+        for b in range(PASSES):
+            round_wg(0, b, early[:, W:])
+        wg1_grouped = area1[:, WG1_AT : WG1_AT + W]
+        round_wg(1, 0, wg1_grouped)
+        group(d10_grouped, planes[1, 0])
+        round_wg(1, 1, wg1_grouped)
+        gather_s_half(5, 1, half_tile("s51", "raw_wg00", -EDGE))
+        gather_s_half(6, 1, half_tile("s61", "raw_wg00", HB - EDGE))
+        make_part(5, 1, half_tile("part51", "s_win1", 3 * HB))
+        make_part(6, 1, half_tile("part61", "part20"))
+        d_q[0, 0], wg_q[0] = quantize_pieces("early", early)
+        (d_q[1, 0],) = quantize_pieces("d10", d10_grouped)
+        finish_part(5, 1)
+        gather_s_half(7, 1, area1[:, STEP + HALF : STEP + 3 * HALF].bitcast(F32))
+        (wg_q[1],) = quantize_pieces("wg1", wg1_grouped, follows="s_win7")
 
         def product(name, half, lhsT, lhsT_scale):
             acc = bank(name)
-            for b in range(PASSES):
+            for b in reversed(range(PASSES)):
                 nc.tensor.matmul_mx(
                     out=acc[:],
                     lhsT=lhsT[b].bitcast(E4M3),
                     lhsT_scale=lhsT_scale[b],
-                    rhs=d_codes[b, half].bitcast(E4M3),
-                    rhs_scale=d_scales[b, half],
-                    start=(b == 0),
-                    stop=(b == PASSES - 1),
+                    rhs=d_q[b, half][0].bitcast(E4M3),
+                    rhs_scale=d_q[b, half][1],
+                    start=(b == PASSES - 1),
+                    stop=(b == 0),
                 )
             return acc
+
+        weight, y = {}, {}
 
         def sigmoid_of_gate(half, c, sig):
             k, first = divmod(c * P, NH)
             words = [slice(b * NH + first, b * NH + first + P) for b in range(PASSES)]
-            gate = product("gate%d%d" % (half, c), half, [wg_codes[k][:, w] for w in words], [wg_scales[k][:, w] for w in words])
+            gate = product("gate%d%d" % (half, c), half, [wg_q[k][0][:, w] for w in words], [wg_q[k][1][:, w] for w in words])
             nc.scalar.activation(out=sig, in_=gate[:], func=SIGMOID, scale=-1.0)
+
+        def weigh(half, c, sig, dst):
+            weight[half, c] = dst
+            nc.gpsimd.tensor_tensor(dst, sig, halves(wgo_sb)[half], MULT)
+
+        def make_weight(half, c, sig, dst):
+            sigmoid_of_gate(half, c, sig)
+            weigh(half, c, sig, dst)
 
         def val_bank(half, c):
             words = [wv_w[:, b, c * P : (c + 1) * P] for b in range(PASSES)]
             return product("val%d%d" % (half, c), half, words, [wv_sc[:, b * N + c * P : b * N + (c + 1) * P] for b in range(PASSES)])
 
-        y = {}
-
-        def y_on_gpsimd(half, c, sig, dst, weight, pieces=(slice(0, HALF),)):
-            sigmoid_of_gate(half, c, sig)
-            nc.scalar.activation(out=dst, in_=val_bank(half, c)[:], func=COPY, scale=-1.0)
-            for cols in pieces:
-                nc.gpsimd.tensor_tensor(weight[:, cols], sig[:, cols], halves(wgo_sb)[half][:, cols], MULT)
-            nc.gpsimd.tensor_tensor(dst, dst, weight, MULT)
+        def y_on_gpsimd(half, c, val, dst, between=None):
             y[half, c] = dst
+            nc.scalar.activation(out=val, in_=val_bank(half, c)[:], func=COPY, scale=-1.0)
+            if between:
+                between()
+            nc.gpsimd.tensor_tensor(dst, val, weight[half, c], MULT)
+
+        def y_on_vector(half, c, dst):
+            y[half, c] = dst
+            nc.vector.scalar_tensor_tensor(
+                out=y[half, c], in0=val_bank(half, c)[:], scalar=-1.0, in1=weight[half, c], op0=MULT, op1=MULT
+            )
 
         def scatter(half, c):
             nc.vector.tensor_copy(page[c][:].indirect(idx2[:, half * LIST_COLS : (half + 1) * LIST_COLS]), y[half, c])
             if half == 1:
                 nc.sync.dma_start(out=out[c * P : (c + 1) * P, :], in_=page[c][:])
 
-        first_sig = held([P, HALF], F32, "sig00", follows="s60")[:]
-        sigmoid_of_gate(0, 0, first_sig)
-        raw_y = held([P, HALF], F32, "raw_y", follows="s0")
-        nc.vector.scalar_tensor_tensor(out=raw_y[:], in0=val_bank(0, 0)[:], scalar=-1.0, in1=first_sig, op0=MULT, op1=MULT)
-        d_from_slope(6, 1)
-        wg_codes[1] = held([P, HALF], U32, "wg_codes1", follows="sig00")[:]
-        wg_scales[1] = held([P, HALF], U8, "wg_scales1")[:]
-        for b in range(PASSES):
-            words = slice(b * NH, (b + 1) * NH)
-            quantize(wg_codes[1][:, words], wg_scales[1][:, words], grouped_wg1[b])
-        y[0, 0] = held([P, HALF], F32, "y00", follows="s1")[:]
-        nc.vector.tensor_tensor(y[0, 0], raw_y[:], halves(wgo_sb)[0], MULT)
-        sig01 = held([P, HALF], F32, "sig01", follows="s2")[:]
-        y01 = held([P, HALF], F32, "y01", follows="s3")[:]
-        y_on_gpsimd(0, 1, sig01, y01, held([P, HALF], F32, "weight01", follows="raw_y")[:])
-        group(grouped_d1[:, W:], planes[1, 1])
+        sig00 = half_tile("sig00", "early")
+        sigmoid_of_gate(0, 0, sig00)
+        val_wgo = area1[:, 3 * STEP - 3 * HALF // 2 : 3 * STEP + HALF // 2].bitcast(F32)
+        nc.vector.scalar_tensor_tensor(
+            out=val_wgo, in0=val_bank(0, 0)[:], scalar=-1.0, in1=halves(wgo_sb)[0], op0=MULT, op1=MULT
+        )
+        finish_part(6, 1)
+        make_part(7, 1, area1[:, 2 * STEP + HALF : 2 * STEP + 3 * HALF].bitcast(F32))
+        ys = [half_tile("y%d" % c, "s_win6", c * HB) for c in range(2)]
+        y[0, 0] = ys[0]
+        nc.vector.tensor_tensor(y[0, 0], val_wgo, sig00, MULT)
+        make_weight(0, 1, area1[:, 3 * STEP + HALF // 2 : 3 * STEP + 5 * HALF // 2].bitcast(F32), half_tile("weight01", "sig00"))
+        finish_part(7, 1)
+        y_on_gpsimd(0, 1, ys[1], ys[1])
         scatter(0, 0)
+        sig02 = half_tile("sig02", "s_win5", HB)
+        sigmoid_of_gate(0, 2, sig02)
+        weigh(0, 2, sig02, half_tile("weight02", "weight01"))
+        y_on_gpsimd(0, 2, half_tile("val02", "s_win6", 2 * HB), area1[:, : 2 * HALF].bitcast(F32), lambda: group(second[:, W:], planes[1, 1]))
         scatter(0, 1)
-        codes = held([P, 2 * HALF], U32, "d1_codes", follows="y01")
-        scales = held([P, 2 * HALF], U8, "d1_scales")
-        for b in range(PASSES):
-            d_codes[b, 1], d_scales[b, 1] = halves(codes)[b], halves(scales)[b]
-        quantize(codes[:], scales[:], grouped_d1)
-        sig02, y02, sig03 = [area[:, planes11_at + EDGE + 2 * HALF * (i - 1) : planes11_at + EDGE + 2 * HALF * i].bitcast(F32) for i in range(3)]
-        y_on_gpsimd(0, 2, sig02, y02, sig01)
-        y_on_gpsimd(0, 3, sig03, sig02, second[:, 2 * W - HALF : 2 * W + HALF].bitcast(F32), (right, left))
+        d_q[0, 1], d_q[1, 1] = quantize_pieces("d1", second[:], follows="y0")
+        make_weight(0, 3, half_tile("sig03", "s_win5", 2 * HB), half_tile("weight03", "second"))
+        y03 = half_tile("y03", "s_win6", 3 * HB)
+        y_on_gpsimd(0, 3, y03, y03)
         scatter(0, 2)
         scatter(0, 3)
-        weight = sig03
+        before = "weight03"
         for c in range(PAGES):
-            sig = ring.tile([P, HALF], F32, name="sig1%d" % c, tag="sig", bufs=3)[:]
-            dst = ring.tile([P, HALF], F32, name="y1%d" % c, tag="y", bufs=3)[:]
-            y_on_gpsimd(1, c, sig, dst, weight)
-            weight = sig
+            sig_c = half_tile("sig1%d" % c, "s_win4", c * HB)
+            make_weight(1, c, sig_c, half_tile("weight1%d" % c, before))
+            before = "weight1%d" % c
+            y_c = half_tile("y1%d" % c, "s_win1", c * HB)
+            y_on_gpsimd(1, c, y_c, y_c)
             scatter(1, c)

@@ -30,6 +30,7 @@ ROW_TILES = H // P
 LAST = ROW_TILES - 1
 PAGES = N // P
 RUN = 4
+LINE = 2
 BANKS = 8
 
 
@@ -54,15 +55,31 @@ def tile_list_botnet_gated_gradients_kernel(
                 top[0] = top[0] + (size + 63) // 64 * 64 + spare
             return keep.tile(shape, dtype, name=name, align_bytes=64, offset=place[name])
 
-        def bank(name):
-            return psum.tile([P, HALF], F32, name=name, tag="bank", bufs=BANKS)
+        bank_of, turn = {}, [0]
+
+        def bank(name, follows=None):
+            if follows:
+                bank_of[name] = bank_of[follows]
+            else:
+                bank_of[name] = turn[0] % BANKS
+                turn[0] = turn[0] + 1
+            return psum.tile([P, HALF], F32, name=name, offset=bank_of[name] * HALF * 4)
 
         def halves(ap):
             return ap[:, :HALF], ap[:, HALF:]
 
-        def group(dst, planes):
+        def grouped_view(dst, first, count, run=RUN):
+            return dst.rearrange("p (c x i) -> p c i x", x=run, i=PACK)[:, :, first : first + count, :]
+
+        def two(flat, first, step):
+            return flat[:, first : first + 2 * step].rearrange("p (i c) -> p i c", i=2)[:, :, :HALF]
+
+        def runs(flat):
+            return flat.rearrange("p i (c x) -> p c i x", x=LINE)
+
+        def group(dst, planes, first=0):
             nc.scalar.copy(
-                out=dst.rearrange("p (c x i) -> p c i x", x=RUN, i=PACK),
+                out=grouped_view(dst, first, planes.shape[1]),
                 in_=planes.rearrange("p i (c x) -> p c i x", x=RUN),
             )
 
@@ -86,7 +103,7 @@ def tile_list_botnet_gated_gradients_kernel(
 
         nc.gpsimd.memset(tab_sc[:].bitcast(I32), 0)
         nc.gpsimd.memset(wv_sc[:].bitcast(I32), 0)
-        for c in range(PAGES - 1):
+        for c in range(PAGES):
             clear_page(c)
 
         def load_columns(window, rows, pieces):
@@ -146,16 +163,16 @@ def tile_list_botnet_gated_gradients_kernel(
                 in_=raw_w1[a, b][:].rearrange("p i (m t) -> p m i t", t=PACK),
             )
 
-        def quantize_pieces(name, grouped, follows=None):
+        def quantize_pieces(name, grouped, follows=None, at=0, scales_follow=None):
             words = grouped.shape[1] // PACK
-            codes = held([P, words], U32, name + "_codes", follows)
-            scales = held([P, words], U8, name + "_scales")
+            codes = held([P, words], U32, name + "_codes", follows, at)
+            scales = held([P, words], U8, name + "_scales", scales_follow)
             quantize(codes[:], scales[:], grouped)
             return [(codes[:, k : k + HALF], scales[:, k : k + HALF]) for k in range(0, words, HALF)]
 
-        def h_bank(u, half):
+        def h_bank(u, half, follows=None):
             b, t = divmod(u, PACK)
-            acc = bank("h%d%d" % (u, half))
+            acc = bank("h%d%d" % (u, half), follows)
             entries = slice(half * HALF, (half + 1) * HALF)
             words = slice(t * P, (t + 1) * P)
             for a in range(PASSES):
@@ -181,8 +198,11 @@ def tile_list_botnet_gated_gradients_kernel(
             slope[u, half] = dst
             nc.scalar.activation(out=slope[u, half], in_=s[u, half], func=COPY, scale=1.0, bias=-1.0)
 
-        def make_slope(u, half):
-            nc.gpsimd.tensor_tensor(slope[u, half], s[u, half], slope[u, half], MULT)
+        def make_slope(u, half, dst=None):
+            rest = slope[u, half]
+            if dst is not None:
+                slope[u, half] = dst
+            nc.gpsimd.tensor_tensor(slope[u, half], s[u, half], rest, MULT)
 
         def copy_h(u, half, dst):
             part[u, half] = dst
@@ -194,10 +214,10 @@ def tile_list_botnet_gated_gradients_kernel(
         def d_on_vector(u, half):
             nc.vector.tensor_tensor(plane(u, half), h_bank(u, half)[:], slope[u, half], MULT)
 
-        def make_part(u, half, dst):
+        def make_part(u, half, dst, acc=None):
             part[u, half] = dst
             nc.vector.scalar_tensor_tensor(
-                out=part[u, half], in0=s[u, half], scalar=-1.0, in1=h_bank(u, half)[:], op0=ADD, op1=MULT
+                out=part[u, half], in0=s[u, half], scalar=-1.0, in1=(acc or h_bank(u, half))[:], op0=ADD, op1=MULT
             )
 
         def finish_part(u, half):
@@ -218,7 +238,7 @@ def tile_list_botnet_gated_gradients_kernel(
 
         nc.sync.dma_start(idx[:], offs)
         nc.sync.dma_start(idx2[:], offs2)
-        load_s(0, pieces=2, spare=4 * HB)
+        load_s(0, pieces=2, spare=24 * HB)
         load_table(0, pieces=2)
         load_w1(0, 0, rows_of_word=(slice(0, 1), slice(1, 2)))
         load_scale_rows(tab_sc, tab_scales)
@@ -227,12 +247,12 @@ def tile_list_botnet_gated_gradients_kernel(
         load_w1(1, 0)
         load_s(1)
         load_s(2)
-        load_w1(0, 1, spare=EDGE)
-        load_s(3, spare=10 * HB)
+        load_w1(0, 1)
+        load_s(3)
         planes[0, 0] = held([P, PACK, HALF], BF16, "planes00")[:]
-        area0 = held([P, 3 * HALF + 2 * W], BF16, "area0")
-        planes[0, 1] = area0[:, :W].rearrange("p (i c) -> p i c", i=PACK)
-        w1_second = area0[:, 3 * HALF :]
+        planes[0, 1] = held([P, PACK, HALF], BF16, "planes01")[:]
+        area0 = held([P, 5 * HALF], F32, "area0")
+        w1_second = area0[:, : 4 * HALF].bitcast(BF16)
 
         gather_s(0)
         load_w1(1, 1, follows="s_win0", at=EDGE)
@@ -243,104 +263,104 @@ def tile_list_botnet_gated_gradients_kernel(
         load_s(4, follows="tab_w0")
         for a in range(PASSES):
             gather_scales(a)
-        w1_00 = held([P, T], F32, "w1_00")[:, : W // 2].bitcast(BF16)
-        round_w1(0, 0, w1_00)
+        w1_00 = held([P, W], BF16, "w1_00")
+        round_w1(0, 0, w1_00[:])
         load_s(5, follows="raw_w1_00")
-        (w1_q[0, 0],) = quantize_pieces("w1_00", w1_00)
-        clear_page(PAGES - 1, follows="w1_00")
+        (w1_q[0, 0],) = quantize_pieces("w1_00", w1_00[:])
         gather_table(1)
         load_s(6, follows="tab_w1")
         w1_10 = held([P, W], BF16, "w1_10")
         round_w1(1, 0, w1_10[:])
-        load_s(7, follows="raw_w1_10")
-        gather_s(1)
-        (w1_q[1, 0],) = quantize_pieces("w1_10", w1_10[:], follows="s_win1")
-        less_one(1, 0, half_tile("slope10"))
-        make_slope(1, 0)
+        (w1_q[1, 0],) = quantize_pieces("w1_10", w1_10[:])
         for half in range(2):
-            copy_h(0, half, half_tile("h_sb0%d" % half, "s0", half * HB))
-            d_on_gpsimd(0, half)
-        copy_h(1, 0, half_tile("h_sb10", "s_win1", HB))
-        d_on_gpsimd(1, 0)
-        gather_s(2)
-        round_w1(0, 1, w1_second[:, :W])
-        for b in range(PASSES):
-            load_wg(0, b, held([P, PACK, NH], F32, "raw_wg0%d" % b, "raw_w1_01", EDGE + 2 * b * HB)[:])
-        make_part(2, 0, half_tile("part20", "s_win2"))
-        make_part(1, 1, half_tile("part11", "s_win2", HB))
-        finish_part(2, 0)
-        gather_s(3)
-        STEP = 5 * HALF
-        area1 = held([P, PACK * STEP], BF16, "area1", follows="s_win3", at=4 * HB - EDGE)
-        planes[1, 1] = area1[:].rearrange("p (i c) -> p i c", i=PACK)[:, :, :HALF]
-        d10_at = STEP + HALF - 32
-        WG1_AT = 2 * STEP + HALF - 64
-        d10_grouped = area1[:, d10_at : d10_at + W]
-        load_wg(1, 0, d10_grouped.bitcast(F32).rearrange("p (i c) -> p i c", i=PACK))
-        load_wg(1, 1, held([P, PACK, NH], F32, "raw_wg11", "s_win3")[:])
-        load_scale_rows(wv_sc, wv_scales)
-        make_part(2, 1, half_tile("part21", "s_win2", 2 * HB))
-        make_part(3, 0, half_tile("part30", "s_win2", 3 * HB))
-        make_part(3, 1, half_tile("part31", "s_win1", 2 * HB))
+            gather_s_half(1, half, half_tile("s1%d" % half, "raw_w1_10", half * HB))
+        load_s(7, follows="s_win1")
+        copy_h(0, 0, half_tile("h_sb00", "s0"))
+        d_on_gpsimd(0, 0)
+        make_part(1, 0, half_tile("part10", "w1_00"))
+        copy_h(0, 1, half_tile("h_sb01", "s0", HB))
+        d_on_gpsimd(0, 1)
+        finish_part(1, 0)
+        gather_s_half(2, 0, half_tile("s20"))
+        make_part(1, 1, half_tile("part11", "w1_00", HB))
         finish_part(1, 1)
-        finish_part(3, 0)
-        finish_part(2, 1)
+        gather_s_half(2, 1, half_tile("s21"))
+        round_w1(0, 1, w1_second[:, :W])
+        for half in range(2):
+            make_part(2, half, half_tile("part2%d" % half, "w1_10", half * HB))
+            finish_part(2, half)
+        for half in range(2):
+            gather_s_half(3, half, half_tile("s3%d" % half))
+        for half in range(2):
+            make_part(3, half, half_tile("part3%d" % half, "raw_w1_10", (2 + half) * HB))
+            finish_part(3, half)
         round_w1(1, 1, w1_second[:, W:])
-        wv_w = held([P, PASSES, N], U32, "wv_w", follows="raw_w1_11", at=-EDGE)
+        area1 = held([P, 24 * HALF], F32, "area1", "s_win0", 4 * HB)
+        for k, first in ((0, 3), (1, 20)):
+            for b in range(PASSES):
+                load_wg(k, b, area1[:, (first - 2 * b) * HALF : (first + 2 - 2 * b) * HALF].rearrange("p (i c) -> p i c", i=PACK))
+        early = held([P, 2 * W], BF16, "early", "s_win0")[:]
+        d00_grouped, wg0_grouped = early[:, :W], early[:, W:]
+        d10_grouped = area1[:, 5 * HALF : 7 * HALF].bitcast(BF16)
+        second = area1[:, 7 * HALF : 11 * HALF].bitcast(BF16)
+        wg1_grouped = area1[:, 11 * HALF - EDGE // 4 : 13 * HALF - EDGE // 4].bitcast(BF16)
+        s67b, part67b = two(area1, 4 * HALF, 7 * HALF), two(area1, 12 * HALF, HALF)
+        lhs45, rhs45 = two(held([P, S], F32, "lhs45", "s_win2", 2 * HB), 0, HALF), two(area0, 3 * HALF, HALF)
+        s67, part67 = two(held([P, S], F32, "s67", "s_win3"), 0, HALF), two(held([P, S], F32, "part67", "s_win3", 2 * HB), 0, HALF)
+        lhs45b, rhs45b = two(held([P, S], F32, "lhs45b", "w1_00"), 0, HALF), two(area1, 0, 3 * HALF)
+
+        def finish_pair(dst, first, parts, values):
+            nc.gpsimd.tensor_tensor(grouped_view(dst, first, 2, LINE), runs(parts), runs(values), MULT)
+
+        for half in range(2):
+            gather_s_half(4, half, half_tile("s4%d" % half, "s_win2", half * HB))
+        load_scale_rows(wv_sc, wv_scales)
+        wv_w = held([P, PASSES, N], U32, "wv_w", follows="s_win4", at=2 * HB)
         nc.sync.dma_start(out=wv_w[:].bitcast(I32), in_=wv_words.rearrange("b p c i -> p b (c i)").bitcast(I32))
-        wgo_sb = held([P, S], F32, "wgo_sb", follows="raw_w1_11", at=2 * HB - EDGE)
-        nc.sync.dma_start(out=wgo_sb[:], in_=wgo)
-        early = held([P, 2 * W], BF16, "early", follows="s_win0", at=4 * HB)[:]
-        group(early[:, :W], planes[0, 0])
-        gather_s(4)
+        wgo_sb = area1[:, 22 * HALF :]
+        nc.sync.dma_start(out=wgo_sb, in_=wgo)
         w1_q[0, 1], w1_q[1, 1] = quantize_pieces("w1_1", w1_second, follows="s_win4")
-        finish_part(3, 1)
-        planes[1, 0] = held([P, PACK, HALF], BF16, "planes10", follows="w1_10")[:]
-        rest41 = half_tile("rest41", "part11")
-        less_one(4, 1, rest41)
-        slope[4, 1] = w1_second[:, W : W + 2 * HALF].bitcast(F32)
-        nc.gpsimd.tensor_tensor(slope[4, 1], s[4, 1], rest41, MULT)
-        second = held([P, 2 * W], BF16, "second")
+        less_one(4, 0, half_tile("rest40", "slope00"))
+        group(d00_grouped, planes[0, 0])
+        less_one(4, 1, half_tile("rest41", "slope01"))
+        make_slope(4, 0, rhs45[:, 0])
+        make_slope(4, 1, rhs45b[:, 0])
+        gather_s_half(5, 0, rhs45[:, 1])
+        make_part(5, 0, lhs45[:, 1])
         group(second[:, :W], planes[0, 1])
-        gather_s_half(5, 0, half_tile("s50"))
-        for u in (4, 5):
-            make_part(u, 0, half_tile("part%d0" % u, "slope0%d" % (u - 4)))
-            finish_part(u, 0)
-        copy_h(4, 1, half_tile("h_sb41", "s_win4", 2 * HB))
-        gather_s_half(6, 0, half_tile("s60"))
-        make_part(6, 0, half_tile("part60", "slope10"))
-        finish_part(6, 0)
-        gather_s_half(7, 0, half_tile("s70"))
-        make_part(7, 0, area1[:, : 2 * HALF].bitcast(F32))
-        finish_part(7, 0)
-        d_on_gpsimd(4, 1)
+        copy_h(4, 0, lhs45[:, 0])
+        finish_pair(d10_grouped, 0, lhs45, rhs45)
+        gather_s_half(6, 0, s67[:, 0])
+        make_part(6, 0, part67[:, 0])
+        copy_h(4, 1, lhs45b[:, 0])
+        gather_s_half(7, 0, s67[:, 1])
+        make_part(7, 0, part67[:, 1])
+        finish_pair(d10_grouped, 2, part67, s67)
         for b in range(PASSES):
-            round_wg(0, b, early[:, W:])
-        wg1_grouped = area1[:, WG1_AT : WG1_AT + W]
-        round_wg(1, 0, wg1_grouped)
-        group(d10_grouped, planes[1, 0])
-        round_wg(1, 1, wg1_grouped)
-        gather_s_half(5, 1, half_tile("s51", "raw_wg00", -EDGE))
-        gather_s_half(6, 1, half_tile("s61", "raw_wg00", HB - EDGE))
-        make_part(5, 1, half_tile("part51", "s_win1", 3 * HB))
-        make_part(6, 1, half_tile("part61", "part20"))
-        d_q[0, 0], wg_q[0] = quantize_pieces("early", early)
-        (d_q[1, 0],) = quantize_pieces("d10", d10_grouped)
-        finish_part(5, 1)
-        gather_s_half(7, 1, area1[:, STEP + HALF : STEP + 3 * HALF].bitcast(F32))
-        (wg_q[1],) = quantize_pieces("wg1", wg1_grouped, follows="s_win7")
+            round_wg(0, b, wg0_grouped)
+        for b in range(PASSES):
+            round_wg(1, b, wg1_grouped)
+        gather_s_half(5, 1, rhs45b[:, 1])
+        gather_s_half(6, 1, s67b[:, 0])
+        make_part(5, 1, lhs45b[:, 1])
+        h61, h71 = h_bank(6, 1), h_bank(7, 1)
+        d_q[0, 0], wg_q[0] = quantize_pieces("early", early, follows="s_win6", scales_follow="s67")
+        (d_q[1, 0],) = quantize_pieces("d10", d10_grouped, follows="s_win6", at=2 * HB)
+        (wg_q[1],) = quantize_pieces("wg1", wg1_grouped)
+        finish_pair(second[:, W:], 0, lhs45b, rhs45b)
+        make_part(6, 1, part67b[:, 0], h61)
 
         def product(name, half, lhsT, lhsT_scale):
             acc = bank(name)
-            for b in reversed(range(PASSES)):
+            for b in range(PASSES):
                 nc.tensor.matmul_mx(
                     out=acc[:],
                     lhsT=lhsT[b].bitcast(E4M3),
                     lhsT_scale=lhsT_scale[b],
                     rhs=d_q[b, half][0].bitcast(E4M3),
                     rhs_scale=d_q[b, half][1],
-                    start=(b == PASSES - 1),
-                    stop=(b == 0),
+                    start=(b == 0),
+                    stop=(b == PASSES - 1),
                 )
             return acc
 
@@ -382,37 +402,42 @@ def tile_list_botnet_gated_gradients_kernel(
             if half == 1:
                 nc.sync.dma_start(out=out[c * P : (c + 1) * P, :], in_=page[c][:])
 
-        sig00 = half_tile("sig00", "early")
-        sigmoid_of_gate(0, 0, sig00)
-        val_wgo = area1[:, 3 * STEP - 3 * HALF // 2 : 3 * STEP + HALF // 2].bitcast(F32)
-        nc.vector.scalar_tensor_tensor(
-            out=val_wgo, in0=val_bank(0, 0)[:], scalar=-1.0, in1=halves(wgo_sb)[0], op0=MULT, op1=MULT
-        )
-        finish_part(6, 1)
-        make_part(7, 1, area1[:, 2 * STEP + HALF : 2 * STEP + 3 * HALF].bitcast(F32))
-        ys = [half_tile("y%d" % c, "s_win6", c * HB) for c in range(2)]
-        y[0, 0] = ys[0]
-        nc.vector.tensor_tensor(y[0, 0], val_wgo, sig00, MULT)
-        make_weight(0, 1, area1[:, 3 * STEP + HALF // 2 : 3 * STEP + 5 * HALF // 2].bitcast(F32), half_tile("weight01", "sig00"))
-        finish_part(7, 1)
-        y_on_gpsimd(0, 1, ys[1], ys[1])
+        weights = area1[:, 14 * HALF : 18 * HALF]
+        sigs = {c: half_tile("sig0%d" % c, "s_win5", c * HB) for c in range(1, PAGES)}
+        sigs[0] = part67b[:, 1]
+        ys = [half_tile("y%d" % c, "raw_w1_10", c * HB) for c in range(PAGES)]
+
+        def weigh_val(c, acc):
+            weight[0, c] = weights[:, c * HALF : (c + 1) * HALF]
+            nc.vector.scalar_tensor_tensor(
+                out=weight[0, c], in0=acc[:], scalar=-1.0, in1=sigs[c], op0=MULT, op1=MULT
+            )
+
+        def gate_val(c):
+            y[0, c] = ys[c]
+            nc.gpsimd.tensor_tensor(ys[c], weight[0, c], halves(wgo_sb)[0], MULT)
+
+        sigmoid_of_gate(0, 0, sigs[0])
+        weigh_val(0, val_bank(0, 0))
+        gather_s_half(7, 1, s67b[:, 1])
+        sigmoid_of_gate(0, 1, sigs[1])
+        weigh_val(1, val_bank(0, 1))
+        make_part(7, 1, part67b[:, 1], h71)
+        gate_val(0)
+        gate_val(1)
+        make_weight(0, 2, sigs[2], weights[:, 2 * HALF : 3 * HALF])
+        finish_pair(second[:, W:], 2, part67b, s67b)
+        y_on_gpsimd(0, 2, ys[2], ys[2])
         scatter(0, 0)
-        sig02 = half_tile("sig02", "s_win5", HB)
-        sigmoid_of_gate(0, 2, sig02)
-        weigh(0, 2, sig02, half_tile("weight02", "weight01"))
-        y_on_gpsimd(0, 2, half_tile("val02", "s_win6", 2 * HB), area1[:, : 2 * HALF].bitcast(F32), lambda: group(second[:, W:], planes[1, 1]))
         scatter(0, 1)
-        d_q[0, 1], d_q[1, 1] = quantize_pieces("d1", second[:], follows="y0")
-        make_weight(0, 3, half_tile("sig03", "s_win5", 2 * HB), half_tile("weight03", "second"))
-        y03 = half_tile("y03", "s_win6", 3 * HB)
-        y_on_gpsimd(0, 3, y03, y03)
+        d_q[0, 1], d_q[1, 1] = quantize_pieces("d1", second, follows="y0")
+        make_weight(0, 3, sigs[3], area1[:, 7 * HALF : 8 * HALF])
+        y_on_gpsimd(0, 3, ys[3], ys[3])
         scatter(0, 2)
         scatter(0, 3)
-        before = "weight03"
         for c in range(PAGES):
-            sig_c = half_tile("sig1%d" % c, "s_win4", c * HB)
-            make_weight(1, c, sig_c, half_tile("weight1%d" % c, before))
-            before = "weight1%d" % c
-            y_c = half_tile("y1%d" % c, "s_win1", c * HB)
+            sig_c = half_tile("sig1%d" % c, "s_win7", c * HB)
+            make_weight(1, c, sig_c, half_tile("weight1%d" % c, "early", c * HB))
+            y_c = half_tile("y1%d" % c, "area0", c * HB)
             y_on_gpsimd(1, c, y_c, y_c)
             scatter(1, c)

@@ -204,9 +204,9 @@ def tile_list_botnet_gated_gradients_kernel(
                 slope[u, half] = dst
             nc.gpsimd.tensor_tensor(slope[u, half], s[u, half], rest, MULT)
 
-        def copy_h(u, half, dst):
+        def copy_h(u, half, dst, acc=None):
             part[u, half] = dst
-            nc.scalar.copy(out=part[u, half], in_=h_bank(u, half)[:])
+            nc.scalar.copy(out=part[u, half], in_=(acc or h_bank(u, half))[:])
 
         def d_on_gpsimd(u, half):
             nc.gpsimd.tensor_tensor(plane(u, half), part[u, half], slope[u, half], MULT)
@@ -304,10 +304,10 @@ def tile_list_botnet_gated_gradients_kernel(
         d10_grouped = area1[:, 5 * HALF : 7 * HALF].bitcast(BF16)
         second = area1[:, 7 * HALF : 11 * HALF].bitcast(BF16)
         wg1_grouped = area1[:, 11 * HALF - EDGE // 4 : 13 * HALF - EDGE // 4].bitcast(BF16)
-        s67b, part67b = two(area1, 4 * HALF, 7 * HALF), two(area1, 12 * HALF, HALF)
+        s67b, part67b = two(area1, 3 * HALF, HALF), two(held([P, S], F32, "part67b", "w1_00"), 0, HALF)
         lhs45, rhs45 = two(held([P, S], F32, "lhs45", "s_win2", 2 * HB), 0, HALF), two(area0, 3 * HALF, HALF)
         s67, part67 = two(held([P, S], F32, "s67", "s_win3"), 0, HALF), two(held([P, S], F32, "part67", "s_win3", 2 * HB), 0, HALF)
-        lhs45b, rhs45b = two(held([P, S], F32, "lhs45b", "w1_00"), 0, HALF), two(area1, 0, 3 * HALF)
+        lhs45b, rhs45b = two(area1, 13 * HALF, HALF), two(area1, 0, 11 * HALF)
 
         def finish_pair(dst, first, parts, values):
             nc.gpsimd.tensor_tensor(grouped_view(dst, first, 2, LINE), runs(parts), runs(values), MULT)
@@ -332,7 +332,7 @@ def tile_list_botnet_gated_gradients_kernel(
         finish_pair(d10_grouped, 0, lhs45, rhs45)
         gather_s_half(6, 0, s67[:, 0])
         make_part(6, 0, part67[:, 0])
-        copy_h(4, 1, lhs45b[:, 0])
+        h41 = h_bank(4, 1)
         gather_s_half(7, 0, s67[:, 1])
         make_part(7, 0, part67[:, 1])
         finish_pair(d10_grouped, 2, part67, s67)
@@ -340,19 +340,25 @@ def tile_list_botnet_gated_gradients_kernel(
             round_wg(0, b, wg0_grouped)
         for b in range(PASSES):
             round_wg(1, b, wg1_grouped)
-        gather_s_half(5, 1, rhs45b[:, 1])
-        gather_s_half(6, 1, s67b[:, 0])
-        make_part(5, 1, lhs45b[:, 1])
-        h61, h71 = h_bank(6, 1), h_bank(7, 1)
-        d_q[0, 0], wg_q[0] = quantize_pieces("early", early, follows="s_win6", scales_follow="s67")
-        (d_q[1, 0],) = quantize_pieces("d10", d10_grouped, follows="s_win6", at=2 * HB)
+        for u in (6, 7):
+            gather_s_half(u, 1, s67b[:, u - 6])
+        for u in (6, 7):
+            make_part(u, 1, part67b[:, u - 6])
+        h51 = h_bank(5, 1)
+        d_q[0, 0], wg_q[0] = quantize_pieces("early", early, follows="s_win7", scales_follow="s67")
+        (d_q[1, 0],) = quantize_pieces("d10", d10_grouped, follows="s_win7", at=2 * HB)
         (wg_q[1],) = quantize_pieces("wg1", wg1_grouped)
-        finish_pair(second[:, W:], 0, lhs45b, rhs45b)
-        make_part(6, 1, part67b[:, 0], h61)
+        finish_pair(second[:, W:], 2, part67b, s67b)
+        gather_s_half(5, 1, rhs45b[:, 1])
 
-        def product(name, half, lhsT, lhsT_scale):
-            acc = bank(name)
-            for b in range(PASSES):
+        accs = {}
+        BANK_AFTER = {"val01": "h61", "gate02": "h71", "val02": "h70", "gate03": "gate00", "val03": "val00"}
+
+        def product(name, half, lhsT, lhsT_scale, passes):
+            if name not in accs:
+                accs[name] = bank(name, BANK_AFTER.get(name))
+            acc = accs[name]
+            for b in passes:
                 nc.tensor.matmul_mx(
                     out=acc[:],
                     lhsT=lhsT[b].bitcast(E4M3),
@@ -366,11 +372,13 @@ def tile_list_botnet_gated_gradients_kernel(
 
         weight, y = {}, {}
 
-        def sigmoid_of_gate(half, c, sig):
+        def gate_bank(half, c, passes=range(PASSES)):
             k, first = divmod(c * P, NH)
             words = [slice(b * NH + first, b * NH + first + P) for b in range(PASSES)]
-            gate = product("gate%d%d" % (half, c), half, [wg_q[k][0][:, w] for w in words], [wg_q[k][1][:, w] for w in words])
-            nc.scalar.activation(out=sig, in_=gate[:], func=SIGMOID, scale=-1.0)
+            return product("gate%d%d" % (half, c), half, [wg_q[k][0][:, w] for w in words], [wg_q[k][1][:, w] for w in words], passes)
+
+        def sigmoid_of_gate(half, c, sig, passes=range(PASSES)):
+            nc.scalar.activation(out=sig, in_=gate_bank(half, c, passes)[:], func=SIGMOID, scale=-1.0)
 
         def weigh(half, c, sig, dst):
             weight[half, c] = dst
@@ -380,9 +388,9 @@ def tile_list_botnet_gated_gradients_kernel(
             sigmoid_of_gate(half, c, sig)
             weigh(half, c, sig, dst)
 
-        def val_bank(half, c):
+        def val_bank(half, c, passes=range(PASSES)):
             words = [wv_w[:, b, c * P : (c + 1) * P] for b in range(PASSES)]
-            return product("val%d%d" % (half, c), half, words, [wv_sc[:, b * N + c * P : b * N + (c + 1) * P] for b in range(PASSES)])
+            return product("val%d%d" % (half, c), half, words, [wv_sc[:, b * N + c * P : b * N + (c + 1) * P] for b in range(PASSES)], passes)
 
         def y_on_gpsimd(half, c, val, dst, between=None):
             y[half, c] = dst
@@ -391,10 +399,10 @@ def tile_list_botnet_gated_gradients_kernel(
                 between()
             nc.gpsimd.tensor_tensor(dst, val, weight[half, c], MULT)
 
-        def y_on_vector(half, c, dst):
+        def y_on_vector(half, c, dst, acc):
             y[half, c] = dst
             nc.vector.scalar_tensor_tensor(
-                out=y[half, c], in0=val_bank(half, c)[:], scalar=-1.0, in1=weight[half, c], op0=MULT, op1=MULT
+                out=y[half, c], in0=acc[:], scalar=-1.0, in1=weight[half, c], op0=MULT, op1=MULT
             )
 
         def scatter(half, c):
@@ -402,41 +410,40 @@ def tile_list_botnet_gated_gradients_kernel(
             if half == 1:
                 nc.sync.dma_start(out=out[c * P : (c + 1) * P, :], in_=page[c][:])
 
-        weights = area1[:, 14 * HALF : 18 * HALF]
-        sigs = {c: half_tile("sig0%d" % c, "s_win5", c * HB) for c in range(1, PAGES)}
-        sigs[0] = part67b[:, 1]
-        ys = [half_tile("y%d" % c, "raw_w1_10", c * HB) for c in range(PAGES)]
+        sigs = {c: half_tile("sig0%d" % c, "s_win6", c * HB) for c in range(PAGES)}
+        gated = [area1[:, 17 * HALF : 18 * HALF], lhs45b[:, 0]]
 
-        def weigh_val(c, acc):
-            weight[0, c] = weights[:, c * HALF : (c + 1) * HALF]
+        def gate_val(c, passes):
+            sigmoid_of_gate(0, c, sigs[c], passes)
             nc.vector.scalar_tensor_tensor(
-                out=weight[0, c], in0=acc[:], scalar=-1.0, in1=sigs[c], op0=MULT, op1=MULT
+                out=gated[c], in0=val_bank(0, c, passes)[:], scalar=-1.0, in1=sigs[c], op0=MULT, op1=MULT
             )
 
-        def gate_val(c):
-            y[0, c] = ys[c]
-            nc.gpsimd.tensor_tensor(ys[c], weight[0, c], halves(wgo_sb)[0], MULT)
+        def weigh_gated(c, dst):
+            y[0, c] = dst
+            nc.gpsimd.tensor_tensor(dst, gated[c], halves(wgo_sb)[0], MULT)
 
-        sigmoid_of_gate(0, 0, sigs[0])
-        weigh_val(0, val_bank(0, 0))
-        gather_s_half(7, 1, s67b[:, 1])
-        sigmoid_of_gate(0, 1, sigs[1])
-        weigh_val(1, val_bank(0, 1))
-        make_part(7, 1, part67b[:, 1], h71)
-        gate_val(0)
-        gate_val(1)
-        make_weight(0, 2, sigs[2], weights[:, 2 * HALF : 3 * HALF])
-        finish_pair(second[:, W:], 2, part67b, s67b)
-        y_on_gpsimd(0, 2, ys[2], ys[2])
+        gate_bank(0, 0, [0])
+        val_bank(0, 0, [0])
+        gate_val(0, [1])
+        make_part(5, 1, lhs45b[:, 1], h51)
+        gate_val(1, range(PASSES))
+        weigh_gated(0, area1[:, 15 * HALF : 16 * HALF])
+        weigh_gated(1, half_tile("y1", "raw_w1_01"))
+        make_weight(0, 2, sigs[2], area1[:, 17 * HALF : 18 * HALF])
+        copy_h(4, 1, lhs45b[:, 0], h41)
+        finish_pair(second[:, W:], 0, lhs45b, rhs45b)
+        y_on_gpsimd(0, 2, half_tile("val02", "raw_w1_10"), lhs45b[:, 0])
         scatter(0, 0)
         scatter(0, 1)
-        d_q[0, 1], d_q[1, 1] = quantize_pieces("d1", second, follows="y0")
+        d_q[0, 1], d_q[1, 1] = quantize_pieces("d1", second, follows="s_win5")
         make_weight(0, 3, sigs[3], area1[:, 7 * HALF : 8 * HALF])
-        y_on_gpsimd(0, 3, ys[3], ys[3])
+        y3 = half_tile("y3", "raw_w1_10", HB)
+        y_on_gpsimd(0, 3, y3, y3)
         scatter(0, 2)
         scatter(0, 3)
         for c in range(PAGES):
-            sig_c = half_tile("sig1%d" % c, "s_win7", c * HB)
+            sig_c = half_tile("sig1%d" % c, "s_win6", c * HB)
             make_weight(1, c, sig_c, half_tile("weight1%d" % c, "early", c * HB))
             y_c = half_tile("y1%d" % c, "area0", c * HB)
             y_on_gpsimd(1, c, y_c, y_c)

@@ -211,8 +211,8 @@ def tile_list_botnet_gated_gradients_kernel(
         def d_on_gpsimd(u, half):
             nc.gpsimd.tensor_tensor(plane(u, half), part[u, half], slope[u, half], MULT)
 
-        def d_on_vector(u, half):
-            nc.vector.tensor_tensor(plane(u, half), h_bank(u, half)[:], slope[u, half], MULT)
+        def d_on_vector(u, half, acc):
+            nc.vector.tensor_tensor(plane(u, half), acc[:], slope[u, half], MULT)
 
         def make_part(u, half, dst, acc=None):
             part[u, half] = dst
@@ -303,17 +303,17 @@ def tile_list_botnet_gated_gradients_kernel(
         d00_grouped, wg0_grouped = early[:, :W], early[:, W:]
         d10_grouped = area1[:, 5 * HALF : 7 * HALF].bitcast(BF16)
         second = area1[:, 7 * HALF : 11 * HALF].bitcast(BF16)
-        wg1_grouped = area1[:, 11 * HALF - EDGE // 4 : 13 * HALF - EDGE // 4].bitcast(BF16)
+        wg1_grouped = area1[:, 14 * HALF : 16 * HALF].bitcast(BF16)
+        late = area1[:, 11 * HALF : 17 * HALF].bitcast(BF16).rearrange("p (i c) -> p i c", i=PACK)[:, :, :HALF]
         s67b, part67b = two(area1, 3 * HALF, HALF), two(held([P, S], F32, "part67b", "w1_00"), 0, HALF)
         lhs45, rhs45 = two(held([P, S], F32, "lhs45", "s_win2", 2 * HB), 0, HALF), two(area0, 3 * HALF, HALF)
         s67, part67 = two(held([P, S], F32, "s67", "s_win3"), 0, HALF), two(held([P, S], F32, "part67", "s_win3", 2 * HB), 0, HALF)
-        lhs45b, rhs45b = two(area1, 13 * HALF, HALF), two(area1, 0, 11 * HALF)
 
         def finish_pair(dst, first, parts, values):
             nc.gpsimd.tensor_tensor(grouped_view(dst, first, 2, LINE), runs(parts), runs(values), MULT)
 
-        for half in range(2):
-            gather_s_half(4, half, half_tile("s4%d" % half, "s_win2", half * HB))
+        gather_s_half(4, 0, half_tile("s40", "s_win2"))
+        gather_s_half(4, 1, area1[:, 8 * HALF : 9 * HALF])
         load_scale_rows(wv_sc, wv_scales)
         wv_w = held([P, PASSES, N], U32, "wv_w", follows="s_win4", at=2 * HB)
         nc.sync.dma_start(out=wv_w[:].bitcast(I32), in_=wv_words.rearrange("b p c i -> p b (c i)").bitcast(I32))
@@ -324,11 +324,12 @@ def tile_list_botnet_gated_gradients_kernel(
         group(d00_grouped, planes[0, 0])
         less_one(4, 1, half_tile("rest41", "slope01"))
         make_slope(4, 0, rhs45[:, 0])
-        make_slope(4, 1, rhs45b[:, 0])
+        make_slope(4, 1, area1[:, :HALF])
         gather_s_half(5, 0, rhs45[:, 1])
         make_part(5, 0, lhs45[:, 1])
-        group(second[:, :W], planes[0, 1])
+        group(second[:, : W // 2], planes[0, 1][:, :, : HALF // 2])
         copy_h(4, 0, lhs45[:, 0])
+        group(second[:, W // 2 : W], planes[0, 1][:, :, HALF // 2 :])
         finish_pair(d10_grouped, 0, lhs45, rhs45)
         gather_s_half(6, 0, s67[:, 0])
         make_part(6, 0, part67[:, 0])
@@ -348,8 +349,10 @@ def tile_list_botnet_gated_gradients_kernel(
         d_q[0, 0], wg_q[0] = quantize_pieces("early", early, follows="s_win7", scales_follow="s67")
         (d_q[1, 0],) = quantize_pieces("d10", d10_grouped, follows="s_win7", at=2 * HB)
         (wg_q[1],) = quantize_pieces("wg1", wg1_grouped)
-        finish_pair(second[:, W:], 2, part67b, s67b)
-        gather_s_half(5, 1, rhs45b[:, 1])
+        planes[1, 1] = late
+        for u in (6, 7):
+            finish_part(u, 1)
+        gather_s_half(5, 1, area1[:, 29 * HALF // 2 : 31 * HALF // 2])
 
         accs = {}
         BANK_AFTER = {"val01": "h61", "gate02": "h71", "val02": "h70", "gate03": "gate00", "val03": "val00"}
@@ -410,8 +413,9 @@ def tile_list_botnet_gated_gradients_kernel(
             if half == 1:
                 nc.sync.dma_start(out=out[c * P : (c + 1) * P, :], in_=page[c][:])
 
-        sigs = {c: half_tile("sig0%d" % c, "s_win6", c * HB) for c in range(PAGES)}
-        gated = [area1[:, 17 * HALF : 18 * HALF], lhs45b[:, 0]]
+        sigs = {c: half_tile("sig0%d" % c, "s_win6", c * HB) for c in range(1, PAGES)}
+        sigs[0] = area1[:, 21 * HALF // 2 : 23 * HALF // 2]
+        gated = [area1[:, 12 * HALF : 13 * HALF], area1[:, 13 * HALF : 14 * HALF]]
 
         def gate_val(c, passes):
             sigmoid_of_gate(0, c, sigs[c], passes)
@@ -426,14 +430,16 @@ def tile_list_botnet_gated_gradients_kernel(
         gate_bank(0, 0, [0])
         val_bank(0, 0, [0])
         gate_val(0, [1])
-        make_part(5, 1, lhs45b[:, 1], h51)
+        make_part(5, 1, half_tile("part51", "planes00"), h51)
         gate_val(1, range(PASSES))
-        weigh_gated(0, area1[:, 15 * HALF : 16 * HALF])
+        d_on_vector(4, 1, h41)
+        weigh_gated(0, area1[:, 17 * HALF : 18 * HALF])
+        finish_part(5, 1)
         weigh_gated(1, half_tile("y1", "raw_w1_01"))
-        make_weight(0, 2, sigs[2], area1[:, 17 * HALF : 18 * HALF])
-        copy_h(4, 1, lhs45b[:, 0], h41)
-        finish_pair(second[:, W:], 0, lhs45b, rhs45b)
-        y_on_gpsimd(0, 2, half_tile("val02", "raw_w1_10"), lhs45b[:, 0])
+        make_weight(0, 2, sigs[2], area1[:, 23 * HALF // 2 : 25 * HALF // 2])
+        y_on_gpsimd(
+            0, 2, half_tile("val02", "raw_w1_10"), area1[:, 31 * HALF // 2 : 33 * HALF // 2], lambda: group(second[:, W:], late)
+        )
         scatter(0, 0)
         scatter(0, 1)
         d_q[0, 1], d_q[1, 1] = quantize_pieces("d1", second, follows="s_win5")

@@ -355,7 +355,7 @@ def tile_list_botnet_gated_gradients_kernel(
         gather_s_half(5, 1, area1[:, 29 * HALF // 2 : 31 * HALF // 2])
 
         accs = {}
-        BANK_AFTER = {"val01": "h61", "gate02": "h71", "val02": "h70", "gate03": "gate00", "val03": "val00"}
+        BANK_AFTER = {"val01": "h61", "gate02": "h71", "val02": "h70", "gate03": "gate00", "val03": "val00", "gate10": "h41", "val10": "h51"}
 
         def product(name, half, lhsT, lhsT_scale, passes):
             if name not in accs:
@@ -430,13 +430,13 @@ def tile_list_botnet_gated_gradients_kernel(
         gate_bank(0, 0, [0])
         val_bank(0, 0, [0])
         gate_val(0, [1])
-        make_part(5, 1, half_tile("part51", "planes00"), h51)
+        make_part(5, 1, area1[:, 3 * HALF // 2 : 5 * HALF // 2], h51)
         gate_val(1, range(PASSES))
         d_on_vector(4, 1, h41)
         weigh_gated(0, area1[:, 17 * HALF : 18 * HALF])
         finish_part(5, 1)
-        weigh_gated(1, half_tile("y1", "raw_w1_01"))
-        make_weight(0, 2, sigs[2], area1[:, 23 * HALF // 2 : 25 * HALF // 2])
+        weigh_gated(1, area1[:, HALF : 2 * HALF])
+        make_weight(0, 2, sigs[2], area1[:, 2 * HALF : 3 * HALF])
         y_on_gpsimd(
             0, 2, half_tile("val02", "raw_w1_10"), area1[:, 31 * HALF // 2 : 33 * HALF // 2], lambda: group(second[:, W:], late)
         )

@@ -437,11 +437,11 @@ def tile_list_botnet_gated_gradients_kernel(
         finish_part(5, 1)
         weigh_gated(1, area1[:, HALF : 2 * HALF])
         make_weight(0, 2, sigs[2], area1[:, 2 * HALF : 3 * HALF])
-        y_on_gpsimd(
-            0, 2, half_tile("val02", "raw_w1_10"), area1[:, 31 * HALF // 2 : 33 * HALF // 2], lambda: group(second[:, W:], late)
-        )
+        val02 = val_bank(0, 2)
+        group(second[:, W:], late)
         scatter(0, 0)
         scatter(0, 1)
+        y_on_vector(0, 2, area1[:, 31 * HALF // 2 : 33 * HALF // 2], val02)
         d_q[0, 1], d_q[1, 1] = quantize_pieces("d1", second, follows="s_win5")
         make_weight(0, 3, sigs[3], area1[:, 7 * HALF : 8 * HALF])
         y3 = half_tile("y3", "raw_w1_10", HB)
@@ -450,7 +450,14 @@ def tile_list_botnet_gated_gradients_kernel(
         scatter(0, 3)
         for c in range(PAGES):
             sig_c = half_tile("sig1%d" % c, "s_win6", c * HB)
-            make_weight(1, c, sig_c, half_tile("weight1%d" % c, "early", c * HB))
             y_c = half_tile("y1%d" % c, "area0", c * HB)
-            y_on_gpsimd(1, c, y_c, y_c)
-            scatter(1, c)
+            if c < PAGES - 1:
+                make_weight(1, c, sig_c, half_tile("weight1%d" % c, "early", c * HB))
+                y_on_gpsimd(1, c, y_c, y_c)
+                scatter(1, c)
+            else:
+                sigmoid_of_gate(1, c, sig_c)
+                weight[1, c] = sig_c
+                y_on_gpsimd(1, c, y_c, half_tile("gated_last", "weight1%d" % (c - 1)))
+                nc.vector.tensor_tensor(page[c][:].indirect(idx2[:, LIST_COLS:]), y[1, c], halves(wgo_sb)[1], MULT)
+                nc.sync.dma_start(out=out[c * P : (c + 1) * P, :], in_=page[c][:])

@@ -112,6 +112,7 @@ def tile_list_botnet_gated_gradients_kernel(
                 nc.sync.dma_start(out=window[:, cols], in_=rows[:, cols])
 
         s_rows = sT.rearrange("(b p t) c -> b t p c", p=P, t=PACK)
+        s_whole = {}
         s_win, s, tab_win, v_w, raw_w1 = {}, {}, {}, {}, {}
 
         def load_s(u, follows=None, pieces=1, spare=0):
@@ -132,7 +133,7 @@ def tile_list_botnet_gated_gradients_kernel(
         def gather_s(u, follows=None):
             dst = held([P, S], F32, "s%d" % u, follows)
             nc.vector.tensor_copy(dst[:], s_win[u][:].indirect(idx[:]))
-            s[u, 0], s[u, 1] = halves(dst)
+            s_whole[u] = dst
 
         def gather_s_half(u, half, dst):
             s[u, half] = dst
@@ -249,16 +250,23 @@ def tile_list_botnet_gated_gradients_kernel(
         load_s(2)
         load_w1(0, 1)
         load_s(3)
-        planes[0, 0] = held([P, PACK, HALF], BF16, "planes00")[:]
-        planes[0, 1] = held([P, PACK, HALF], BF16, "planes01")[:]
+        planes0 = held([P, 2 * W], BF16, "planes0")[:].rearrange("p (i h c) -> p i h c", h=2, i=PACK)
+        planes[0, 0], planes[0, 1] = planes0[:, :, 0], planes0[:, :, 1]
+
+        def by_half(flat):
+            return flat.rearrange("p (h c) -> p h c", h=2)
+
+        def finish_tile(u, parts, values):
+            nc.gpsimd.tensor_tensor(planes0[:, u], by_half(parts[:]), by_half(values[:]), MULT)
+
         area0 = held([P, 5 * HALF], F32, "area0")
         w1_second = area0[:, : 4 * HALF].bitcast(BF16)
 
         gather_s(0)
         load_w1(1, 1, follows="s_win0", at=EDGE)
-        for half in range(2):
-            less_one(0, half, half_tile("slope0%d" % half))
-            make_slope(0, half)
+        slope0 = held([P, S], F32, "slope0")
+        nc.scalar.activation(out=slope0[:], in_=s_whole[0][:], func=COPY, scale=1.0, bias=-1.0)
+        nc.gpsimd.tensor_tensor(slope0[:], s_whole[0][:], slope0[:], MULT)
         gather_table(0)
         load_s(4, follows="tab_w0")
         for a in range(PASSES):
@@ -272,28 +280,31 @@ def tile_list_botnet_gated_gradients_kernel(
         w1_10 = held([P, W], BF16, "w1_10")
         round_w1(1, 0, w1_10[:])
         (w1_q[1, 0],) = quantize_pieces("w1_10", w1_10[:])
-        for half in range(2):
-            gather_s_half(1, half, half_tile("s1%d" % half, "raw_w1_10", half * HB))
+
+
+        def gather_in_halves(u, follows=None):
+            s_whole[u] = held([P, S], F32, "s%d" % u, follows)
+            for half in range(2):
+                gather_s_half(u, half, halves(s_whole[u])[half])
+
+        def first_pass_tile(u, follows, at=0):
+            parts = held([P, S], F32, "part%d" % u, follows, at)
+            for half in range(2):
+                make_part(u, half, halves(parts)[half])
+            finish_tile(u, parts, s_whole[u])
+
+        gather_in_halves(1, "raw_w1_10")
         load_s(7, follows="s_win1")
-        copy_h(0, 0, half_tile("h_sb00", "s0"))
-        d_on_gpsimd(0, 0)
-        make_part(1, 0, half_tile("part10", "w1_00"))
-        copy_h(0, 1, half_tile("h_sb01", "s0", HB))
-        d_on_gpsimd(0, 1)
-        finish_part(1, 0)
-        gather_s_half(2, 0, half_tile("s20"))
-        make_part(1, 1, half_tile("part11", "w1_00", HB))
-        finish_part(1, 1)
-        gather_s_half(2, 1, half_tile("s21"))
+        h0 = held([P, S], F32, "h0", "s0")
+        for half in range(2):
+            copy_h(0, half, halves(h0)[half])
+        finish_tile(0, h0, slope0)
+        first_pass_tile(1, "w1_00")
+        gather_in_halves(2)
         round_w1(0, 1, w1_second[:, :W])
-        for half in range(2):
-            make_part(2, half, half_tile("part2%d" % half, "w1_10", half * HB))
-            finish_part(2, half)
-        for half in range(2):
-            gather_s_half(3, half, half_tile("s3%d" % half))
-        for half in range(2):
-            make_part(3, half, half_tile("part3%d" % half, "raw_w1_10", (2 + half) * HB))
-            finish_part(3, half)
+        first_pass_tile(2, "w1_10")
+        gather_in_halves(3)
+        first_pass_tile(3, "raw_w1_10", 2 * HB)
         round_w1(1, 1, w1_second[:, W:])
         area1 = held([P, 24 * HALF], F32, "area1", "s_win0", 4 * HB)
         for k, first in ((0, 3), (1, 20)):
@@ -303,33 +314,30 @@ def tile_list_botnet_gated_gradients_kernel(
         d00_grouped, wg0_grouped = early[:, :W], early[:, W:]
         d10_grouped = area1[:, 5 * HALF : 7 * HALF].bitcast(BF16)
         second = area1[:, 7 * HALF : 11 * HALF].bitcast(BF16)
-        wg1_grouped = area1[:, 14 * HALF : 16 * HALF].bitcast(BF16)
+        wg1_grouped = area1[:, 29 * HALF // 2 : 33 * HALF // 2].bitcast(BF16)
         late = area1[:, 11 * HALF : 17 * HALF].bitcast(BF16).rearrange("p (i c) -> p i c", i=PACK)[:, :, :HALF]
         s67b, part67b = two(area1, 3 * HALF, HALF), two(held([P, S], F32, "part67b", "w1_00"), 0, HALF)
-        lhs45, rhs45 = two(held([P, S], F32, "lhs45", "s_win2", 2 * HB), 0, HALF), two(area0, 3 * HALF, HALF)
+        lhs45, rhs45 = two(held([P, S], F32, "lhs45", "s_win2", 2 * HB), 0, HALF), two(held([P, S], F32, "s45"), 0, HALF)
         s67, part67 = two(held([P, S], F32, "s67", "s_win3"), 0, HALF), two(held([P, S], F32, "part67", "s_win3", 2 * HB), 0, HALF)
 
         def finish_pair(dst, first, parts, values):
             nc.gpsimd.tensor_tensor(grouped_view(dst, first, 2, LINE), runs(parts), runs(values), MULT)
 
-        gather_s_half(4, 0, half_tile("s40", "s_win2"))
-        gather_s_half(4, 1, area1[:, 8 * HALF : 9 * HALF])
+        gather_s_half(4, 0, rhs45[:, 0])
+        gather_s_half(4, 1, half_tile("s41", "s_win2"))
         load_scale_rows(wv_sc, wv_scales)
         wv_w = held([P, PASSES, N], U32, "wv_w", follows="s_win4", at=2 * HB)
         nc.sync.dma_start(out=wv_w[:].bitcast(I32), in_=wv_words.rearrange("b p c i -> p b (c i)").bitcast(I32))
         wgo_sb = area1[:, 22 * HALF :]
         nc.sync.dma_start(out=wgo_sb, in_=wgo)
         w1_q[0, 1], w1_q[1, 1] = quantize_pieces("w1_1", w1_second, follows="s_win4")
-        less_one(4, 0, half_tile("rest40", "slope00"))
+        less_one(4, 1, area1[:, 7 * HALF : 8 * HALF])
         group(d00_grouped, planes[0, 0])
-        less_one(4, 1, half_tile("rest41", "slope01"))
-        make_slope(4, 0, rhs45[:, 0])
-        make_slope(4, 1, area1[:, :HALF])
+        make_slope(4, 1, area0[:, 3 * HALF : 4 * HALF])
         gather_s_half(5, 0, rhs45[:, 1])
-        make_part(5, 0, lhs45[:, 1])
-        group(second[:, : W // 2], planes[0, 1][:, :, : HALF // 2])
-        copy_h(4, 0, lhs45[:, 0])
-        group(second[:, W // 2 : W], planes[0, 1][:, :, HALF // 2 :])
+        for u in (5, 4):
+            make_part(u, 0, lhs45[:, u - 4])
+        group(second[:, :W], planes[0, 1])
         finish_pair(d10_grouped, 0, lhs45, rhs45)
         gather_s_half(6, 0, s67[:, 0])
         make_part(6, 0, part67[:, 0])
@@ -350,9 +358,8 @@ def tile_list_botnet_gated_gradients_kernel(
         (d_q[1, 0],) = quantize_pieces("d10", d10_grouped, follows="s_win7", at=2 * HB)
         (wg_q[1],) = quantize_pieces("wg1", wg1_grouped)
         planes[1, 1] = late
-        for u in (6, 7):
-            finish_part(u, 1)
-        gather_s_half(5, 1, area1[:, 29 * HALF // 2 : 31 * HALF // 2])
+        nc.gpsimd.tensor_tensor(late[:, 2:], part67b, s67b, MULT)
+        gather_s_half(5, 1, area1[:, 16 * HALF : 17 * HALF])
 
         accs = {}
         BANK_AFTER = {"val01": "h61", "gate02": "h71", "val02": "h70", "gate03": "gate00", "val03": "val00", "gate10": "h41", "val10": "h51"}
@@ -438,14 +445,13 @@ def tile_list_botnet_gated_gradients_kernel(
         weigh_gated(1, area1[:, HALF : 2 * HALF])
         make_weight(0, 2, sigs[2], area1[:, 2 * HALF : 3 * HALF])
         val02 = val_bank(0, 2)
+        make_weight(0, 3, sigs[3], half_tile("weight03", "sig02"))
         group(second[:, W:], late)
         scatter(0, 0)
         scatter(0, 1)
         y_on_vector(0, 2, area1[:, 31 * HALF // 2 : 33 * HALF // 2], val02)
         d_q[0, 1], d_q[1, 1] = quantize_pieces("d1", second, follows="s_win5")
-        make_weight(0, 3, sigs[3], area1[:, 7 * HALF : 8 * HALF])
-        y3 = half_tile("y3", "raw_w1_10", HB)
-        y_on_gpsimd(0, 3, y3, y3)
+        y_on_gpsimd(0, 3, half_tile("val03", "raw_w1_10"), area1[:, 7 * HALF : 8 * HALF])
         scatter(0, 2)
         scatter(0, 3)
         for c in range(PAGES):

@@ -304,7 +304,9 @@ def tile_list_botnet_gated_gradients_kernel(
         round_w1(0, 1, w1_second[:, :W])
         first_pass_tile(2, "w1_10")
         gather_in_halves(3)
-        first_pass_tile(3, "raw_w1_10", 2 * HB)
+        for half in range(2):
+            make_part(3, half, half_tile("part3%d" % half, "raw_w1_10", (2 + half) * HB))
+            finish_part(3, half)
         round_w1(1, 1, w1_second[:, W:])
         area1 = held([P, 24 * HALF], F32, "area1", "s_win0", 4 * HB)
         for k, first in ((0, 3), (1, 20)):
@@ -317,27 +319,30 @@ def tile_list_botnet_gated_gradients_kernel(
         wg1_grouped = area1[:, 29 * HALF // 2 : 33 * HALF // 2].bitcast(BF16)
         late = area1[:, 11 * HALF : 17 * HALF].bitcast(BF16).rearrange("p (i c) -> p i c", i=PACK)[:, :, :HALF]
         s67b, part67b = two(area1, 3 * HALF, HALF), two(held([P, S], F32, "part67b", "w1_00"), 0, HALF)
-        lhs45, rhs45 = two(held([P, S], F32, "lhs45", "s_win2", 2 * HB), 0, HALF), two(held([P, S], F32, "s45"), 0, HALF)
+        lhs45, rhs45 = two(held([P, S], F32, "lhs45", "s_win2", 2 * HB), 0, HALF), two(area0, 3 * HALF, HALF)
         s67, part67 = two(held([P, S], F32, "s67", "s_win3"), 0, HALF), two(held([P, S], F32, "part67", "s_win3", 2 * HB), 0, HALF)
 
         def finish_pair(dst, first, parts, values):
             nc.gpsimd.tensor_tensor(grouped_view(dst, first, 2, LINE), runs(parts), runs(values), MULT)
 
-        gather_s_half(4, 0, rhs45[:, 0])
-        gather_s_half(4, 1, half_tile("s41", "s_win2"))
+        gather_s_half(4, 0, half_tile("s40", "s_win2"))
+        gather_s_half(4, 1, area1[:, 8 * HALF : 9 * HALF])
         load_scale_rows(wv_sc, wv_scales)
         wv_w = held([P, PASSES, N], U32, "wv_w", follows="s_win4", at=2 * HB)
         nc.sync.dma_start(out=wv_w[:].bitcast(I32), in_=wv_words.rearrange("b p c i -> p b (c i)").bitcast(I32))
         wgo_sb = area1[:, 22 * HALF :]
         nc.sync.dma_start(out=wgo_sb, in_=wgo)
         w1_q[0, 1], w1_q[1, 1] = quantize_pieces("w1_1", w1_second, follows="s_win4")
-        less_one(4, 1, area1[:, 7 * HALF : 8 * HALF])
+        less_one(4, 0, half_tile("rest40", "slope0"))
         group(d00_grouped, planes[0, 0])
-        make_slope(4, 1, area0[:, 3 * HALF : 4 * HALF])
+        less_one(4, 1, half_tile("rest41", "slope0", HB))
+        make_slope(4, 0, rhs45[:, 0])
+        make_slope(4, 1, area1[:, :HALF])
         gather_s_half(5, 0, rhs45[:, 1])
-        for u in (5, 4):
-            make_part(u, 0, lhs45[:, u - 4])
-        group(second[:, :W], planes[0, 1])
+        make_part(5, 0, lhs45[:, 1])
+        group(second[:, : W // 2], planes[0, 1][:, :, : HALF // 2])
+        copy_h(4, 0, lhs45[:, 0])
+        group(second[:, W // 2 : W], planes[0, 1][:, :, HALF // 2 :])
         finish_pair(d10_grouped, 0, lhs45, rhs45)
         gather_s_half(6, 0, s67[:, 0])
         make_part(6, 0, part67[:, 0])

@@ -367,7 +367,7 @@ def tile_list_botnet_gated_gradients_kernel(
         gather_s_half(5, 1, area1[:, 16 * HALF : 17 * HALF])
 
         accs = {}
-        BANK_AFTER = {"val01": "h61", "gate02": "h71", "val02": "h70", "gate03": "gate00", "val03": "val00", "gate10": "h41", "val10": "h51"}
+        BANK_AFTER = {"val01": "h61", "gate02": "h71", "val02": "h70", "gate03": "val01", "val03": "gate02", "gate10": "h41", "val10": "h51"}
 
         def product(name, half, lhsT, lhsT_scale, passes):
             if name not in accs:

@@ -326,18 +326,16 @@ def tile_list_botnet_gated_gradients_kernel(
             nc.gpsimd.tensor_tensor(grouped_view(dst, first, 2, LINE), runs(parts), runs(values), MULT)
 
         gather_s_half(4, 0, half_tile("s40", "s_win2"))
-        gather_s_half(4, 1, area1[:, 8 * HALF : 9 * HALF])
+        gather_s_half(4, 1, area1[:, 13 * HALF : 14 * HALF])
         load_scale_rows(wv_sc, wv_scales)
         wv_w = held([P, PASSES, N], U32, "wv_w", follows="s_win4", at=2 * HB)
         nc.sync.dma_start(out=wv_w[:].bitcast(I32), in_=wv_words.rearrange("b p c i -> p b (c i)").bitcast(I32))
         wgo_sb = area1[:, 22 * HALF :]
         nc.sync.dma_start(out=wgo_sb, in_=wgo)
         w1_q[0, 1], w1_q[1, 1] = quantize_pieces("w1_1", w1_second, follows="s_win4")
-        less_one(4, 0, half_tile("rest40", "slope0"))
+        less_one(4, 0, area1[:, 8 * HALF : 9 * HALF])
         group(d00_grouped, planes[0, 0])
-        less_one(4, 1, half_tile("rest41", "slope0", HB))
         make_slope(4, 0, rhs45[:, 0])
-        make_slope(4, 1, area1[:, :HALF])
         gather_s_half(5, 0, rhs45[:, 1])
         make_part(5, 0, lhs45[:, 1])
         group(second[:, : W // 2], planes[0, 1][:, :, : HALF // 2])
@@ -426,8 +424,8 @@ def tile_list_botnet_gated_gradients_kernel(
                 nc.sync.dma_start(out=out[c * P : (c + 1) * P, :], in_=page[c][:])
 
         sigs = {c: half_tile("sig0%d" % c, "s_win6", c * HB) for c in range(1, PAGES)}
-        sigs[0] = area1[:, 21 * HALF // 2 : 23 * HALF // 2]
-        gated = [area1[:, 12 * HALF : 13 * HALF], area1[:, 13 * HALF : 14 * HALF]]
+        sigs[0] = area1[:, HALF : 2 * HALF]
+        gated = [area1[:, 12 * HALF : 13 * HALF], area1[:, :HALF]]
 
         def gate_val(c, passes):
             sigmoid_of_gate(0, c, sigs[c], passes)
@@ -442,21 +440,22 @@ def tile_list_botnet_gated_gradients_kernel(
         gate_bank(0, 0, [0])
         val_bank(0, 0, [0])
         gate_val(0, [1])
-        make_part(5, 1, area1[:, 3 * HALF // 2 : 5 * HALF // 2], h51)
+        make_part(5, 1, area1[:, 2 * HALF : 3 * HALF], h51)
         gate_val(1, range(PASSES))
-        d_on_vector(4, 1, h41)
+        make_part(4, 1, sigs[0], h41)
         weigh_gated(0, area1[:, 17 * HALF : 18 * HALF])
-        finish_part(5, 1)
-        weigh_gated(1, area1[:, HALF : 2 * HALF])
+        weigh_gated(1, half_tile("y1", "raw_w1_01"))
+        nc.gpsimd.tensor_tensor(late[:, :2], two(area1, HALF, HALF), two(area1, 13 * HALF, 3 * HALF), MULT)
         make_weight(0, 2, sigs[2], area1[:, 2 * HALF : 3 * HALF])
         val02 = val_bank(0, 2)
-        make_weight(0, 3, sigs[3], half_tile("weight03", "sig02"))
         group(second[:, W:], late)
         scatter(0, 0)
         scatter(0, 1)
         y_on_vector(0, 2, area1[:, 31 * HALF // 2 : 33 * HALF // 2], val02)
         d_q[0, 1], d_q[1, 1] = quantize_pieces("d1", second, follows="s_win5")
-        y_on_gpsimd(0, 3, half_tile("val03", "raw_w1_10"), area1[:, 7 * HALF : 8 * HALF])
+        make_weight(0, 3, sigs[3], area1[:, 7 * HALF : 8 * HALF])
+        y3 = half_tile("y3", "raw_w1_10")
+        y_on_gpsimd(0, 3, y3, y3)
         scatter(0, 2)
         scatter(0, 3)
         for c in range(PAGES):

from contextlib import ExitStack

import concourse.mybir as mybir

K, T, S, H, N, T2 = 1024, 2048, 1024, 1024, 512, 2048
FLOPS = 2 * K * H * S + 2 * 2 * H * N * S

F32 = mybir.dt.float32
BF16 = mybir.dt.bfloat16
I32 = mybir.dt.int32
U32 = mybir.dt.uint32
U16 = mybir.dt.uint16
U8 = mybir.dt.uint8
E4M3 = mybir.dt.float8_e4m3fn_x4
E5M2 = mybir.dt.float8_e5m2_x4
MULT = mybir.AluOpType.mult
ADD = mybir.AluOpType.add
COPY = mybir.ActivationFunctionType.Copy
SIGMOID = mybir.ActivationFunctionType.Sigmoid

BYTES_OF = {F32: 4, BF16: 2, U32: 4, U16: 2, U8: 1}

P = 128
PACK = 4
PASS = P * PACK
PASSES = 2
HALF = 512
LIST_COLS = HALF // 16
ROW_TILES = H // P
LAST = ROW_TILES - 1
PAGES = N // P
RUN = 4
LINE = 2
BANKS = 8


def tile_list_botnet_gated_gradients_kernel(
    tc, tab_words, tab_scales, offs, offs2, sT, w1, wv_words, wv_scales, wg, wgo, out
):
    nc = tc.nc
    with ExitStack() as ctx:
        keep = ctx.enter_context(tc.tile_pool(name="keep", bufs=1))
        psum = ctx.enter_context(tc.psum_pool(name="psum", bufs=1))

        place, top = {}, [0]

        def held(shape, dtype, name, follows=None, at=0, spare=0):
            size = BYTES_OF[dtype]
            for extent in shape[1:]:
                size = size * extent
            if follows:
                place[name] = place[follows] + at
            else:
                place[name] = top[0]
                top[0] = top[0] + (size + 63) // 64 * 64 + spare
            return keep.tile(shape, dtype, name=name, align_bytes=64, offset=place[name])

        bank_of, turn = {}, [0]

        def bank(name, follows=None):
            if follows:
                bank_of[name] = bank_of[follows]
            else:
                bank_of[name] = turn[0] % BANKS
                turn[0] = turn[0] + 1
            return psum.tile([P, HALF], F32, name=name, offset=bank_of[name] * HALF * 4)

        def halves(ap):
            return ap[:, :HALF], ap[:, HALF:]

        def grouped_view(dst, first, count, run=RUN):
            return dst.rearrange("p (c x i) -> p c i x", x=run, i=PACK)[:, :, first : first + count, :]

        def two(flat, first, step):
            return flat[:, first : first + 2 * step].rearrange("p (i c) -> p i c", i=2)[:, :, :HALF]

        def runs(flat):
            return flat.rearrange("p i (c x) -> p c i x", x=LINE)

        def group(dst, planes, first=0):
            nc.scalar.copy(
                out=grouped_view(dst, first, planes.shape[1]),
                in_=planes.rearrange("p i (c x) -> p c i x", x=RUN),
            )

        def quantize(codes, scales, grouped):
            nc.vector.quantize_mx(out=codes.bitcast(E4M3), scales=scales, in_=grouped)

        W = PACK * HALF
        NH = N // 2
        HB = HALF * 4
        EDGE = 64

        idx = held([P, S // 16], U16, "idx")
        idx2 = held([P, S // 16], U16, "idx2")
        tab_sc = held([P, PASSES * T], U8, "tab_sc")
        wv_sc = held([P, PASSES * N], U8, "wv_sc")
        page = {}

        def clear_page(c, follows=None):
            page[c] = held([P, T2], F32, "page%d" % c, follows)
            nc.gpsimd.memset(page[c][:], 0.0)

        nc.gpsimd.memset(tab_sc[:].bitcast(I32), 0)
        nc.gpsimd.memset(wv_sc[:].bitcast(I32), 0)
        for c in range(PAGES):
            clear_page(c)

        def load_columns(window, rows, pieces):
            for k in range(pieces):
                cols = slice(k * T // pieces, (k + 1) * T // pieces)
                nc.sync.dma_start(out=window[:, cols], in_=rows[:, cols])

        s_rows = sT.rearrange("(b p t) c -> b t p c", p=P, t=PACK)
        s_whole = {}
        s_win, s, tab_win, v_w, raw_w1 = {}, {}, {}, {}, {}

        def load_s(u, follows=None, pieces=1, spare=0):
            s_win[u] = held([P, T], F32, "s_win%d" % u, follows, spare=spare)
            load_columns(s_win[u][:], s_rows[u // PACK, u % PACK], pieces)

        def load_table(a, pieces=1):
            tab_win[a] = held([P, T], U32, "tab_w%d" % a)
            load_columns(tab_win[a][:].bitcast(I32), tab_words[a].rearrange("p t i -> p (t i)").bitcast(I32), pieces)

        def load_w1(a, b, follows=None, rows_of_word=(slice(0, PACK),), at=0, spare=0):
            if (a, b) not in raw_w1:
                raw_w1[a, b] = held([P, PACK, HALF], F32, "raw_w1_%d%d" % (a, b), follows, at, spare)
            rows = w1[a * PASS : (a + 1) * PASS, b * PASS : (b + 1) * PASS].rearrange("(p i) c -> p i c", i=PACK)
            for part in rows_of_word:
                nc.sync.dma_start(out=raw_w1[a, b][:, part], in_=rows[:, part])

        def gather_s(u, follows=None):
            dst = held([P, S], F32, "s%d" % u, follows)
            nc.vector.tensor_copy(dst[:], s_win[u][:].indirect(idx[:]))
            s_whole[u] = dst

        def gather_s_half(u, half, dst):
            s[u, half] = dst
            nc.vector.tensor_copy(s[u, half], s_win[u][:].indirect(idx[:, half * LIST_COLS : (half + 1) * LIST_COLS]))

        v_sc = {}

        def gather_scales(a, follows=None):
            v_sc[a] = held([P, S], U8, "v_sc%d" % a, follows)
            nc.vector.tensor_copy(v_sc[a][:], tab_sc[:, a * T : (a + 1) * T].indirect(idx[:]))

        def load_scale_rows(tile, scale_rows):
            for quad in range(4):
                nc.sync.dma_start(
                    out=tile[32 * quad : 32 * quad + 4, :].bitcast(I32).rearrange("x (a c) -> x a c", a=PASSES),
                    in_=scale_rows[:, 4 * quad : 4 * quad + 4, :].bitcast(I32).rearrange("a x c -> x a c"),
                )

        def gather_table(a):
            v_w[a] = held([P, S], U32, "v_w%d" % a)
            nc.vector.tensor_copy(v_w[a][:], tab_win[a][:].indirect(idx[:]))

        w1_q, d_q, wg_q = {}, {}, {}

        def round_w1(a, b, dst):
            nc.scalar.copy(
                out=dst.rearrange("p (t m i) -> p m i t", t=PACK, i=PACK),
                in_=raw_w1[a, b][:].rearrange("p i (m t) -> p m i t", t=PACK),
            )

        def quantize_pieces(name, grouped, follows=None, at=0, scales_follow=None):
            words = grouped.shape[1] // PACK
            codes = held([P, words], U32, name + "_codes", follows, at)
            scales = held([P, words], U8, name + "_scales", scales_follow)
            quantize(codes[:], scales[:], grouped)
            return [(codes[:, k : k + HALF], scales[:, k : k + HALF]) for k in range(0, words, HALF)]

        def h_bank(u, half, follows=None):
            b, t = divmod(u, PACK)
            acc = bank("h%d%d" % (u, half), follows)
            entries = slice(half * HALF, (half + 1) * HALF)
            words = slice(t * P, (t + 1) * P)
            for a in range(PASSES):
                nc.tensor.matmul_mx(
                    out=acc[:],
                    lhsT=w1_q[a, b][0][:, words].bitcast(E4M3),
                    lhsT_scale=w1_q[a, b][1][:, words],
                    rhs=v_w[a][:, entries].bitcast(E5M2),
                    rhs_scale=v_sc[a][:, entries],
                    start=(a == 0),
                    stop=(a == PASSES - 1),
                )
            return acc

        planes = {}

        def plane(u, half):
            return planes[u // PACK, half][:, u % PACK, :]

        slope, part = {}, {}

        def less_one(u, half, dst):
            slope[u, half] = dst
            nc.scalar.activation(out=slope[u, half], in_=s[u, half], func=COPY, scale=1.0, bias=-1.0)

        def make_slope(u, half, dst=None):
            rest = slope[u, half]
            if dst is not None:
                slope[u, half] = dst
            nc.gpsimd.tensor_tensor(slope[u, half], s[u, half], rest, MULT)

        def copy_h(u, half, dst, acc=None):
            part[u, half] = dst
            nc.scalar.copy(out=part[u, half], in_=(acc or h_bank(u, half))[:])

        def d_on_gpsimd(u, half):
            nc.gpsimd.tensor_tensor(plane(u, half), part[u, half], slope[u, half], MULT)

        def d_on_vector(u, half, acc):
            nc.vector.tensor_tensor(plane(u, half), acc[:], slope[u, half], MULT)

        def make_part(u, half, dst, acc=None):
            part[u, half] = dst
            nc.vector.scalar_tensor_tensor(
                out=part[u, half], in0=s[u, half], scalar=-1.0, in1=(acc or h_bank(u, half))[:], op0=ADD, op1=MULT
            )

        def finish_part(u, half):
            nc.gpsimd.tensor_tensor(plane(u, half), part[u, half], s[u, half], MULT)

        raw_wg = {}

        def load_wg(k, b, raw):
            raw_wg[k, b] = raw
            rows = wg[b * PASS : (b + 1) * PASS, k * NH : (k + 1) * NH]
            nc.sync.dma_start(out=raw, in_=rows.rearrange("(p i) c -> p i c", i=PACK))

        def round_wg(k, b, dst):
            group(dst[:, b * W // 2 : (b + 1) * W // 2], raw_wg[k, b])

        def half_tile(name, follows=None, at=0):
            return held([P, HALF], F32, name, follows, at)[:]

        nc.sync.dma_start(idx[:], offs)
        nc.sync.dma_start(idx2[:], offs2)
        load_s(0, pieces=2, spare=24 * HB)
        load_table(0, pieces=2)
        load_w1(0, 0, rows_of_word=(slice(0, 1), slice(1, 2)))
        load_scale_rows(tab_sc, tab_scales)
        load_w1(0, 0, rows_of_word=(slice(2, 4),))
        load_table(1)
        load_w1(1, 0)
        load_s(1)
        load_s(2)
        load_w1(0, 1)
        load_s(3)
        planes0 = held([P, 2 * W], BF16, "planes0")[:].rearrange("p (i h c) -> p i h c", h=2, i=PACK)
        planes[0, 0], planes[0, 1] = planes0[:, :, 0], planes0[:, :, 1]

        def by_half(flat):
            return flat.rearrange("p (h c) -> p h c", h=2)

        def finish_tile(u, parts, values):
            nc.gpsimd.tensor_tensor(planes0[:, u], by_half(parts[:]), by_half(values[:]), MULT)

        area0 = held([P, 5 * HALF], F32, "area0")
        w1_second = area0[:, : 4 * HALF].bitcast(BF16)

        gather_s(0)
        load_w1(1, 1, follows="s_win0", at=EDGE)
        slope0 = held([P, S], F32, "slope0")
        nc.scalar.activation(out=slope0[:], in_=s_whole[0][:], func=COPY, scale=1.0, bias=-1.0)
        nc.gpsimd.tensor_tensor(slope0[:], s_whole[0][:], slope0[:], MULT)
        gather_table(0)
        load_s(4, follows="tab_w0")
        for a in range(PASSES):
            gather_scales(a)
        w1_00 = held([P, W], BF16, "w1_00")
        round_w1(0, 0, w1_00[:])
        load_s(5, follows="raw_w1_00")
        (w1_q[0, 0],) = quantize_pieces("w1_00", w1_00[:])
        gather_table(1)
        load_s(6, follows="tab_w1")
        w1_10 = held([P, W], BF16, "w1_10")
        round_w1(1, 0, w1_10[:])
        (w1_q[1, 0],) = quantize_pieces("w1_10", w1_10[:])


        def gather_in_halves(u, follows=None):
            s_whole[u] = held([P, S], F32, "s%d" % u, follows)
            for half in range(2):
                gather_s_half(u, half, halves(s_whole[u])[half])

        def first_pass_tile(u, follows, at=0):
            parts = held([P, S], F32, "part%d" % u, follows, at)
            for half in range(2):
                make_part(u, half, halves(parts)[half])
            finish_tile(u, parts, s_whole[u])

        gather_in_halves(1, "raw_w1_10")
        load_s(7, follows="s_win1")
        h0 = held([P, S], F32, "h0", "s0")
        for half in range(2):
            copy_h(0, half, halves(h0)[half])
        finish_tile(0, h0, slope0)
        first_pass_tile(1, "w1_00")
        gather_in_halves(2)
        round_w1(0, 1, w1_second[:, :W])
        first_pass_tile(2, "w1_10")
        gather_in_halves(3)
        for half in range(2):
            make_part(3, half, half_tile("part3%d" % half, "raw_w1_10", (2 + half) * HB))
            finish_part(3, half)
        round_w1(1, 1, w1_second[:, W:])
        area1 = held([P, 24 * HALF], F32, "area1", "s_win0", 4 * HB)
        for k, first in ((0, 3), (1, 20)):
            for b in range(PASSES):
                load_wg(k, b, area1[:, (first - 2 * b) * HALF : (first + 2 - 2 * b) * HALF].rearrange("p (i c) -> p i c", i=PACK))
        early = held([P, 2 * W], BF16, "early", "s_win0")[:]
        d00_grouped, wg0_grouped = early[:, :W], early[:, W:]
        d10_grouped = area1[:, 5 * HALF : 7 * HALF].bitcast(BF16)
        second = area1[:, 7 * HALF : 11 * HALF].bitcast(BF16)
        wg1_grouped = area1[:, 29 * HALF // 2 : 33 * HALF // 2].bitcast(BF16)
        late = area1[:, 11 * HALF : 17 * HALF].bitcast(BF16).rearrange("p (i c) -> p i c", i=PACK)[:, :, :HALF]
        s67b, part67b = two(area1, 3 * HALF, HALF), two(held([P, S], F32, "part67b", "w1_00"), 0, HALF)
        lhs45, rhs45 = two(held([P, S], F32, "lhs45", "s_win2", 2 * HB), 0, HALF), two(area0, 3 * HALF, HALF)
        s67, part67 = two(held([P, S], F32, "s67", "s_win3"), 0, HALF), two(held([P, S], F32, "part67", "s_win3", 2 * HB), 0, HALF)

        def finish_pair(dst, first, parts, values):
            nc.gpsimd.tensor_tensor(grouped_view(dst, first, 2, LINE), runs(parts), runs(values), MULT)

        gather_s_half(4, 0, half_tile("s40", "s_win2"))
        gather_s_half(4, 1, area1[:, 13 * HALF : 14 * HALF])
        load_scale_rows(wv_sc, wv_scales)
        wv_w = held([P, PASSES, N], U32, "wv_w", follows="s_win4", at=2 * HB)
        nc.sync.dma_start(out=wv_w[:].bitcast(I32), in_=wv_words.rearrange("b p c i -> p b (c i)").bitcast(I32))
        wgo_sb = area1[:, 22 * HALF :]
        nc.sync.dma_start(out=wgo_sb, in_=wgo)
        w1_q[0, 1], w1_q[1, 1] = quantize_pieces("w1_1", w1_second, follows="s_win4")
        less_one(4, 0, area1[:, 8 * HALF : 9 * HALF])
        group(d00_grouped, planes[0, 0])
        make_slope(4, 0, rhs45[:, 0])
        gather_s_half(5, 0, rhs45[:, 1])
        make_part(5, 0, lhs45[:, 1])
        group(second[:, : W // 2], planes[0, 1][:, :, : HALF // 2])
        copy_h(4, 0, lhs45[:, 0])
        group(second[:, W // 2 : W], planes[0, 1][:, :, HALF // 2 :])
        finish_pair(d10_grouped, 0, lhs45, rhs45)
        gather_s_half(6, 0, s67[:, 0])
        make_part(6, 0, part67[:, 0])
        h41 = h_bank(4, 1)
        gather_s_half(7, 0, s67[:, 1])
        make_part(7, 0, part67[:, 1])
        finish_pair(d10_grouped, 2, part67, s67)
        for b in range(PASSES):
            round_wg(0, b, wg0_grouped)
        for b in range(PASSES):
            round_wg(1, b, wg1_grouped)
        for u in (6, 7):
            gather_s_half(u, 1, s67b[:, u - 6])
        for u in (6, 7):
            make_part(u, 1, part67b[:, u - 6])
        h51 = h_bank(5, 1)
        d_q[0, 0], wg_q[0] = quantize_pieces("early", early, follows="s_win7", scales_follow="s67")
        (d_q[1, 0],) = quantize_pieces("d10", d10_grouped, follows="s_win7", at=2 * HB)
        (wg_q[1],) = quantize_pieces("wg1", wg1_grouped)
        planes[1, 1] = late
        nc.gpsimd.tensor_tensor(late[:, 2:], part67b, s67b, MULT)
        gather_s_half(5, 1, area1[:, 16 * HALF : 17 * HALF])

        accs = {}
        BANK_AFTER = {"val01": "h61", "gate02": "h71", "val02": "h70", "gate03": "val01", "val03": "gate02", "gate10": "h41", "val10": "h51"}

        def product(name, half, lhsT, lhsT_scale, passes):
            if name not in accs:
                accs[name] = bank(name, BANK_AFTER.get(name))
            acc = accs[name]
            for b in passes:
                nc.tensor.matmul_mx(
                    out=acc[:],
                    lhsT=lhsT[b].bitcast(E4M3),
                    lhsT_scale=lhsT_scale[b],
                    rhs=d_q[b, half][0].bitcast(E4M3),
                    rhs_scale=d_q[b, half][1],
                    start=(b == 0),
                    stop=(b == PASSES - 1),
                )
            return acc

        weight, y = {}, {}

        def gate_bank(half, c, passes=range(PASSES)):
            k, first = divmod(c * P, NH)
            words = [slice(b * NH + first, b * NH + first + P) for b in range(PASSES)]
            return product("gate%d%d" % (half, c), half, [wg_q[k][0][:, w] for w in words], [wg_q[k][1][:, w] for w in words], passes)

        def sigmoid_of_gate(half, c, sig, passes=range(PASSES)):
            nc.scalar.activation(out=sig, in_=gate_bank(half, c, passes)[:], func=SIGMOID, scale=-1.0)

        def weigh(half, c, sig, dst):
            weight[half, c] = dst
            nc.gpsimd.tensor_tensor(dst, sig, halves(wgo_sb)[half], MULT)

        def make_weight(half, c, sig, dst):
            sigmoid_of_gate(half, c, sig)
            weigh(half, c, sig, dst)

        def val_bank(half, c, passes=range(PASSES)):
            words = [wv_w[:, b, c * P : (c + 1) * P] for b in range(PASSES)]
            return product("val%d%d" % (half, c), half, words, [wv_sc[:, b * N + c * P : b * N + (c + 1) * P] for b in range(PASSES)], passes)

        def y_on_gpsimd(half, c, val, dst, between=None):
            y[half, c] = dst
            nc.scalar.activation(out=val, in_=val_bank(half, c)[:], func=COPY, scale=-1.0)
            if between:
                between()
            nc.gpsimd.tensor_tensor(dst, val, weight[half, c], MULT)

        def y_on_vector(half, c, dst, acc):
            y[half, c] = dst
            nc.vector.scalar_tensor_tensor(
                out=y[half, c], in0=acc[:], scalar=-1.0, in1=weight[half, c], op0=MULT, op1=MULT
            )

        def scatter(half, c):
            nc.vector.tensor_copy(page[c][:].indirect(idx2[:, half * LIST_COLS : (half + 1) * LIST_COLS]), y[half, c])
            if half == 1:
                nc.sync.dma_start(out=out[c * P : (c + 1) * P, :], in_=page[c][:])

        sigs = {c: half_tile("sig0%d" % c, "s_win6", c * HB) for c in range(1, PAGES)}
        sigs[0] = area1[:, HALF : 2 * HALF]
        gated = [area1[:, 12 * HALF : 13 * HALF], area1[:, :HALF]]

        def gate_val(c, passes):
            sigmoid_of_gate(0, c, sigs[c], passes)
            nc.vector.scalar_tensor_tensor(
                out=gated[c], in0=val_bank(0, c, passes)[:], scalar=-1.0, in1=sigs[c], op0=MULT, op1=MULT
            )

        def weigh_gated(c, dst):
            y[0, c] = dst
            nc.gpsimd.tensor_tensor(dst, gated[c], halves(wgo_sb)[0], MULT)

        gate_bank(0, 0, [0])
        val_bank(0, 0, [0])
        gate_val(0, [1])
        make_part(5, 1, area1[:, 2 * HALF : 3 * HALF], h51)
        gate_val(1, range(PASSES))
        make_part(4, 1, sigs[0], h41)
        weigh_gated(0, area1[:, 17 * HALF : 18 * HALF])
        weigh_gated(1, half_tile("y1", "raw_w1_01"))
        nc.gpsimd.tensor_tensor(late[:, :2], two(area1, HALF, HALF), two(area1, 13 * HALF, 3 * HALF), MULT)
        make_weight(0, 2, sigs[2], area1[:, 2 * HALF : 3 * HALF])
        val02 = val_bank(0, 2)
        group(second[:, W:], late)
        scatter(0, 0)
        scatter(0, 1)
        y_on_vector(0, 2, area1[:, 31 * HALF // 2 : 33 * HALF // 2], val02)
        d_q[0, 1], d_q[1, 1] = quantize_pieces("d1", second, follows="s_win5")
        make_weight(0, 3, sigs[3], area1[:, 7 * HALF : 8 * HALF])
        y3 = half_tile("y3", "raw_w1_10")
        y_on_gpsimd(0, 3, y3, y3)
        scatter(0, 2)
        scatter(0, 3)
        for c in range(PAGES):
            sig_c = half_tile("sig1%d" % c, "s_win6", c * HB)
            y_c = half_tile("y1%d" % c, "area0", c * HB)
            if c < PAGES - 1:
                make_weight(1, c, sig_c, half_tile("weight1%d" % c, "early", c * HB))
                y_on_gpsimd(1, c, y_c, y_c)
                scatter(1, c)
            else:
                sigmoid_of_gate(1, c, sig_c)
                weight[1, c] = sig_c
                y_on_gpsimd(1, c, y_c, half_tile("gated_last", "weight1%d" % (c - 1)))
                nc.vector.tensor_tensor(page[c][:].indirect(idx2[:, LIST_COLS:]), y[1, c], halves(wgo_sb)[1], MULT)
                nc.sync.dma_start(out=out[c * P : (c + 1) * P, :], in_=page[c][:])
